import numpy as np
import ml_dtypes


def mxq(x, axis, fmt="e4m3"):
    dtype, down = {"e4m3": (ml_dtypes.float8_e4m3fn, 7), "e5m2": (ml_dtypes.float8_e5m2, 14)}[fmt]
    v = np.moveaxis(np.asarray(x, np.float32).astype(ml_dtypes.bfloat16).astype(np.float64), axis, -1)
    blocks = v.reshape(v.shape[:-1] + (-1, 32))
    amax = np.abs(blocks).max(-1, keepdims=True)
    byte = np.maximum(np.where(amax > 0, np.frexp(amax)[1] - 1 + 127, 0) - down, 1)
    scale = np.exp2(byte - 127.0)
    codes = (blocks / scale).astype(np.float32).astype(dtype).astype(np.float64)
    return np.moveaxis((codes * scale).reshape(v.shape), -1, axis)


WIDE = False


def mx_kscale(k):
    if not WIDE:
        return np.ones(k)
    levels = np.array([10, -10, 5, -5, 0])
    if k % 512:
        return np.exp2(np.random.permutation(np.resize(levels, k // 32))).repeat(32)
    a = np.empty((k // 512, 16))
    for p in range(k // 512):
        a[p, :8] = np.random.permutation(np.resize(levels, 8))
        for g in range(8):
            far = levels[np.abs(levels - a[p, g]) >= 10]
            a[p, g + 8] = far[np.random.randint(len(far))]
    return np.exp2(a.ravel()).repeat(32)


def f64(x):
    return np.asarray(x).astype(np.float64)


def striped(idx):
    return np.tile(idx.reshape(-1, 16).T, (8, 1)).astype(np.uint16)


def unstriped(offs):
    return offs[:16].T.reshape(-1).astype(np.int64)


E2M1 = np.array([0.0, 0.5, 1.0, 1.5, 2.0, 3.0, 4.0, 6.0, -0.0, -0.5, -1.0, -1.5, -2.0, -3.0, -4.0, -6.0])


def pack_weight(w, fmt):
    k, n = w.shape
    w = f64(np.asarray(w, np.float32).astype(ml_dtypes.bfloat16)).reshape(k // 32, 32, n)
    amax = np.abs(w).max(1)
    if fmt == "e4m3":
        byte = np.frexp(amax)[1] - 1 + 127 - 7
    else:
        mant, ex = np.frexp(amax / 6.0)
        byte = np.where(mant > 0.5, ex, ex - 1) + 127
    byte = np.clip(np.where(amax > 0, byte, 1), 1, 254)
    scaled = (w * np.exp2(127.0 - byte)[:, None, :]).reshape(k, n).astype(np.float32)
    by_word = np.ascontiguousarray(scaled.reshape(k // 512, 128, 4, n).transpose(0, 1, 3, 2))
    if fmt == "e4m3":
        words = by_word.astype(ml_dtypes.float8_e4m3fn).view(np.uint8)
    else:
        c = by_word.astype(ml_dtypes.float4_e2m1fn).view(np.uint8) & 0xF
        words = (c[..., 0::2] | (c[..., 1::2] << 4)).reshape(k // 512, 128, 2 * n)
    return np.ascontiguousarray(words), np.ascontiguousarray(byte.astype(np.uint8).reshape(k // 512, 16, n))


def unpack_weight(words, scales, fmt):
    g, _, n = scales.shape
    words = np.ascontiguousarray(words).reshape(g, 128, n, -1)
    if fmt == "e4m3":
        vals = words.view(ml_dtypes.float8_e4m3fn).astype(np.float64)
    else:
        nib = np.empty((g, 128, n, 4), np.uint8)
        nib[..., 0::2] = words & 0xF
        nib[..., 1::2] = words >> 4
        vals = E2M1[nib]
    vals = vals * np.repeat(np.exp2(scales.astype(np.float64) - 127.0), 8, axis=1)[..., None]
    return vals.transpose(0, 1, 3, 2).reshape(g * 512, n)


def gelu(v):
    return 0.5 * v * (1.0 + np.tanh(np.sqrt(2.0 / np.pi) * (v + 0.044715 * v**3)))


def bf(x):
    return np.asarray(x, np.float32).astype(ml_dtypes.bfloat16)

def planes(Y):
    n, m = Y.shape
    b = f64(bf(Y)).reshape(n // 32, 32, m)
    amax = np.abs(b).max(1)
    byte = np.clip(np.where(amax > 0, np.frexp(amax)[1] - 1 + 127 - 7, 1), 1, 254)
    codes = (b * np.exp2(127.0 - byte)[:, None, :]).reshape(n, m).astype(np.float32).astype(ml_dtypes.float8_e4m3fn).view(np.uint8)
    words = codes.reshape(n // 512, 128, 4, m).transpose(0, 1, 3, 2)
    return np.ascontiguousarray(words), np.ascontiguousarray(byte.astype(np.uint8).reshape(n // 512, 16, m))


K, T, S, T2, S2, N = 1024, 2048, 1024, 4096, 1024, 512

def setup_inputs():
    n = np.random.standard_normal
    s = mx_kscale(K)[:, None]
    u = mx_kscale(S)[:, None]
    tab_words, tab_scales = pack_weight(n((K, T)) * s, "e4m3")
    tab2_words, tab2_scales = pack_weight(n((K, T2)) / np.sqrt(K) / s, "e4m3")
    offs = striped(np.random.permutation(T)[:S])
    offs2 = striped(np.random.permutation(T2)[:S2])
    abund = np.exp(0.3 * n(S)) * u[:, 0]
    w = n((S, N)) * (2.0 / np.sqrt(S)) * np.exp(0.8 * n(N)) / u
    w4_words, w4_scales = pack_weight(n((S, N)) * (2.0 / np.sqrt(S)) / u, "e2m1")
    return {"tab_words": tab_words, "tab_scales": tab_scales,
            "tab2_words": tab2_words, "tab2_scales": tab2_scales,
            "offs": offs, "offs2": offs2,
            "abund": abund.astype(np.float32), "w": w.astype(np.float32),
            "w4_words": w4_words, "w4_scales": w4_scales}

def reference(tab_words, tab_scales, tab2_words, tab2_scales, offs, offs2, abund, w, w4_words, w4_scales):
    v = unpack_weight(tab_words, tab_scales, "e4m3")[:, unstriped(offs)]
    v2 = unpack_weight(tab2_words, tab2_scales, "e4m3")[:, unstriped(offs2)]
    A = v.T @ v2
    sq = A * A
    h = sq / (1.0 + sq) * f64(abund)[:, None]
    hq = mxq(h, 0, "e4m3")
    p1 = mxq(f64(w), 0, "e4m3").T @ hq
    p2 = unpack_weight(w4_words, w4_scales, "e2m1").T @ hq
    y = p1 * p2
    words, scales = planes(y)
    return y, words, scales

@@ -1,0 +1,253 @@
+from contextlib import ExitStack
+
+import concourse.mybir as mybir
+
+K, T1, T2, S1, S2, N = 1024, 2048, 4096, 1024, 1024, 512
+FLOPS = 2 * K * S1 * S2 + 2 * 2 * S1 * N * S2
+
+F32 = mybir.dt.float32
+BF16 = mybir.dt.bfloat16
+I32 = mybir.dt.int32
+U32 = mybir.dt.uint32
+U16 = mybir.dt.uint16
+U8 = mybir.dt.uint8
+FP8X4 = mybir.dt.float8_e4m3fn_x4
+FP4X4 = mybir.dt.float4_e2m1fn_x4
+ACT = mybir.ActivationFunctionType
+ALU = mybir.AluOpType
+
+P = 128
+PACK = 4
+PASS = P * PACK
+HALF = 512
+JC = 256
+ROW1 = 0
+ROW2 = 8
+
+
+def tile_list_motif_promoter_activity_kernel(
+    tc, tab_words, tab_scales, tab2_words, tab2_scales, offs, offs2, abund, w, w4_words, w4_scales,
+    out_0, out_1, out_2,
+):
+    nc = tc.nc
+    with ExitStack() as ctx:
+        keep = ctx.enter_context(tc.tile_pool(name="keep", bufs=1))
+        work = ctx.enter_context(tc.tile_pool(name="work", bufs=3))
+        psum = ctx.enter_context(tc.psum_pool(name="psum", bufs=2))
+
+        def held(shape, dtype, name):
+            return keep.tile(shape, dtype, name=name, align_bytes=64)
+
+        win1_s = held([P, T1], U8, "win1_s")
+        win2_s = held([P, T2], U8, "win2_s")
+        w4_s_raw = held([P, 2 * N], U8, "w4_s_raw")
+        nc.vector.memset(win1_s[:].bitcast(I32), 0)
+        nc.vector.memset(win2_s[:].bitcast(I32), 0)
+        nc.vector.memset(w4_s_raw[:].bitcast(I32), 0)
+        one = held([P, 1], F32, "one")
+        warm = held([P, 1], F32, "warm")
+        nc.vector.memset(one[:], 1.0)
+        nc.scalar.activation(warm[:], one[:], ACT.Abs_reciprocal_sqrt)
+
+        idx1 = keep.tile([P, S1 // 16], U16, name="idx1")
+        idx2 = keep.tile([P, S2 // 16], U16, name="idx2")
+        win1 = [held([P, T1], U32, "win1_%d" % a) for a in range(2)]
+        win2 = [held([P, T2], U32, "win2_%d" % a) for a in range(2)]
+
+        def load_words(dst, src):
+            nc.sync.dma_start(dst[:].bitcast(I32), src.rearrange("p n t -> p (n t)").bitcast(I32))
+
+        def load_scales(win, src, row):
+            for q in range(4):
+                nc.sync.dma_start(
+                    win[32 * q + row : 32 * q + row + 8, :].bitcast(I32),
+                    src[:, 4 * q : 4 * q + 4, :].bitcast(I32),
+                )
+
+        nc.sync.dma_start(idx1[:], offs)
+        load_words(win1[0], tab_words[0])
+        load_scales(win1_s, tab_scales, ROW1)
+        nc.sync.dma_start(idx2[:], offs2)
+        load_words(win1[1], tab_words[1])
+        load_scales(win2_s, tab2_scales, ROW2)
+        load_words(win2[0], tab2_words[0])
+        load_words(win2[1], tab2_words[1])
+        for q in range(4):
+            nc.sync.dma_start(
+                w4_s_raw[32 * q : 32 * q + 4, :].bitcast(I32).rearrange("r (a n) -> r a n", a=2),
+                w4_scales[:, 4 * q : 4 * q + 4, :].bitcast(I32).rearrange("a r n -> r a n"),
+            )
+        w4_raw = held([P, 2 * 2 * N], U8, "w4_raw")
+        nc.sync.dma_start(
+            w4_raw[:].bitcast(I32).rearrange("p (a n) -> p a n", a=2),
+            w4_words.bitcast(I32).rearrange("a p n -> p a n"),
+        )
+        ab = held([P, 2 * PACK], F32, "ab")
+        nc.sync.dma_start(
+            ab[:].rearrange("p (b t) -> p b t", b=2), abund.rearrange("(b p t) -> p b t", b=2, t=PACK)
+        )
+        w_raw = [held([P, PACK, N], F32, "w_raw%d" % b) for b in range(2)]
+        for b in range(2):
+            nc.sync.dma_start(w_raw[b][:], w[b * PASS : (b + 1) * PASS, :].rearrange("(p r) n -> p r n", r=PACK))
+
+        def cols(h):
+            return slice(h * HALF // 16, (h + 1) * HALF // 16)
+
+        v1 = {}
+        v1_s = {}
+        v2 = {}
+        v2_s = {}
+
+        def gather1(h):
+            for a in range(2):
+                v1[a, h] = held([P, HALF], U32, "v1_%d_%d" % (a, h))
+                nc.vector.tensor_copy(
+                    v1[a, h][:].rearrange("p (t m) -> p m t", t=PACK), win1[a][:].indirect(idx1[:, cols(h)])
+                )
+            picked = held([P, HALF], U8, "v1_s_picked%d" % h)
+            nc.vector.tensor_copy(picked[:], win1_s[:].indirect(idx1[:, cols(h)]))
+            v1_s[h] = held([P, HALF], U8, "v1_s%d" % h)
+            nc.vector.tensor_copy(
+                v1_s[h][:].rearrange("p (t m) -> p t m", t=PACK), picked[:].rearrange("p (m t) -> p t m", t=PACK)
+            )
+
+        def gather2(h):
+            v2_s[h] = held([P, HALF], U8, "v2_s%d" % h)
+            nc.vector.tensor_copy(v2_s[h][:], win2_s[:].indirect(idx2[:, cols(h)]))
+            for a in range(2):
+                v2[a, h] = held([P, HALF], U32, "v2_%d_%d" % (a, h))
+                nc.vector.tensor_copy(v2[a, h][:], win2[a][:].indirect(idx2[:, cols(h)]))
+
+        w4 = held([P, 2 * 2 * N], U8, "w4")
+        w4_s = held([P, 2 * N], U8, "w4_s")
+
+        def deal_w4():
+            nc.vector.tensor_copy(
+                w4[:].bitcast(U16).rearrange("p (a t m) -> p a t m", a=2, t=PACK),
+                w4_raw[:].bitcast(U16).rearrange("p (a m t) -> p a t m", a=2, t=PACK),
+            )
+            nc.vector.tensor_copy(
+                w4_s[:].rearrange("p (a t m) -> p a t m", a=2, t=PACK),
+                w4_s_raw[:].rearrange("p (a m t) -> p a t m", a=2, t=PACK),
+            )
+
+        wq = [held([P, N], U32, "wq%d" % b) for b in range(2)]
+        wq_s = [held([P, N], U8, "wq_s%d" % b) for b in range(2)]
+        w_bf = [held([P, N * PACK], BF16, "w_bf%d" % b) for b in range(2)]
+
+        def cast_w(b):
+            nc.vector.tensor_copy(
+                w_bf[b][:].rearrange("p (t m r) -> p m r t", t=PACK, r=PACK),
+                w_raw[b][:].rearrange("p r (m t) -> p m r t", t=PACK),
+            )
+
+        def quant_w(b):
+            nc.vector.quantize_mx(out=wq[b][:].bitcast(FP8X4), scales=wq_s[b][:], in_=w_bf[b][:])
+
+        hq = {}
+        hq_s = {}
+
+        def occupancy(c, b):
+            h, j0 = divmod(c * JC, HALF)
+            sq = work.tile([P, PACK * JC], F32, name="sq")
+            for u in range(2):
+                aff = psum.tile([P, 2 * JC], F32, name="aff", bufs=4)
+                for e in range(2):
+                    m = slice((2 * u + e) * P, (2 * u + e + 1) * P)
+                    for a in range(2):
+                        nc.tensor.matmul_mx(
+                            out=aff[:, e * JC : (e + 1) * JC],
+                            lhsT=v1[a, b][:, m].bitcast(FP8X4),
+                            lhsT_scale=v1_s[b][ROW1 + 4 * a :, m],
+                            rhs=v2[a, h][:, j0 : j0 + JC].bitcast(FP8X4),
+                            rhs_scale=v2_s[h][ROW2 + 4 * a :, j0 : j0 + JC],
+                            start=(a == 0),
+                            stop=(a == 1),
+                        )
+                nc.scalar.activation(sq[:, 2 * u * JC : 2 * (u + 1) * JC], aff[:], ACT.Square)
+            rs = work.tile([P, PACK * JC], F32, name="rs")
+            nc.scalar.activation(rs[:], sq[:], ACT.Abs_reciprocal_sqrt, bias=1.0)
+            inv = work.tile([P, PACK * JC], F32, name="inv")
+            nc.scalar.activation(inv[:], rs[:], ACT.Square)
+            hb = work.tile([P, PACK * JC], BF16, name="hb")
+            for t in range(PACK):
+                s = slice(t * JC, (t + 1) * JC)
+                nc.vector.scalar_tensor_tensor(
+                    hb[:, s], sq[:, s], ab[:, PACK * b + t : PACK * b + t + 1], inv[:, s], ALU.mult, ALU.mult
+                )
+            hi = work.tile([P, PACK * JC], BF16, name="hi", align_bytes=64)
+            nc.vector.tensor_copy(
+                hi[:].rearrange("p (g i t) -> p g t i", i=4, t=PACK),
+                hb[:].rearrange("p (t g i) -> p g t i", i=4, t=PACK),
+            )
+            hq[c, b] = work.tile([P, JC], U32, name="hq", bufs=4, align_bytes=64)
+            hq_s[c, b] = work.tile([P, JC], U8, name="hq_s", bufs=4, align_bytes=64)
+            nc.vector.quantize_mx(out=hq[c, b][:].bitcast(FP8X4), scales=hq_s[c, b][:], in_=hi[:])
+
+        y_s = held([P, S2], U8, "y_s")
+        out_rows = out_0.rearrange("(p t) j -> p t j", t=PACK)
+        out_words = out_1[0].rearrange("p m t -> p (m t)").bitcast(I32)
+
+        def pathways(c):
+            y = work.tile([P, PACK * JC], F32, name="y", bufs=2)
+            for u in range(2):
+                p1 = psum.tile([P, 2 * JC], F32, name="p1")
+                p2 = psum.tile([P, 2 * JC], F32, name="p2")
+                for e in range(2):
+                    m = slice((2 * u + e) * P, (2 * u + e + 1) * P)
+                    for b in range(2):
+                        nc.tensor.matmul_mx(
+                            out=p1[:, e * JC : (e + 1) * JC],
+                            lhsT=wq[b][:, m].bitcast(FP8X4),
+                            lhsT_scale=wq_s[b][:, m],
+                            rhs=hq[c, b][:].bitcast(FP8X4),
+                            rhs_scale=hq_s[c, b][:],
+                            start=(b == 0),
+                            stop=(b == 1),
+                        )
+                for e in range(2):
+                    m0 = (2 * u + e) * P
+                    for j0 in range(0, JC, P):
+                        for b in range(2):
+                            nc.tensor.matmul_mx(
+                                out=p2[:, e * JC + j0 : e * JC + j0 + P],
+                                lhsT=w4[:, 2 * (b * N + m0) : 2 * (b * N + m0 + P)].bitcast(FP4X4),
+                                lhsT_scale=w4_s[:, b * N + m0 : b * N + m0 + P],
+                                rhs=hq[c, b][:, j0 : j0 + P].bitcast(FP8X4),
+                                rhs_scale=hq_s[c, b][:, j0 : j0 + P],
+                                start=(b == 0),
+                                stop=(b == 1),
+                            )
+                first = work.tile([P, 2 * JC], F32, name="first")
+                nc.scalar.copy(first[:], p1[:])
+                nc.vector.tensor_tensor(y[:, 2 * u * JC : 2 * (u + 1) * JC], p2[:], first[:], ALU.mult)
+            js = slice(c * JC, (c + 1) * JC)
+            nc.sync.dma_start(out_rows[:, :, js], y[:].rearrange("p (t j) -> p t j", t=PACK))
+            yi = work.tile([P, PACK * JC], BF16, name="yi", bufs=2, align_bytes=64)
+            nc.vector.tensor_copy(
+                yi[:].rearrange("p (g i t) -> p g t i", i=4, t=PACK),
+                y[:].rearrange("p (t g i) -> p g t i", i=4, t=PACK),
+            )
+            yq = work.tile([P, JC], U32, name="yq", bufs=2, align_bytes=64)
+            nc.vector.quantize_mx(out=yq[:].bitcast(FP8X4), scales=y_s[:, js], in_=yi[:])
+            nc.sync.dma_start(out_words[:, js], yq[:].bitcast(I32))
+
+        gather1(0)
+        gather2(0)
+        gather1(1)
+        occupancy(0, 0)
+        deal_w4()
+        gather2(1)
+        occupancy(0, 1)
+        cast_w(0)
+        cast_w(1)
+        quant_w(0)
+        quant_w(1)
+        chunks = S2 // JC
+        for c in range(1, chunks):
+            occupancy(c, 0)
+            pathways(c - 1)
+            occupancy(c, 1)
+        pathways(chunks - 1)
+        for q in range(4):
+            nc.sync.dma_start(out_2[0, 4 * q : 4 * q + 4, :].bitcast(I32), y_s[32 * q : 32 * q + 4, :].bitcast(I32))

@@ -20,7 +20,8 @@ P = 128
 PACK = 4
 PASS = P * PACK
 HALF = 512
-JC = 256
+CHUNKS = (256, 256, 256, 128, 128)
+BANK = 512
 ROW1 = 0
 ROW2 = 8
 
@@ -35,13 +36,13 @@ def tile_list_motif_promoter_activity_kernel(
         work = ctx.enter_context(tc.tile_pool(name="work", bufs=3))
         psum = ctx.enter_context(tc.psum_pool(name="psum", bufs=2))
 
-        def held(shape, dtype, name):
-            return keep.tile(shape, dtype, name=name, align_bytes=64)
+        def held(shape, dtype, name, tag=""):
+            return keep.tile(shape, dtype, name=name, tag=tag, align_bytes=64)
 
         win1_s = held([P, T1], U8, "win1_s")
         win2_s = held([P, T2], U8, "win2_s")
-        w4_s_raw = held([P, 2 * N], U8, "w4_s_raw")
-        nc.vector.memset(win1_s[:].bitcast(I32), 0)
+        w4_s_raw = held([P, 2 * N], U8, "w4_s_raw", tag="late_s")
+        nc.gpsimd.memset(win1_s[:].bitcast(I32), 0)
         nc.vector.memset(win2_s[:].bitcast(I32), 0)
         nc.vector.memset(w4_s_raw[:].bitcast(I32), 0)
         one = held([P, 1], F32, "one")
@@ -57,35 +58,32 @@ def tile_list_motif_promoter_activity_kernel(
         def load_words(dst, src):
             nc.sync.dma_start(dst[:].bitcast(I32), src.rearrange("p n t -> p (n t)").bitcast(I32))
 
-        def load_scales(win, src, row):
+        nc.sync.dma_start(idx1[:], offs)
+        load_words(win1[0], tab_words[0])
+        nc.sync.dma_start(idx2[:], offs2)
+        ab = held([P, 2 * PACK], F32, "ab")
+        nc.sync.dma_start(
+            ab[:].rearrange("p (b t) -> p b t", b=2), abund.rearrange("(b p t) -> p b t", b=2, t=PACK)
+        )
+        load_words(win1[1], tab_words[1])
+        load_words(win2[0], tab2_words[0])
+        load_words(win2[1], tab2_words[1])
+        for win, src, row in ((win1_s, tab_scales, ROW1), (win2_s, tab2_scales, ROW2)):
             for q in range(4):
-                nc.sync.dma_start(
+                nc.gpsimd.dma_start(
                     win[32 * q + row : 32 * q + row + 8, :].bitcast(I32),
                     src[:, 4 * q : 4 * q + 4, :].bitcast(I32),
                 )
-
-        nc.sync.dma_start(idx1[:], offs)
-        load_words(win1[0], tab_words[0])
-        load_scales(win1_s, tab_scales, ROW1)
-        nc.sync.dma_start(idx2[:], offs2)
-        load_words(win1[1], tab_words[1])
-        load_scales(win2_s, tab2_scales, ROW2)
-        load_words(win2[0], tab2_words[0])
-        load_words(win2[1], tab2_words[1])
+        w4_raw = held([P, 2 * 2 * N], U8, "w4_raw", tag="late_w")
+        nc.sync.dma_start(
+            w4_raw[:].bitcast(I32).rearrange("p (a n) -> p a n", a=2),
+            w4_words.bitcast(I32).rearrange("a p n -> p a n"),
+        )
         for q in range(4):
             nc.sync.dma_start(
                 w4_s_raw[32 * q : 32 * q + 4, :].bitcast(I32).rearrange("r (a n) -> r a n", a=2),
                 w4_scales[:, 4 * q : 4 * q + 4, :].bitcast(I32).rearrange("a r n -> r a n"),
             )
-        w4_raw = held([P, 2 * 2 * N], U8, "w4_raw")
-        nc.sync.dma_start(
-            w4_raw[:].bitcast(I32).rearrange("p (a n) -> p a n", a=2),
-            w4_words.bitcast(I32).rearrange("a p n -> p a n"),
-        )
-        ab = held([P, 2 * PACK], F32, "ab")
-        nc.sync.dma_start(
-            ab[:].rearrange("p (b t) -> p b t", b=2), abund.rearrange("(b p t) -> p b t", b=2, t=PACK)
-        )
         w_raw = [held([P, PACK, N], F32, "w_raw%d" % b) for b in range(2)]
         for b in range(2):
             nc.sync.dma_start(w_raw[b][:], w[b * PASS : (b + 1) * PASS, :].rearrange("(p r) n -> p r n", r=PACK))
@@ -112,10 +110,10 @@ def tile_list_motif_promoter_activity_kernel(
             )
 
         def gather2(h):
-            v2_s[h] = held([P, HALF], U8, "v2_s%d" % h)
+            v2_s[h] = held([P, HALF], U8, "v2_s%d" % h, tag="late_s" if h else "")
             nc.vector.tensor_copy(v2_s[h][:], win2_s[:].indirect(idx2[:, cols(h)]))
             for a in range(2):
-                v2[a, h] = held([P, HALF], U32, "v2_%d_%d" % (a, h))
+                v2[a, h] = held([P, HALF], U32, "v2_%d_%d" % (a, h), tag="late_w" if (a, h) == (0, 1) else "")
                 nc.vector.tensor_copy(v2[a, h][:], win2[a][:].indirect(idx2[:, cols(h)]))
 
         w4 = held([P, 2 * 2 * N], U8, "w4")
@@ -147,41 +145,48 @@ def tile_list_motif_promoter_activity_kernel(
         hq = {}
         hq_s = {}
 
-        def occupancy(c, b):
-            h, j0 = divmod(c * JC, HALF)
-            sq = work.tile([P, PACK * JC], F32, name="sq")
-            for u in range(2):
-                aff = psum.tile([P, 2 * JC], F32, name="aff", bufs=4)
-                for e in range(2):
-                    m = slice((2 * u + e) * P, (2 * u + e + 1) * P)
-                    for a in range(2):
+        starts = [sum(CHUNKS[:c]) for c in range(len(CHUNKS))]
+
+        def occupancy(c, b, by_bank=False):
+            jc = CHUNKS[c]
+            per_bank = BANK // jc
+            h, j0 = divmod(starts[c], HALF)
+            sq = work.tile([P, PACK * jc], F32, name="sq")
+            rs = work.tile([P, PACK * jc], F32, name="rs")
+            inv = work.tile([P, PACK * jc], F32, name="inv")
+            for u in range(PACK // per_bank):
+                aff = psum.tile([P, BANK], F32, name="aff", bufs=4)
+                for a in range(2):
+                    for e in range(per_bank):
+                        m = slice((per_bank * u + e) * P, (per_bank * u + e + 1) * P)
                         nc.tensor.matmul_mx(
-                            out=aff[:, e * JC : (e + 1) * JC],
+                            out=aff[:, e * jc : (e + 1) * jc],
                             lhsT=v1[a, b][:, m].bitcast(FP8X4),
                             lhsT_scale=v1_s[b][ROW1 + 4 * a :, m],
-                            rhs=v2[a, h][:, j0 : j0 + JC].bitcast(FP8X4),
-                            rhs_scale=v2_s[h][ROW2 + 4 * a :, j0 : j0 + JC],
-                            start=(a == 0),
-                            stop=(a == 1),
+                            rhs=v2[a, h][:, j0 : j0 + jc].bitcast(FP8X4),
+                            rhs_scale=v2_s[h][ROW2 + 4 * a :, j0 : j0 + jc],
+                            start=(a == 0 and e == 0),
+                            stop=(a == 1 and e == per_bank - 1),
                         )
-                nc.scalar.activation(sq[:, 2 * u * JC : 2 * (u + 1) * JC], aff[:], ACT.Square)
-            rs = work.tile([P, PACK * JC], F32, name="rs")
-            nc.scalar.activation(rs[:], sq[:], ACT.Abs_reciprocal_sqrt, bias=1.0)
-            inv = work.tile([P, PACK * JC], F32, name="inv")
-            nc.scalar.activation(inv[:], rs[:], ACT.Square)
-            hb = work.tile([P, PACK * JC], BF16, name="hb")
+                nc.scalar.activation(sq[:, u * BANK : (u + 1) * BANK], aff[:], ACT.Square)
+            step = BANK if by_bank else min(2 * BANK, PACK * jc)
+            for s0 in range(0, PACK * jc, step):
+                nc.scalar.activation(rs[:, s0 : s0 + step], sq[:, s0 : s0 + step], ACT.Abs_reciprocal_sqrt, bias=1.0)
+            for s0 in range(0, PACK * jc, step):
+                nc.scalar.activation(inv[:, s0 : s0 + step], rs[:, s0 : s0 + step], ACT.Square)
+            hb = work.tile([P, PACK * jc], BF16, name="hb")
             for t in range(PACK):
-                s = slice(t * JC, (t + 1) * JC)
+                s = slice(t * jc, (t + 1) * jc)
                 nc.vector.scalar_tensor_tensor(
                     hb[:, s], sq[:, s], ab[:, PACK * b + t : PACK * b + t + 1], inv[:, s], ALU.mult, ALU.mult
                 )
-            hi = work.tile([P, PACK * JC], BF16, name="hi", align_bytes=64)
+            hi = work.tile([P, PACK * jc], BF16, name="hi", align_bytes=64)
             nc.vector.tensor_copy(
                 hi[:].rearrange("p (g i t) -> p g t i", i=4, t=PACK),
                 hb[:].rearrange("p (t g i) -> p g t i", i=4, t=PACK),
             )
-            hq[c, b] = work.tile([P, JC], U32, name="hq", bufs=4, align_bytes=64)
-            hq_s[c, b] = work.tile([P, JC], U8, name="hq_s", bufs=4, align_bytes=64)
+            hq[c, b] = work.tile([P, jc], U32, name="hq", bufs=4, align_bytes=64)
+            hq_s[c, b] = work.tile([P, jc], U8, name="hq_s", bufs=4, align_bytes=64)
             nc.vector.quantize_mx(out=hq[c, b][:].bitcast(FP8X4), scales=hq_s[c, b][:], in_=hi[:])
 
         y_s = held([P, S2], U8, "y_s")
@@ -189,53 +194,55 @@ def tile_list_motif_promoter_activity_kernel(
         out_words = out_1[0].rearrange("p m t -> p (m t)").bitcast(I32)
 
         def pathways(c):
-            y = work.tile([P, PACK * JC], F32, name="y", bufs=2)
-            for u in range(2):
-                p1 = psum.tile([P, 2 * JC], F32, name="p1")
-                p2 = psum.tile([P, 2 * JC], F32, name="p2")
-                for e in range(2):
-                    m = slice((2 * u + e) * P, (2 * u + e + 1) * P)
-                    for b in range(2):
+            jc = CHUNKS[c]
+            per_bank = BANK // jc
+            y = work.tile([P, PACK * jc], F32, name="y", bufs=2)
+            for u in range(PACK // per_bank):
+                p1 = psum.tile([P, BANK], F32, name="p1")
+                p2 = psum.tile([P, BANK], F32, name="p2")
+                for b in range(2):
+                    for e in range(per_bank):
+                        m = slice((per_bank * u + e) * P, (per_bank * u + e + 1) * P)
                         nc.tensor.matmul_mx(
-                            out=p1[:, e * JC : (e + 1) * JC],
+                            out=p1[:, e * jc : (e + 1) * jc],
                             lhsT=wq[b][:, m].bitcast(FP8X4),
                             lhsT_scale=wq_s[b][:, m],
                             rhs=hq[c, b][:].bitcast(FP8X4),
                             rhs_scale=hq_s[c, b][:],
-                            start=(b == 0),
-                            stop=(b == 1),
+                            start=(b == 0 and e == 0),
+                            stop=(b == 1 and e == per_bank - 1),
                         )
-                for e in range(2):
-                    m0 = (2 * u + e) * P
-                    for j0 in range(0, JC, P):
-                        for b in range(2):
+                for b in range(2):
+                    for e in range(per_bank):
+                        m0 = (per_bank * u + e) * P
+                        for j0 in range(0, jc, P):
                             nc.tensor.matmul_mx(
-                                out=p2[:, e * JC + j0 : e * JC + j0 + P],
+                                out=p2[:, e * jc + j0 : e * jc + j0 + P],
                                 lhsT=w4[:, 2 * (b * N + m0) : 2 * (b * N + m0 + P)].bitcast(FP4X4),
                                 lhsT_scale=w4_s[:, b * N + m0 : b * N + m0 + P],
                                 rhs=hq[c, b][:, j0 : j0 + P].bitcast(FP8X4),
                                 rhs_scale=hq_s[c, b][:, j0 : j0 + P],
-                                start=(b == 0),
-                                stop=(b == 1),
+                                start=(b == 0 and e == 0 and j0 == 0),
+                                stop=(b == 1 and e == per_bank - 1 and j0 == jc - P),
                             )
-                first = work.tile([P, 2 * JC], F32, name="first")
+                first = work.tile([P, BANK], F32, name="first")
                 nc.scalar.copy(first[:], p1[:])
-                nc.vector.tensor_tensor(y[:, 2 * u * JC : 2 * (u + 1) * JC], p2[:], first[:], ALU.mult)
-            js = slice(c * JC, (c + 1) * JC)
+                nc.vector.tensor_tensor(y[:, u * BANK : (u + 1) * BANK], p2[:], first[:], ALU.mult)
+            js = slice(starts[c], starts[c] + jc)
             nc.sync.dma_start(out_rows[:, :, js], y[:].rearrange("p (t j) -> p t j", t=PACK))
-            yi = work.tile([P, PACK * JC], BF16, name="yi", bufs=2, align_bytes=64)
+            yi = work.tile([P, PACK * jc], BF16, name="yi", bufs=2, align_bytes=64)
             nc.vector.tensor_copy(
                 yi[:].rearrange("p (g i t) -> p g t i", i=4, t=PACK),
                 y[:].rearrange("p (t g i) -> p g t i", i=4, t=PACK),
             )
-            yq = work.tile([P, JC], U32, name="yq", bufs=2, align_bytes=64)
+            yq = work.tile([P, jc], U32, name="yq", bufs=2, align_bytes=64)
             nc.vector.quantize_mx(out=yq[:].bitcast(FP8X4), scales=y_s[:, js], in_=yi[:])
             nc.sync.dma_start(out_words[:, js], yq[:].bitcast(I32))
 
         gather1(0)
         gather2(0)
         gather1(1)
-        occupancy(0, 0)
+        occupancy(0, 0, by_bank=True)
         deal_w4()
         gather2(1)
         occupancy(0, 1)
@@ -243,11 +250,11 @@ def tile_list_motif_promoter_activity_kernel(
         cast_w(1)
         quant_w(0)
         quant_w(1)
-        chunks = S2 // JC
-        for c in range(1, chunks):
+        for c in range(1, len(CHUNKS)):
             occupancy(c, 0)
             pathways(c - 1)
             occupancy(c, 1)
-        pathways(chunks - 1)
+        pathways(len(CHUNKS) - 1)
         for q in range(4):
-            nc.sync.dma_start(out_2[0, 4 * q : 4 * q + 4, :].bitcast(I32), y_s[32 * q : 32 * q + 4, :].bitcast(I32))
+            queue = nc.scalar if q % 2 else nc.sync
+            queue.dma_start(out_2[0, 4 * q : 4 * q + 4, :].bitcast(I32), y_s[32 * q : 32 * q + 4, :].bitcast(I32))

@@ -19,11 +19,13 @@ ALU = mybir.AluOpType
 P = 128
 PACK = 4
 PASS = P * PACK
+PASSES = 2
 HALF = 512
-CHUNKS = (256, 256, 256, 128, 128)
 BANK = 512
-ROW1 = 0
-ROW2 = 8
+LINE = 4
+CHUNKS = (256, 256, 256, 128, 128)
+ROW1, ROW2 = 0, 8
+AHEAD = 5
 
 
 def tile_list_motif_promoter_activity_kernel(
@@ -39,154 +41,162 @@ def tile_list_motif_promoter_activity_kernel(
         def held(shape, dtype, name, tag=""):
             return keep.tile(shape, dtype, name=name, tag=tag, align_bytes=64)
 
+        def interleave(dst, src):
+            nc.vector.tensor_copy(
+                dst[:].rearrange("p (g i t) -> p g t i", i=LINE, t=PACK),
+                src[:].rearrange("p (t g i) -> p g t i", i=LINE, t=PACK),
+            )
+
         win1_s = held([P, T1], U8, "win1_s")
         win2_s = held([P, T2], U8, "win2_s")
-        w4_s_raw = held([P, 2 * N], U8, "w4_s_raw", tag="late_s")
-        nc.gpsimd.memset(win1_s[:].bitcast(I32), 0)
-        nc.vector.memset(win2_s[:].bitcast(I32), 0)
-        nc.vector.memset(w4_s_raw[:].bitcast(I32), 0)
+        w4_s_raw = held([P, PASSES * N], U8, "w4_s_raw", tag="after_w4_s")
         one = held([P, 1], F32, "one")
-        warm = held([P, 1], F32, "warm")
-        nc.vector.memset(one[:], 1.0)
-        nc.scalar.activation(warm[:], one[:], ACT.Abs_reciprocal_sqrt)
+        nc.vector.memset(win2_s[:].bitcast(I32), 0)
+        nc.gpsimd.memset(one[:], 1.0)
+        nc.gpsimd.memset(win1_s[:].bitcast(I32), 0)
+        nc.gpsimd.memset(w4_s_raw[:].bitcast(I32), 0)
+        unit = held([P, 1], F32, "unit")
+        nc.scalar.activation(unit[:], one[:], ACT.Abs_reciprocal_sqrt)
 
         idx1 = keep.tile([P, S1 // 16], U16, name="idx1")
         idx2 = keep.tile([P, S2 // 16], U16, name="idx2")
-        win1 = [held([P, T1], U32, "win1_%d" % a) for a in range(2)]
-        win2 = [held([P, T2], U32, "win2_%d" % a) for a in range(2)]
+        win1 = [held([P, T1], U32, "win1_%d" % a) for a in range(PASSES)]
+        win2 = [held([P, T2], U32, "win2_%d" % a) for a in range(PASSES)]
 
-        def load_words(dst, src):
-            nc.sync.dma_start(dst[:].bitcast(I32), src.rearrange("p n t -> p (n t)").bitcast(I32))
+        def load_words(dst, src, pieces):
+            words = src.rearrange("p n t -> p (n t)").bitcast(I32)
+            step = words.shape[1] // pieces
+            for c0 in range(0, words.shape[1], step):
+                nc.sync.dma_start(dst[:, c0 : c0 + step].bitcast(I32), words[:, c0 : c0 + step])
 
-        nc.sync.dma_start(idx1[:], offs)
-        load_words(win1[0], tab_words[0])
-        nc.sync.dma_start(idx2[:], offs2)
-        ab = held([P, 2 * PACK], F32, "ab")
-        nc.sync.dma_start(
-            ab[:].rearrange("p (b t) -> p b t", b=2), abund.rearrange("(b p t) -> p b t", b=2, t=PACK)
-        )
-        load_words(win1[1], tab_words[1])
-        load_words(win2[0], tab2_words[0])
-        load_words(win2[1], tab2_words[1])
-        for win, src, row in ((win1_s, tab_scales, ROW1), (win2_s, tab2_scales, ROW2)):
+        def load_scales(queue, win, src, row):
             for q in range(4):
-                nc.gpsimd.dma_start(
-                    win[32 * q + row : 32 * q + row + 8, :].bitcast(I32),
+                queue.dma_start(
+                    win[32 * q + row : 32 * q + row + 4 * PASSES, :].bitcast(I32),
                     src[:, 4 * q : 4 * q + 4, :].bitcast(I32),
                 )
-        w4_raw = held([P, 2 * 2 * N], U8, "w4_raw", tag="late_w")
+
+        load_scales(nc.gpsimd, win2_s, tab2_scales, ROW2)
+        nc.sync.dma_start(idx1[:], offs)
+        load_words(win1[0], tab_words[0], 2)
+        load_words(win1[1], tab_words[1], 2)
+        nc.sync.dma_start(idx2[:], offs2)
+        ab = held([P, PASSES * PACK], F32, "ab")
         nc.sync.dma_start(
-            w4_raw[:].bitcast(I32).rearrange("p (a n) -> p a n", a=2),
-            w4_words.bitcast(I32).rearrange("a p n -> p a n"),
+            ab[:].rearrange("p (b t) -> p b t", b=PASSES), abund.rearrange("(b p t) -> p b t", b=PASSES, t=PACK)
+        )
+        load_scales(nc.sync, win1_s, tab_scales, ROW1)
+        load_words(win2[0], tab2_words[0], 1)
+        load_words(win2[1], tab2_words[1], 1)
+        w4_raw = held([P, PASSES * 2 * N], U8, "w4_raw", tag="after_w4")
+        nc.sync.dma_start(
+            w4_raw[:].bitcast(I32).rearrange("p (b n) -> p b n", b=PASSES),
+            w4_words.bitcast(I32).rearrange("b p n -> p b n"),
         )
         for q in range(4):
             nc.sync.dma_start(
-                w4_s_raw[32 * q : 32 * q + 4, :].bitcast(I32).rearrange("r (a n) -> r a n", a=2),
-                w4_scales[:, 4 * q : 4 * q + 4, :].bitcast(I32).rearrange("a r n -> r a n"),
+                w4_s_raw[32 * q : 32 * q + 4, :].bitcast(I32).rearrange("r (b n) -> r b n", b=PASSES),
+                w4_scales[:, 4 * q : 4 * q + 4, :].bitcast(I32).rearrange("b r n -> r b n"),
             )
-        w_raw = [held([P, PACK, N], F32, "w_raw%d" % b) for b in range(2)]
-        for b in range(2):
+        w_raw = [held([P, PACK, N], F32, "w_raw%d" % b) for b in range(PASSES)]
+        for b in range(PASSES):
             nc.sync.dma_start(w_raw[b][:], w[b * PASS : (b + 1) * PASS, :].rearrange("(p r) n -> p r n", r=PACK))
 
-        def cols(h):
-            return slice(h * HALF // 16, (h + 1) * HALF // 16)
+        v1, v1_s, v2, v2_s = {}, {}, {}, {}
 
-        v1 = {}
-        v1_s = {}
-        v2 = {}
-        v2_s = {}
+        def entries(half):
+            return slice(half * HALF // 16, (half + 1) * HALF // 16)
 
-        def gather1(h):
-            for a in range(2):
-                v1[a, h] = held([P, HALF], U32, "v1_%d_%d" % (a, h))
+        def gather1(half):
+            for a in range(PASSES):
+                tag = "after_deal" if (a, half) == (0, 1) else ""
+                v1[a, half] = held([P, HALF], U32, "v1_%d_%d" % (a, half), tag=tag)
                 nc.vector.tensor_copy(
-                    v1[a, h][:].rearrange("p (t m) -> p m t", t=PACK), win1[a][:].indirect(idx1[:, cols(h)])
+                    v1[a, half][:].rearrange("p (t m) -> p m t", t=PACK), win1[a][:].indirect(idx1[:, entries(half)])
                 )
-            picked = held([P, HALF], U8, "v1_s_picked%d" % h)
-            nc.vector.tensor_copy(picked[:], win1_s[:].indirect(idx1[:, cols(h)]))
-            v1_s[h] = held([P, HALF], U8, "v1_s%d" % h)
+            picked = held([P, HALF], U8, "v1_s_picked%d" % half, tag="" if half else "after_deal")
+            nc.vector.tensor_copy(picked[:], win1_s[:].indirect(idx1[:, entries(half)]))
+            v1_s[half] = held([P, HALF], U8, "v1_s%d" % half)
             nc.vector.tensor_copy(
-                v1_s[h][:].rearrange("p (t m) -> p t m", t=PACK), picked[:].rearrange("p (m t) -> p t m", t=PACK)
+                v1_s[half][:].rearrange("p (t m) -> p t m", t=PACK), picked[:].rearrange("p (m t) -> p t m", t=PACK)
             )
 
-        def gather2(h):
-            v2_s[h] = held([P, HALF], U8, "v2_s%d" % h, tag="late_s" if h else "")
-            nc.vector.tensor_copy(v2_s[h][:], win2_s[:].indirect(idx2[:, cols(h)]))
-            for a in range(2):
-                v2[a, h] = held([P, HALF], U32, "v2_%d_%d" % (a, h), tag="late_w" if (a, h) == (0, 1) else "")
-                nc.vector.tensor_copy(v2[a, h][:], win2[a][:].indirect(idx2[:, cols(h)]))
+        def gather2(half):
+            v2_s[half] = held([P, HALF], U8, "v2_s%d" % half, tag="after_w4_s" if half else "")
+            nc.vector.tensor_copy(v2_s[half][:], win2_s[:].indirect(idx2[:, entries(half)]))
+            for a in range(PASSES):
+                tag = "after_w4" if (a, half) == (0, 1) else ""
+                v2[a, half] = held([P, HALF], U32, "v2_%d_%d" % (a, half), tag=tag)
+                nc.vector.tensor_copy(v2[a, half][:], win2[a][:].indirect(idx2[:, entries(half)]))
 
-        w4 = held([P, 2 * 2 * N], U8, "w4")
-        w4_s = held([P, 2 * N], U8, "w4_s")
+        w4 = held([P, PASSES * 2 * N], U8, "w4")
+        w4_s = held([P, PASSES * N], U8, "w4_s")
 
         def deal_w4():
             nc.vector.tensor_copy(
-                w4[:].bitcast(U16).rearrange("p (a t m) -> p a t m", a=2, t=PACK),
-                w4_raw[:].bitcast(U16).rearrange("p (a m t) -> p a t m", a=2, t=PACK),
+                w4[:].bitcast(U16).rearrange("p (b t m) -> p b t m", b=PASSES, t=PACK),
+                w4_raw[:].bitcast(U16).rearrange("p (b m t) -> p b t m", b=PASSES, t=PACK),
             )
             nc.vector.tensor_copy(
-                w4_s[:].rearrange("p (a t m) -> p a t m", a=2, t=PACK),
-                w4_s_raw[:].rearrange("p (a m t) -> p a t m", a=2, t=PACK),
+                w4_s[:].rearrange("p (b t m) -> p b t m", b=PASSES, t=PACK),
+                w4_s_raw[:].rearrange("p (b m t) -> p b t m", b=PASSES, t=PACK),
             )
 
-        wq = [held([P, N], U32, "wq%d" % b) for b in range(2)]
-        wq_s = [held([P, N], U8, "wq_s%d" % b) for b in range(2)]
-        w_bf = [held([P, N * PACK], BF16, "w_bf%d" % b) for b in range(2)]
+        wq = [held([P, N], U32, "wq%d" % b) for b in range(PASSES)]
+        wq_s = [held([P, N], U8, "wq_s%d" % b) for b in range(PASSES)]
+        w_bf = [held([P, N * PACK], BF16, "w_bf%d" % b) for b in range(PASSES)]
 
-        def cast_w(b):
-            nc.vector.tensor_copy(
-                w_bf[b][:].rearrange("p (t m r) -> p m r t", t=PACK, r=PACK),
-                w_raw[b][:].rearrange("p r (m t) -> p m r t", t=PACK),
-            )
-
-        def quant_w(b):
-            nc.vector.quantize_mx(out=wq[b][:].bitcast(FP8X4), scales=wq_s[b][:], in_=w_bf[b][:])
-
-        hq = {}
-        hq_s = {}
+        def quantise_w():
+            for b in range(PASSES):
+                nc.vector.tensor_copy(
+                    w_bf[b][:].rearrange("p (t m r) -> p m t r", t=PACK, r=PACK),
+                    w_raw[b][:].rearrange("p r (m t) -> p m t r", t=PACK),
+                )
+            for b in range(PASSES):
+                nc.vector.quantize_mx(out=wq[b][:].bitcast(FP8X4), scales=wq_s[b][:], in_=w_bf[b][:])
 
         starts = [sum(CHUNKS[:c]) for c in range(len(CHUNKS))]
+        hq, hq_s = {}, {}
 
-        def occupancy(c, b, by_bank=False):
+        def occupancy(c, b, banks_a_step=2):
             jc = CHUNKS[c]
             per_bank = BANK // jc
-            h, j0 = divmod(starts[c], HALF)
-            sq = work.tile([P, PACK * jc], F32, name="sq")
+            half, j0 = divmod(starts[c], HALF)
+            sq = work.tile([P, PACK * jc], F32, name="sq", bufs=AHEAD)
             rs = work.tile([P, PACK * jc], F32, name="rs")
-            inv = work.tile([P, PACK * jc], F32, name="inv")
+            inv = work.tile([P, PACK * jc], F32, name="inv", bufs=AHEAD)
             for u in range(PACK // per_bank):
                 aff = psum.tile([P, BANK], F32, name="aff", bufs=4)
-                for a in range(2):
+                for a in range(PASSES):
                     for e in range(per_bank):
                         m = slice((per_bank * u + e) * P, (per_bank * u + e + 1) * P)
                         nc.tensor.matmul_mx(
                             out=aff[:, e * jc : (e + 1) * jc],
                             lhsT=v1[a, b][:, m].bitcast(FP8X4),
                             lhsT_scale=v1_s[b][ROW1 + 4 * a :, m],
-                            rhs=v2[a, h][:, j0 : j0 + jc].bitcast(FP8X4),
-                            rhs_scale=v2_s[h][ROW2 + 4 * a :, j0 : j0 + jc],
+                            rhs=v2[a, half][:, j0 : j0 + jc].bitcast(FP8X4),
+                            rhs_scale=v2_s[half][ROW2 + 4 * a :, j0 : j0 + jc],
                             start=(a == 0 and e == 0),
-                            stop=(a == 1 and e == per_bank - 1),
+                            stop=(a == PASSES - 1 and e == per_bank - 1),
                         )
                 nc.scalar.activation(sq[:, u * BANK : (u + 1) * BANK], aff[:], ACT.Square)
-            step = BANK if by_bank else min(2 * BANK, PACK * jc)
+            step = min(banks_a_step * BANK, PACK * jc)
             for s0 in range(0, PACK * jc, step):
-                nc.scalar.activation(rs[:, s0 : s0 + step], sq[:, s0 : s0 + step], ACT.Abs_reciprocal_sqrt, bias=1.0)
+                nc.scalar.activation(
+                    rs[:, s0 : s0 + step], sq[:, s0 : s0 + step], ACT.Abs_reciprocal_sqrt, bias=unit[:]
+                )
             for s0 in range(0, PACK * jc, step):
                 nc.scalar.activation(inv[:, s0 : s0 + step], rs[:, s0 : s0 + step], ACT.Square)
-            hb = work.tile([P, PACK * jc], BF16, name="hb")
+            hb = work.tile([P, PACK * jc], BF16, name="hb", bufs=AHEAD - 1)
             for t in range(PACK):
-                s = slice(t * jc, (t + 1) * jc)
+                cols = slice(t * jc, (t + 1) * jc)
                 nc.vector.scalar_tensor_tensor(
-                    hb[:, s], sq[:, s], ab[:, PACK * b + t : PACK * b + t + 1], inv[:, s], ALU.mult, ALU.mult
+                    hb[:, cols], sq[:, cols], ab[:, PACK * b + t : PACK * b + t + 1], inv[:, cols], ALU.mult, ALU.mult
                 )
-            hi = work.tile([P, PACK * jc], BF16, name="hi", align_bytes=64)
-            nc.vector.tensor_copy(
-                hi[:].rearrange("p (g i t) -> p g t i", i=4, t=PACK),
-                hb[:].rearrange("p (t g i) -> p g t i", i=4, t=PACK),
-            )
-            hq[c, b] = work.tile([P, jc], U32, name="hq", bufs=4, align_bytes=64)
-            hq_s[c, b] = work.tile([P, jc], U8, name="hq_s", bufs=4, align_bytes=64)
+            hi = work.tile([P, PACK * jc], BF16, name="hi", bufs=AHEAD - 1, align_bytes=64)
+            interleave(hi, hb)
+            hq[c, b] = work.tile([P, jc], U32, name="hq", bufs=AHEAD + 1, align_bytes=64)
+            hq_s[c, b] = work.tile([P, jc], U8, name="hq_s", bufs=AHEAD + 1, align_bytes=64)
             nc.vector.quantize_mx(out=hq[c, b][:].bitcast(FP8X4), scales=hq_s[c, b][:], in_=hi[:])
 
         y_s = held([P, S2], U8, "y_s")
@@ -196,11 +206,11 @@ def tile_list_motif_promoter_activity_kernel(
         def pathways(c):
             jc = CHUNKS[c]
             per_bank = BANK // jc
-            y = work.tile([P, PACK * jc], F32, name="y", bufs=2)
+            y = work.tile([P, PACK * jc], F32, name="y")
             for u in range(PACK // per_bank):
                 p1 = psum.tile([P, BANK], F32, name="p1")
                 p2 = psum.tile([P, BANK], F32, name="p2")
-                for b in range(2):
+                for b in range(PASSES):
                     for e in range(per_bank):
                         m = slice((per_bank * u + e) * P, (per_bank * u + e + 1) * P)
                         nc.tensor.matmul_mx(
@@ -210,50 +220,44 @@ def tile_list_motif_promoter_activity_kernel(
                             rhs=hq[c, b][:].bitcast(FP8X4),
                             rhs_scale=hq_s[c, b][:],
                             start=(b == 0 and e == 0),
-                            stop=(b == 1 and e == per_bank - 1),
+                            stop=(b == PASSES - 1 and e == per_bank - 1),
                         )
-                for b in range(2):
+                for b in range(PASSES):
                     for e in range(per_bank):
-                        m0 = (per_bank * u + e) * P
+                        m0 = b * N + (per_bank * u + e) * P
                         for j0 in range(0, jc, P):
                             nc.tensor.matmul_mx(
                                 out=p2[:, e * jc + j0 : e * jc + j0 + P],
-                                lhsT=w4[:, 2 * (b * N + m0) : 2 * (b * N + m0 + P)].bitcast(FP4X4),
-                                lhsT_scale=w4_s[:, b * N + m0 : b * N + m0 + P],
+                                lhsT=w4[:, 2 * m0 : 2 * (m0 + P)].bitcast(FP4X4),
+                                lhsT_scale=w4_s[:, m0 : m0 + P],
                                 rhs=hq[c, b][:, j0 : j0 + P].bitcast(FP8X4),
                                 rhs_scale=hq_s[c, b][:, j0 : j0 + P],
                                 start=(b == 0 and e == 0 and j0 == 0),
-                                stop=(b == 1 and e == per_bank - 1 and j0 == jc - P),
+                                stop=(b == PASSES - 1 and e == per_bank - 1 and j0 == jc - P),
                             )
-                first = work.tile([P, BANK], F32, name="first")
+                first = work.tile([P, BANK], F32, name="first", bufs=AHEAD - 1)
                 nc.scalar.copy(first[:], p1[:])
                 nc.vector.tensor_tensor(y[:, u * BANK : (u + 1) * BANK], p2[:], first[:], ALU.mult)
-            js = slice(starts[c], starts[c] + jc)
-            nc.sync.dma_start(out_rows[:, :, js], y[:].rearrange("p (t j) -> p t j", t=PACK))
+            genes = slice(starts[c], starts[c] + jc)
+            nc.sync.dma_start(out_rows[:, :, genes], y[:].rearrange("p (t j) -> p t j", t=PACK))
             yi = work.tile([P, PACK * jc], BF16, name="yi", bufs=2, align_bytes=64)
-            nc.vector.tensor_copy(
-                yi[:].rearrange("p (g i t) -> p g t i", i=4, t=PACK),
-                y[:].rearrange("p (t g i) -> p g t i", i=4, t=PACK),
-            )
+            interleave(yi, y)
             yq = work.tile([P, jc], U32, name="yq", bufs=2, align_bytes=64)
-            nc.vector.quantize_mx(out=yq[:].bitcast(FP8X4), scales=y_s[:, js], in_=yi[:])
-            nc.sync.dma_start(out_words[:, js], yq[:].bitcast(I32))
+            nc.vector.quantize_mx(out=yq[:].bitcast(FP8X4), scales=y_s[:, genes], in_=yi[:])
+            nc.sync.dma_start(out_words[:, genes], yq[:].bitcast(I32))
 
         gather1(0)
         gather2(0)
         gather1(1)
-        occupancy(0, 0, by_bank=True)
+        occupancy(0, 0, banks_a_step=1)
         deal_w4()
         gather2(1)
         occupancy(0, 1)
-        cast_w(0)
-        cast_w(1)
-        quant_w(0)
-        quant_w(1)
+        quantise_w()
         for c in range(1, len(CHUNKS)):
             occupancy(c, 0)
-            pathways(c - 1)
             occupancy(c, 1)
+            pathways(c - 1)
         pathways(len(CHUNKS) - 1)
         for q in range(4):
             queue = nc.scalar if q % 2 else nc.sync

@@ -26,6 +26,8 @@ LINE = 4
 CHUNKS = (256, 256, 256, 128, 128)
 ROW1, ROW2 = 0, 8
 AHEAD = 5
+Y_ON_SCALAR = 0
+PAIR = 4
 
 
 def tile_list_motif_promoter_activity_kernel(
@@ -41,33 +43,31 @@ def tile_list_motif_promoter_activity_kernel(
         def held(shape, dtype, name, tag=""):
             return keep.tile(shape, dtype, name=name, tag=tag, align_bytes=64)
 
-        def interleave(dst, src):
-            nc.vector.tensor_copy(
+        def on_scalar(g):
+            return True
+
+        def interleave(copy, dst, src):
+            copy(
                 dst[:].rearrange("p (g i t) -> p g t i", i=LINE, t=PACK),
                 src[:].rearrange("p (t g i) -> p g t i", i=LINE, t=PACK),
             )
 
-        win1_s = held([P, T1], U8, "win1_s")
-        win2_s = held([P, T2], U8, "win2_s")
-        w4_s_raw = held([P, PASSES * N], U8, "w4_s_raw", tag="after_w4_s")
+        win1_s = held([P, T1], U8, "win1_s", tag="win1_s")
+        win2_s = held([P, T2], U8, "win2_s", tag="win2_s")
         one = held([P, 1], F32, "one")
         nc.vector.memset(win2_s[:].bitcast(I32), 0)
+        nc.vector.memset(win1_s[:].bitcast(I32), 0)
         nc.gpsimd.memset(one[:], 1.0)
-        nc.gpsimd.memset(win1_s[:].bitcast(I32), 0)
-        nc.gpsimd.memset(w4_s_raw[:].bitcast(I32), 0)
         unit = held([P, 1], F32, "unit")
         nc.scalar.activation(unit[:], one[:], ACT.Abs_reciprocal_sqrt)
 
         idx1 = keep.tile([P, S1 // 16], U16, name="idx1")
         idx2 = keep.tile([P, S2 // 16], U16, name="idx2")
-        win1 = [held([P, T1], U32, "win1_%d" % a) for a in range(PASSES)]
-        win2 = [held([P, T2], U32, "win2_%d" % a) for a in range(PASSES)]
+        win1 = [held([P, T1], U32, "win1_%d" % a, tag="win1_%d" % a) for a in range(PASSES)]
+        win2 = [held([P, T2], U32, "win2_%d" % a, tag="win2_%d" % a) for a in range(PASSES)]
 
-        def load_words(dst, src, pieces):
-            words = src.rearrange("p n t -> p (n t)").bitcast(I32)
-            step = words.shape[1] // pieces
-            for c0 in range(0, words.shape[1], step):
-                nc.sync.dma_start(dst[:, c0 : c0 + step].bitcast(I32), words[:, c0 : c0 + step])
+        def load_words(dst, src):
+            nc.sync.dma_start(dst[:].bitcast(I32), src.rearrange("p n t -> p (n t)").bitcast(I32))
 
         def load_scales(queue, win, src, row):
             for q in range(4):
@@ -76,128 +76,173 @@ def tile_list_motif_promoter_activity_kernel(
                     src[:, 4 * q : 4 * q + 4, :].bitcast(I32),
                 )
 
-        load_scales(nc.gpsimd, win2_s, tab2_scales, ROW2)
         nc.sync.dma_start(idx1[:], offs)
-        load_words(win1[0], tab_words[0], 2)
-        load_words(win1[1], tab_words[1], 2)
         nc.sync.dma_start(idx2[:], offs2)
         ab = held([P, PASSES * PACK], F32, "ab")
         nc.sync.dma_start(
             ab[:].rearrange("p (b t) -> p b t", b=PASSES), abund.rearrange("(b p t) -> p b t", b=PASSES, t=PACK)
         )
-        load_scales(nc.sync, win1_s, tab_scales, ROW1)
-        load_words(win2[0], tab2_words[0], 1)
-        load_words(win2[1], tab2_words[1], 1)
-        w4_raw = held([P, PASSES * 2 * N], U8, "w4_raw", tag="after_w4")
+        for a in range(PASSES):
+            load_words(win1[a], tab_words[a])
+        for a in range(PASSES):
+            load_words(win2[a], tab2_words[a])
+        load_scales(nc.scalar, win1_s, tab_scales, ROW1)
+        load_scales(nc.gpsimd, win2_s, tab2_scales, ROW2)
+
+        def deal(dst, src, run):
+            nc.vector.tensor_copy(
+                dst.rearrange("p (b t g i) -> p b g t i", b=PASSES, t=PACK, i=run),
+                src.rearrange("p (b g i t) -> p b g t i", b=PASSES, t=PACK, i=run),
+            )
+
+        picked = [held([P, S1], U32, "picked%d" % a, tag="picked%d" % a) for a in range(PASSES)]
+        v1 = [held([P, S1], U32, "v1_%d" % a) for a in range(PASSES)]
+        picked_s = held([P, S1], U8, "picked_s")
+        v1_s = held([P, S1], U8, "v1_s")
+        v2_s = held([P, S2], U8, "v2_s", tag="win1_s")
+        for a in range(PASSES):
+            nc.vector.tensor_copy(picked[a][:], win1[a][:].indirect(idx1[:]))
+        deal(v1[0][:], picked[0][:], 4)
+        nc.vector.tensor_copy(picked_s[:], win1_s[:].indirect(idx1[:]))
+        deal(v1[1][:], picked[1][:], 4)
+        nc.vector.tensor_copy(v2_s[:], win2_s[:].indirect(idx2[:]))
+        deal(v1_s[:], picked_s[:], 16)
+
+        w_raw = [held([P, PACK, N], F32, "w_raw%d" % b, tag="win1_%d" % b) for b in range(PASSES)]
+        for b in range(PASSES):
+            nc.sync.dma_start(w_raw[b][:], w[b * PASS : (b + 1) * PASS, :].rearrange("(p r) n -> p r n", r=PACK))
+        w4_raw = held([P, PASSES * 2 * N], U8, "w4_raw", tag="picked0")
         nc.sync.dma_start(
             w4_raw[:].bitcast(I32).rearrange("p (b n) -> p b n", b=PASSES),
             w4_words.bitcast(I32).rearrange("b p n -> p b n"),
         )
+        w4_s_raw = held([P, PASSES * N], U8, "w4_s_raw", tag="picked1")
+        nc.vector.memset(w4_s_raw[:].bitcast(I32), 0)
         for q in range(4):
             nc.sync.dma_start(
                 w4_s_raw[32 * q : 32 * q + 4, :].bitcast(I32).rearrange("r (b n) -> r b n", b=PASSES),
                 w4_scales[:, 4 * q : 4 * q + 4, :].bitcast(I32).rearrange("b r n -> r b n"),
             )
-        w_raw = [held([P, PACK, N], F32, "w_raw%d" % b) for b in range(PASSES)]
-        for b in range(PASSES):
-            nc.sync.dma_start(w_raw[b][:], w[b * PASS : (b + 1) * PASS, :].rearrange("(p r) n -> p r n", r=PACK))
-
-        v1, v1_s, v2, v2_s = {}, {}, {}, {}
 
         def entries(half):
             return slice(half * HALF // 16, (half + 1) * HALF // 16)
 
-        def gather1(half):
-            for a in range(PASSES):
-                tag = "after_deal" if (a, half) == (0, 1) else ""
-                v1[a, half] = held([P, HALF], U32, "v1_%d_%d" % (a, half), tag=tag)
-                nc.vector.tensor_copy(
-                    v1[a, half][:].rearrange("p (t m) -> p m t", t=PACK), win1[a][:].indirect(idx1[:, entries(half)])
-                )
-            picked = held([P, HALF], U8, "v1_s_picked%d" % half, tag="" if half else "after_deal")
-            nc.vector.tensor_copy(picked[:], win1_s[:].indirect(idx1[:, entries(half)]))
-            v1_s[half] = held([P, HALF], U8, "v1_s%d" % half)
-            nc.vector.tensor_copy(
-                v1_s[half][:].rearrange("p (t m) -> p t m", t=PACK), picked[:].rearrange("p (m t) -> p t m", t=PACK)
-            )
+        v2 = {}
+        first_half = held([P, PASSES * HALF], U32, "v2_first", tag="win2_s")
+        for a in range(PASSES):
+            v2[a, 0] = first_half[:, a * HALF : (a + 1) * HALF]
+            nc.vector.tensor_copy(v2[a, 0], win2[a][:].indirect(idx2[:, entries(0)]))
 
-        def gather2(half):
-            v2_s[half] = held([P, HALF], U8, "v2_s%d" % half, tag="after_w4_s" if half else "")
-            nc.vector.tensor_copy(v2_s[half][:], win2_s[:].indirect(idx2[:, entries(half)]))
-            for a in range(PASSES):
-                tag = "after_w4" if (a, half) == (0, 1) else ""
-                v2[a, half] = held([P, HALF], U32, "v2_%d_%d" % (a, half), tag=tag)
-                nc.vector.tensor_copy(v2[a, half][:], win2[a][:].indirect(idx2[:, entries(half)]))
+        def gather_second_half():
+            for a in reversed(range(PASSES)):
+                second = held([P, HALF], U32, "v2_%d" % a, tag="" if a else "win2_1")
+                v2[a, 1] = second[:]
+                nc.vector.tensor_copy(v2[a, 1], win2[a][:].indirect(idx2[:, entries(1)]))
 
-        w4 = held([P, PASSES * 2 * N], U8, "w4")
-        w4_s = held([P, PASSES * N], U8, "w4_s")
+        w4_tiles = []
 
         def deal_w4():
-            nc.vector.tensor_copy(
-                w4[:].bitcast(U16).rearrange("p (b t m) -> p b t m", b=PASSES, t=PACK),
-                w4_raw[:].bitcast(U16).rearrange("p (b m t) -> p b t m", b=PASSES, t=PACK),
-            )
-            nc.vector.tensor_copy(
-                w4_s[:].rearrange("p (b t m) -> p b t m", b=PASSES, t=PACK),
-                w4_s_raw[:].rearrange("p (b m t) -> p b t m", b=PASSES, t=PACK),
-            )
+            w4 = held([P, PASSES * 2 * N], U8, "w4", tag="win1_0")
+            w4_s = held([P, PASSES * N], U8, "w4_s", tag="win1_1")
+            deal(w4[:].bitcast(U16), w4_raw[:].bitcast(U16), 8)
+            deal(w4_s[:], w4_s_raw[:], 16)
+            w4_tiles.extend([w4, w4_s])
 
         wq = [held([P, N], U32, "wq%d" % b) for b in range(PASSES)]
         wq_s = [held([P, N], U8, "wq_s%d" % b) for b in range(PASSES)]
-        w_bf = [held([P, N * PACK], BF16, "w_bf%d" % b) for b in range(PASSES)]
+
+        w_bf = []
+
+        def cast_w():
+            both = held([P, PASSES * N * PACK], BF16, "w_bf", tag="win2_0")
+            w_bf.extend(both[:, b * N * PACK : (b + 1) * N * PACK] for b in range(PASSES))
+            for b in range(PASSES):
+                nc.vector.tensor_copy(
+                    w_bf[b].rearrange("p (t m r) -> p m t r", t=PACK, r=PACK),
+                    w_raw[b][:].rearrange("p r (m t) -> p m t r", t=PACK),
+                )
 
         def quantise_w():
             for b in range(PASSES):
-                nc.vector.tensor_copy(
-                    w_bf[b][:].rearrange("p (t m r) -> p m t r", t=PACK, r=PACK),
-                    w_raw[b][:].rearrange("p r (m t) -> p m t r", t=PACK),
-                )
-            for b in range(PASSES):
-                nc.vector.quantize_mx(out=wq[b][:].bitcast(FP8X4), scales=wq_s[b][:], in_=w_bf[b][:])
+                nc.vector.quantize_mx(out=wq[b][:].bitcast(FP8X4), scales=wq_s[b][:], in_=w_bf[b])
 
         starts = [sum(CHUNKS[:c]) for c in range(len(CHUNKS))]
-        hq, hq_s = {}, {}
+        groups = PASSES * len(CHUNKS)
+        sq, rs, inv, hb, hi, hq, hq_s, y, yi = {}, {}, {}, {}, {}, {}, {}, {}, {}
 
-        def occupancy(c, b, banks_a_step=2):
+        def width(g):
+            return CHUNKS[g // PASSES]
+
+        def banks(jc):
+            return PACK * jc // BANK
+
+        def square(g, u):
+            c, b = divmod(g, PASSES)
             jc = CHUNKS[c]
+            if u >= banks(jc):
+                return
             per_bank = BANK // jc
             half, j0 = divmod(starts[c], HALF)
-            sq = work.tile([P, PACK * jc], F32, name="sq", bufs=AHEAD)
-            rs = work.tile([P, PACK * jc], F32, name="rs")
-            inv = work.tile([P, PACK * jc], F32, name="inv", bufs=AHEAD)
-            for u in range(PACK // per_bank):
-                aff = psum.tile([P, BANK], F32, name="aff", bufs=4)
-                for a in range(PASSES):
-                    for e in range(per_bank):
-                        m = slice((per_bank * u + e) * P, (per_bank * u + e + 1) * P)
-                        nc.tensor.matmul_mx(
-                            out=aff[:, e * jc : (e + 1) * jc],
-                            lhsT=v1[a, b][:, m].bitcast(FP8X4),
-                            lhsT_scale=v1_s[b][ROW1 + 4 * a :, m],
-                            rhs=v2[a, half][:, j0 : j0 + jc].bitcast(FP8X4),
-                            rhs_scale=v2_s[half][ROW2 + 4 * a :, j0 : j0 + jc],
-                            start=(a == 0 and e == 0),
-                            stop=(a == PASSES - 1 and e == per_bank - 1),
-                        )
-                nc.scalar.activation(sq[:, u * BANK : (u + 1) * BANK], aff[:], ACT.Square)
-            step = min(banks_a_step * BANK, PACK * jc)
-            for s0 in range(0, PACK * jc, step):
-                nc.scalar.activation(
-                    rs[:, s0 : s0 + step], sq[:, s0 : s0 + step], ACT.Abs_reciprocal_sqrt, bias=unit[:]
-                )
-            for s0 in range(0, PACK * jc, step):
-                nc.scalar.activation(inv[:, s0 : s0 + step], rs[:, s0 : s0 + step], ACT.Square)
-            hb = work.tile([P, PACK * jc], BF16, name="hb", bufs=AHEAD - 1)
+            if u == 0:
+                sq[g] = work.tile([P, PACK * jc], F32, name="sq", bufs=AHEAD)
+            aff = psum.tile([P, BANK], F32, name="aff", bufs=4)
+            for a in range(PASSES):
+                for e in range(per_bank):
+                    m0 = b * PASS + (per_bank * u + e) * P
+                    nc.tensor.matmul_mx(
+                        out=aff[:, e * jc : (e + 1) * jc],
+                        lhsT=v1[a][:, m0 : m0 + P].bitcast(FP8X4),
+                        lhsT_scale=v1_s[ROW1 + 4 * a :, m0 : m0 + P],
+                        rhs=v2[a, half][:, j0 : j0 + jc].bitcast(FP8X4),
+                        rhs_scale=v2_s[ROW2 + 4 * a :, starts[c] : starts[c] + jc],
+                        start=(a == 0 and e == 0),
+                        stop=(a == PASSES - 1 and e == per_bank - 1),
+                    )
+            nc.scalar.activation(sq[g][:, u * BANK : (u + 1) * BANK], aff[:], ACT.Square)
+
+        def pieces(g):
+            step = BANK if g == 0 else PACK * width(g)
+            return [slice(s0, s0 + step) for s0 in range(0, PACK * width(g), step)]
+
+        def root(g):
+            rs[g] = work.tile([P, PACK * width(g)], F32, name="rs", bufs=AHEAD - 1)
+            for cols in pieces(g):
+                nc.scalar.activation(rs[g][:, cols], sq[g][:, cols], ACT.Abs_reciprocal_sqrt, bias=unit[:])
+
+        def inverse(g):
+            inv[g] = work.tile([P, PACK * width(g)], F32, name="inv", bufs=AHEAD)
+            if on_scalar(g):
+                for cols in pieces(g):
+                    nc.scalar.activation(inv[g][:, cols], rs[g][:, cols], ACT.Square)
+
+        def weigh(g):
+            jc, b = width(g), g % PASSES
+            if on_scalar(g):
+                hb[g] = work.tile([P, PACK * jc], BF16, name="hb", bufs=3)
             for t in range(PACK):
                 cols = slice(t * jc, (t + 1) * jc)
-                nc.vector.scalar_tensor_tensor(
-                    hb[:, cols], sq[:, cols], ab[:, PACK * b + t : PACK * b + t + 1], inv[:, cols], ALU.mult, ALU.mult
+                scalar = ab[:, PACK * b + t : PACK * b + t + 1]
+                if on_scalar(g):
+                    nc.vector.scalar_tensor_tensor(hb[g][:, cols], sq[g][:, cols], scalar, inv[g][:, cols], ALU.mult, ALU.mult)
+                else:
+                    nc.vector.scalar_tensor_tensor(inv[g][:, cols], sq[g][:, cols], scalar, rs[g][:, cols], ALU.mult, ALU.mult)
+
+        def weave(g):
+            hi[g] = work.tile([P, PACK * width(g)], BF16, name="hi", bufs=3, align_bytes=64)
+            if on_scalar(g):
+                interleave(nc.vector.tensor_copy, hi[g], hb[g])
+            else:
+                nc.vector.tensor_tensor(
+                    hi[g][:].rearrange("p (g i t) -> p g t i", i=PAIR, t=PACK),
+                    inv[g][:].rearrange("p (t g i) -> p g t i", i=PAIR, t=PACK),
+                    rs[g][:].rearrange("p (t g i) -> p g t i", i=PAIR, t=PACK),
+                    ALU.mult,
                 )
-            hi = work.tile([P, PACK * jc], BF16, name="hi", bufs=AHEAD - 1, align_bytes=64)
-            interleave(hi, hb)
-            hq[c, b] = work.tile([P, jc], U32, name="hq", bufs=AHEAD + 1, align_bytes=64)
-            hq_s[c, b] = work.tile([P, jc], U8, name="hq_s", bufs=AHEAD + 1, align_bytes=64)
-            nc.vector.quantize_mx(out=hq[c, b][:].bitcast(FP8X4), scales=hq_s[c, b][:], in_=hi[:])
+
+        def quantise_h(g):
+            hq[g] = work.tile([P, width(g)], U32, name="hq", bufs=AHEAD + 1, align_bytes=64)
+            hq_s[g] = work.tile([P, width(g)], U8, name="hq_s", bufs=AHEAD + 1, align_bytes=64)
+            nc.vector.quantize_mx(out=hq[g][:].bitcast(FP8X4), scales=hq_s[g][:], in_=hi[g][:])
 
         y_s = held([P, S2], U8, "y_s")
         out_rows = out_0.rearrange("(p t) j -> p t j", t=PACK)
@@ -206,8 +251,9 @@ def tile_list_motif_promoter_activity_kernel(
         def pathways(c):
             jc = CHUNKS[c]
             per_bank = BANK // jc
-            y = work.tile([P, PACK * jc], F32, name="y")
-            for u in range(PACK // per_bank):
+            w4, w4_s = w4_tiles
+            y[c] = work.tile([P, PACK * jc], F32, name="y")
+            for u in range(banks(jc)):
                 p1 = psum.tile([P, BANK], F32, name="p1")
                 p2 = psum.tile([P, BANK], F32, name="p2")
                 for b in range(PASSES):
@@ -217,48 +263,72 @@ def tile_list_motif_promoter_activity_kernel(
                             out=p1[:, e * jc : (e + 1) * jc],
                             lhsT=wq[b][:, m].bitcast(FP8X4),
                             lhsT_scale=wq_s[b][:, m],
-                            rhs=hq[c, b][:].bitcast(FP8X4),
-                            rhs_scale=hq_s[c, b][:],
+                            rhs=hq[PASSES * c + b][:].bitcast(FP8X4),
+                            rhs_scale=hq_s[PASSES * c + b][:],
                             start=(b == 0 and e == 0),
                             stop=(b == PASSES - 1 and e == per_bank - 1),
                         )
+                run = BANK if jc == BANK else P
                 for b in range(PASSES):
                     for e in range(per_bank):
                         m0 = b * N + (per_bank * u + e) * P
-                        for j0 in range(0, jc, P):
+                        for j0 in range(0, jc, run):
                             nc.tensor.matmul_mx(
-                                out=p2[:, e * jc + j0 : e * jc + j0 + P],
+                                out=p2[:, e * jc + j0 : e * jc + j0 + run],
                                 lhsT=w4[:, 2 * m0 : 2 * (m0 + P)].bitcast(FP4X4),
                                 lhsT_scale=w4_s[:, m0 : m0 + P],
-                                rhs=hq[c, b][:, j0 : j0 + P].bitcast(FP8X4),
-                                rhs_scale=hq_s[c, b][:, j0 : j0 + P],
+                                rhs=hq[PASSES * c + b][:, j0 : j0 + run].bitcast(FP8X4),
+                                rhs_scale=hq_s[PASSES * c + b][:, j0 : j0 + run],
                                 start=(b == 0 and e == 0 and j0 == 0),
-                                stop=(b == PASSES - 1 and e == per_bank - 1 and j0 == jc - P),
+                                stop=(b == PASSES - 1 and e == per_bank - 1 and j0 == jc - run),
                             )
                 first = work.tile([P, BANK], F32, name="first", bufs=AHEAD - 1)
                 nc.scalar.copy(first[:], p1[:])
-                nc.vector.tensor_tensor(y[:, u * BANK : (u + 1) * BANK], p2[:], first[:], ALU.mult)
+                nc.vector.tensor_tensor(y[c][:, u * BANK : (u + 1) * BANK], p2[:], first[:], ALU.mult)
             genes = slice(starts[c], starts[c] + jc)
-            nc.sync.dma_start(out_rows[:, :, genes], y[:].rearrange("p (t j) -> p t j", t=PACK))
-            yi = work.tile([P, PACK * jc], BF16, name="yi", bufs=2, align_bytes=64)
-            interleave(yi, y)
-            yq = work.tile([P, jc], U32, name="yq", bufs=2, align_bytes=64)
-            nc.vector.quantize_mx(out=yq[:].bitcast(FP8X4), scales=y_s[:, genes], in_=yi[:])
+            nc.sync.dma_start(out_rows[:, :, genes], y[c][:].rearrange("p (t j) -> p t j", t=PACK))
+
+        def weave_y(c):
+            yi[c] = work.tile([P, PACK * CHUNKS[c]], BF16, name="yi", bufs=2, align_bytes=64)
+            interleave(nc.scalar.copy if c < Y_ON_SCALAR else nc.vector.tensor_copy, yi[c], y[c])
+
+        def quantise_y(c):
+            genes = slice(starts[c], starts[c] + CHUNKS[c])
+            yq = work.tile([P, CHUNKS[c]], U32, name="yq", bufs=2, align_bytes=64)
+            nc.vector.quantize_mx(out=yq[:].bitcast(FP8X4), scales=y_s[:, genes], in_=yi[c][:])
             nc.sync.dma_start(out_words[:, genes], yq[:].bitcast(I32))
 
-        gather1(0)
-        gather2(0)
-        gather1(1)
-        occupancy(0, 0, banks_a_step=1)
-        deal_w4()
-        gather2(1)
-        occupancy(0, 1)
-        quantise_w()
-        for c in range(1, len(CHUNKS)):
-            occupancy(c, 0)
-            occupancy(c, 1)
-            pathways(c - 1)
-        pathways(len(CHUNKS) - 1)
+        for u in range(PACK):
+            square(0, u)
+        for step in range(groups + 4):
+            if step + 1 < groups:
+                square(step + 1, 0)
+            if step < groups:
+                root(step)
+            if step + 1 < groups:
+                for u in range(1, PACK):
+                    square(step + 1, u)
+            if step < groups:
+                inverse(step)
+                weigh(step)
+            woven = (step - 4) // PASSES if step >= 4 and step % PASSES == 0 else None
+            if woven is not None:
+                weave_y(woven)
+            if 1 <= step <= groups:
+                quantise_h(step - 1)
+            if step < groups:
+                weave(step)
+            if woven is not None:
+                quantise_y(woven)
+            if step == 0:
+                gather_second_half()
+            if step == 1:
+                cast_w()
+            if step == 2:
+                deal_w4()
+                quantise_w()
+            if step >= 3 and step % PASSES == 1 and (step - 3) // PASSES < len(CHUNKS):
+                pathways((step - 3) // PASSES)
         for q in range(4):
             queue = nc.scalar if q % 2 else nc.sync
             queue.dma_start(out_2[0, 4 * q : 4 * q + 4, :].bitcast(I32), y_s[32 * q : 32 * q + 4, :].bitcast(I32))

@@ -56,8 +56,8 @@ def tile_list_motif_promoter_activity_kernel(
         win2_s = held([P, T2], U8, "win2_s", tag="win2_s")
         one = held([P, 1], F32, "one")
         nc.vector.memset(win2_s[:].bitcast(I32), 0)
-        nc.vector.memset(win1_s[:].bitcast(I32), 0)
         nc.gpsimd.memset(one[:], 1.0)
+        nc.gpsimd.memset(win1_s[:].bitcast(I32), 0)
         unit = held([P, 1], F32, "unit")
         nc.scalar.activation(unit[:], one[:], ACT.Abs_reciprocal_sqrt)
 
@@ -66,8 +66,11 @@ def tile_list_motif_promoter_activity_kernel(
         win1 = [held([P, T1], U32, "win1_%d" % a, tag="win1_%d" % a) for a in range(PASSES)]
         win2 = [held([P, T2], U32, "win2_%d" % a, tag="win2_%d" % a) for a in range(PASSES)]
 
-        def load_words(dst, src):
-            nc.sync.dma_start(dst[:].bitcast(I32), src.rearrange("p n t -> p (n t)").bitcast(I32))
+        def load_words(dst, src, pieces):
+            words = src.rearrange("p n t -> p (n t)").bitcast(I32)
+            step = words.shape[1] // pieces
+            for c0 in range(0, words.shape[1], step):
+                nc.sync.dma_start(dst[:, c0 : c0 + step].bitcast(I32), words[:, c0 : c0 + step])
 
         def load_scales(queue, win, src, row):
             for q in range(4):
@@ -76,18 +79,18 @@ def tile_list_motif_promoter_activity_kernel(
                     src[:, 4 * q : 4 * q + 4, :].bitcast(I32),
                 )
 
+        load_scales(nc.gpsimd, win2_s, tab2_scales, ROW2)
         nc.sync.dma_start(idx1[:], offs)
+        for a in range(PASSES):
+            load_words(win1[a], tab_words[a], 2)
         nc.sync.dma_start(idx2[:], offs2)
         ab = held([P, PASSES * PACK], F32, "ab")
         nc.sync.dma_start(
             ab[:].rearrange("p (b t) -> p b t", b=PASSES), abund.rearrange("(b p t) -> p b t", b=PASSES, t=PACK)
         )
+        load_scales(nc.sync, win1_s, tab_scales, ROW1)
         for a in range(PASSES):
-            load_words(win1[a], tab_words[a])
-        for a in range(PASSES):
-            load_words(win2[a], tab2_words[a])
-        load_scales(nc.scalar, win1_s, tab_scales, ROW1)
-        load_scales(nc.gpsimd, win2_s, tab2_scales, ROW2)
+            load_words(win2[a], tab2_words[a], 1)
 
         def deal(dst, src, run):
             nc.vector.tensor_copy(

@@ -26,7 +26,9 @@ LINE = 4
 CHUNKS = (256, 256, 256, 128, 128)
 ROW1, ROW2 = 0, 8
 AHEAD = 5
-Y_ON_SCALAR = 0
+COPY_LAG = 4
+AFF_BANKS = 4
+Y_ON_SCALAR = ()
 PAIR = 4
 
 
@@ -44,7 +46,7 @@ def tile_list_motif_promoter_activity_kernel(
             return keep.tile(shape, dtype, name=name, tag=tag, align_bytes=64)
 
         def on_scalar(g):
-            return True
+            return g >= 2
 
         def interleave(copy, dst, src):
             copy(
@@ -127,20 +129,13 @@ def tile_list_motif_promoter_activity_kernel(
                 w4_scales[:, 4 * q : 4 * q + 4, :].bitcast(I32).rearrange("b r n -> r b n"),
             )
 
-        def entries(half):
-            return slice(half * HALF // 16, (half + 1) * HALF // 16)
-
-        v2 = {}
-        first_half = held([P, PASSES * HALF], U32, "v2_first", tag="win2_s")
-        for a in range(PASSES):
-            v2[a, 0] = first_half[:, a * HALF : (a + 1) * HALF]
-            nc.vector.tensor_copy(v2[a, 0], win2[a][:].indirect(idx2[:, entries(0)]))
-
-        def gather_second_half():
-            for a in reversed(range(PASSES)):
-                second = held([P, HALF], U32, "v2_%d" % a, tag="" if a else "win2_1")
-                v2[a, 1] = second[:]
-                nc.vector.tensor_copy(v2[a, 1], win2[a][:].indirect(idx2[:, entries(1)]))
+        v2 = [
+            held([P, S2], U32, "v2_0", tag="win2_s"),
+            held([P, S2], U32, "v2_1", tag="win2_0"),
+        ]
+        nc.vector.tensor_copy(v2[0][:], win2[0][:].indirect(idx2[:]))
+        for e0 in range(0, S2, HALF):
+            nc.vector.tensor_copy(v2[1][:, e0 : e0 + HALF], win2[1][:].indirect(idx2[:, e0 // 16 : (e0 + HALF) // 16]))
 
         w4_tiles = []
 
@@ -157,7 +152,7 @@ def tile_list_motif_promoter_activity_kernel(
         w_bf = []
 
         def cast_w():
-            both = held([P, PASSES * N * PACK], BF16, "w_bf", tag="win2_0")
+            both = held([P, PASSES * N * PACK], BF16, "w_bf", tag="win2_1")
             w_bf.extend(both[:, b * N * PACK : (b + 1) * N * PACK] for b in range(PASSES))
             for b in range(PASSES):
                 nc.vector.tensor_copy(
@@ -179,36 +174,42 @@ def tile_list_motif_promoter_activity_kernel(
         def banks(jc):
             return PACK * jc // BANK
 
-        def square(g, u):
+        aff = {}
+
+        def affinity(g, u, a):
             c, b = divmod(g, PASSES)
             jc = CHUNKS[c]
-            if u >= banks(jc):
-                return
             per_bank = BANK // jc
-            half, j0 = divmod(starts[c], HALF)
+            if a == 0:
+                aff[g, u] = psum.tile([P, BANK], F32, name="aff", bufs=AFF_BANKS)
+            for e in range(per_bank):
+                m0 = b * PASS + (per_bank * u + e) * P
+                nc.tensor.matmul_mx(
+                    out=aff[g, u][:, e * jc : (e + 1) * jc],
+                    lhsT=v1[a][:, m0 : m0 + P].bitcast(FP8X4),
+                    lhsT_scale=v1_s[ROW1 + 4 * a :, m0 : m0 + P],
+                    rhs=v2[a][:, starts[c] : starts[c] + jc].bitcast(FP8X4),
+                    rhs_scale=v2_s[ROW2 + 4 * a :, starts[c] : starts[c] + jc],
+                    start=(a == 0 and e == 0),
+                    stop=(a == PASSES - 1 and e == per_bank - 1),
+                )
+
+        def square(g, u):
+            if u >= banks(width(g)):
+                return
             if u == 0:
-                sq[g] = work.tile([P, PACK * jc], F32, name="sq", bufs=AHEAD)
-            aff = psum.tile([P, BANK], F32, name="aff", bufs=4)
-            for a in range(PASSES):
-                for e in range(per_bank):
-                    m0 = b * PASS + (per_bank * u + e) * P
-                    nc.tensor.matmul_mx(
-                        out=aff[:, e * jc : (e + 1) * jc],
-                        lhsT=v1[a][:, m0 : m0 + P].bitcast(FP8X4),
-                        lhsT_scale=v1_s[ROW1 + 4 * a :, m0 : m0 + P],
-                        rhs=v2[a, half][:, j0 : j0 + jc].bitcast(FP8X4),
-                        rhs_scale=v2_s[ROW2 + 4 * a :, starts[c] : starts[c] + jc],
-                        start=(a == 0 and e == 0),
-                        stop=(a == PASSES - 1 and e == per_bank - 1),
-                    )
-            nc.scalar.activation(sq[g][:, u * BANK : (u + 1) * BANK], aff[:], ACT.Square)
+                sq[g] = work.tile([P, PACK * width(g)], F32, name="sq", bufs=AHEAD)
+            if (g, u) not in aff:
+                affinity(g, u, 0)
+            affinity(g, u, 1)
+            nc.scalar.activation(sq[g][:, u * BANK : (u + 1) * BANK], aff[g, u][:], ACT.Square)
 
         def pieces(g):
             step = BANK if g == 0 else PACK * width(g)
             return [slice(s0, s0 + step) for s0 in range(0, PACK * width(g), step)]
 
         def root(g):
-            rs[g] = work.tile([P, PACK * width(g)], F32, name="rs", bufs=AHEAD - 1)
+            rs[g] = held([P, PACK * width(g)], F32, "rs_%d" % g, tag="rs_%d" % g)
             for cols in pieces(g):
                 nc.scalar.activation(rs[g][:, cols], sq[g][:, cols], ACT.Abs_reciprocal_sqrt, bias=unit[:])
 
@@ -256,6 +257,8 @@ def tile_list_motif_promoter_activity_kernel(
             per_bank = BANK // jc
             w4, w4_s = w4_tiles
             y[c] = work.tile([P, PACK * jc], F32, name="y")
+            behind = PASSES * c + COPY_LAG
+            first = held([P, PACK * jc], F32, "first_%d" % c, tag="rs_%d" % behind if behind < groups else "")
             for u in range(banks(jc)):
                 p1 = psum.tile([P, BANK], F32, name="p1")
                 p2 = psum.tile([P, BANK], F32, name="p2")
@@ -271,29 +274,27 @@ def tile_list_motif_promoter_activity_kernel(
                             start=(b == 0 and e == 0),
                             stop=(b == PASSES - 1 and e == per_bank - 1),
                         )
-                run = BANK if jc == BANK else P
-                for b in range(PASSES):
                     for e in range(per_bank):
                         m0 = b * N + (per_bank * u + e) * P
-                        for j0 in range(0, jc, run):
+                        for j0 in range(0, jc, P):
                             nc.tensor.matmul_mx(
-                                out=p2[:, e * jc + j0 : e * jc + j0 + run],
+                                out=p2[:, e * jc + j0 : e * jc + j0 + P],
                                 lhsT=w4[:, 2 * m0 : 2 * (m0 + P)].bitcast(FP4X4),
                                 lhsT_scale=w4_s[:, m0 : m0 + P],
-                                rhs=hq[PASSES * c + b][:, j0 : j0 + run].bitcast(FP8X4),
-                                rhs_scale=hq_s[PASSES * c + b][:, j0 : j0 + run],
+                                rhs=hq[PASSES * c + b][:, j0 : j0 + P].bitcast(FP8X4),
+                                rhs_scale=hq_s[PASSES * c + b][:, j0 : j0 + P],
                                 start=(b == 0 and e == 0 and j0 == 0),
-                                stop=(b == PASSES - 1 and e == per_bank - 1 and j0 == jc - run),
+                                stop=(b == PASSES - 1 and e == per_bank - 1 and j0 == jc - P),
                             )
-                first = work.tile([P, BANK], F32, name="first", bufs=AHEAD - 1)
-                nc.scalar.copy(first[:], p1[:])
-                nc.vector.tensor_tensor(y[c][:, u * BANK : (u + 1) * BANK], p2[:], first[:], ALU.mult)
+                cols = slice(u * BANK, (u + 1) * BANK)
+                nc.scalar.copy(first[:, cols], p1[:])
+                nc.vector.tensor_tensor(y[c][:, cols], p2[:], first[:, cols], ALU.mult)
             genes = slice(starts[c], starts[c] + jc)
             nc.sync.dma_start(out_rows[:, :, genes], y[c][:].rearrange("p (t j) -> p t j", t=PACK))
 
         def weave_y(c):
             yi[c] = work.tile([P, PACK * CHUNKS[c]], BF16, name="yi", bufs=2, align_bytes=64)
-            interleave(nc.scalar.copy if c < Y_ON_SCALAR else nc.vector.tensor_copy, yi[c], y[c])
+            interleave(nc.scalar.copy if c in Y_ON_SCALAR else nc.vector.tensor_copy, yi[c], y[c])
 
         def quantise_y(c):
             genes = slice(starts[c], starts[c] + CHUNKS[c])
@@ -301,37 +302,38 @@ def tile_list_motif_promoter_activity_kernel(
             nc.vector.quantize_mx(out=yq[:].bitcast(FP8X4), scales=y_s[:, genes], in_=yi[c][:])
             nc.sync.dma_start(out_words[:, genes], yq[:].bitcast(I32))
 
+        def finish(c):
+            pathways(c)
+            weave_y(c)
+            quantise_y(c)
+
+        for bank in range(AFF_BANKS):
+            affinity(*divmod(bank, banks(CHUNKS[0])), 0)
         for u in range(PACK):
             square(0, u)
-        for step in range(groups + 4):
+        for step in range(groups):
             if step + 1 < groups:
                 square(step + 1, 0)
-            if step < groups:
-                root(step)
+            root(step)
             if step + 1 < groups:
                 for u in range(1, PACK):
                     square(step + 1, u)
-            if step < groups:
-                inverse(step)
-                weigh(step)
-            woven = (step - 4) // PASSES if step >= 4 and step % PASSES == 0 else None
-            if woven is not None:
-                weave_y(woven)
-            if 1 <= step <= groups:
+            inverse(step)
+            weigh(step)
+            if step >= 1:
                 quantise_h(step - 1)
-            if step < groups:
-                weave(step)
-            if woven is not None:
-                quantise_y(woven)
-            if step == 0:
-                gather_second_half()
+            weave(step)
             if step == 1:
                 cast_w()
             if step == 2:
                 deal_w4()
                 quantise_w()
-            if step >= 3 and step % PASSES == 1 and (step - 3) // PASSES < len(CHUNKS):
-                pathways((step - 3) // PASSES)
+            if step >= COPY_LAG and (step - COPY_LAG) % PASSES == 0:
+                finish((step - COPY_LAG) // PASSES)
+        quantise_h(groups - 1)
+        for c in range(len(CHUNKS)):
+            if c not in y:
+                finish(c)
         for q in range(4):
             queue = nc.scalar if q % 2 else nc.sync
             queue.dma_start(out_2[0, 4 * q : 4 * q + 4, :].bitcast(I32), y_s[32 * q : 32 * q + 4, :].bitcast(I32))

@@ -23,13 +23,15 @@ PASSES = 2
 HALF = 512
 BANK = 512
 LINE = 4
+PAIR = 2
+LINE_BYTES = 16
 CHUNKS = (256, 256, 256, 128, 128)
 ROW1, ROW2 = 0, 8
 AHEAD = 5
-COPY_LAG = 4
 AFF_BANKS = 4
-Y_ON_SCALAR = ()
-PAIR = 4
+SQUARED_FROM = 3
+COPY_LAG = 3
+WOVEN_ON_SCALAR = (2, 3)
 
 
 def tile_list_motif_promoter_activity_kernel(
@@ -45,14 +47,11 @@ def tile_list_motif_promoter_activity_kernel(
         def held(shape, dtype, name, tag=""):
             return keep.tile(shape, dtype, name=name, tag=tag, align_bytes=64)
 
-        def on_scalar(g):
-            return g >= 2
+        def woven(dst, run):
+            return dst[:].rearrange("p (x i t) -> p x t i", i=run, t=PACK)
 
-        def interleave(copy, dst, src):
-            copy(
-                dst[:].rearrange("p (g i t) -> p g t i", i=LINE, t=PACK),
-                src[:].rearrange("p (t g i) -> p g t i", i=LINE, t=PACK),
-            )
+        def sliced(src, run):
+            return src[:].rearrange("p (t x i) -> p x t i", i=run, t=PACK)
 
         win1_s = held([P, T1], U8, "win1_s", tag="win1_s")
         win2_s = held([P, T2], U8, "win2_s", tag="win2_s")
@@ -94,10 +93,11 @@ def tile_list_motif_promoter_activity_kernel(
         for a in range(PASSES):
             load_words(win2[a], tab2_words[a], 1)
 
-        def deal(dst, src, run):
+        def deal(dst, src, column_bytes):
+            per_line = LINE_BYTES // column_bytes
             nc.vector.tensor_copy(
-                dst.rearrange("p (b t g i) -> p b g t i", b=PASSES, t=PACK, i=run),
-                src.rearrange("p (b g i t) -> p b g t i", b=PASSES, t=PACK, i=run),
+                dst.rearrange("p (b t x i) -> p b x t i", b=PASSES, t=PACK, i=per_line),
+                src.rearrange("p (b x i t) -> p b x t i", b=PASSES, t=PACK, i=per_line),
             )
 
         picked = [held([P, S1], U32, "picked%d" % a, tag="picked%d" % a) for a in range(PASSES)]
@@ -111,7 +111,7 @@ def tile_list_motif_promoter_activity_kernel(
         nc.vector.tensor_copy(picked_s[:], win1_s[:].indirect(idx1[:]))
         deal(v1[1][:], picked[1][:], 4)
         nc.vector.tensor_copy(v2_s[:], win2_s[:].indirect(idx2[:]))
-        deal(v1_s[:], picked_s[:], 16)
+        deal(v1_s[:], picked_s[:], 1)
 
         w_raw = [held([P, PACK, N], F32, "w_raw%d" % b, tag="win1_%d" % b) for b in range(PASSES)]
         for b in range(PASSES):
@@ -129,52 +129,43 @@ def tile_list_motif_promoter_activity_kernel(
                 w4_scales[:, 4 * q : 4 * q + 4, :].bitcast(I32).rearrange("b r n -> r b n"),
             )
 
-        v2 = [
-            held([P, S2], U32, "v2_0", tag="win2_s"),
-            held([P, S2], U32, "v2_1", tag="win2_0"),
-        ]
+        v2 = [held([P, S2], U32, "v2_0", tag="win2_s"), held([P, S2], U32, "v2_1", tag="win2_0")]
         nc.vector.tensor_copy(v2[0][:], win2[0][:].indirect(idx2[:]))
         for e0 in range(0, S2, HALF):
             nc.vector.tensor_copy(v2[1][:, e0 : e0 + HALF], win2[1][:].indirect(idx2[:, e0 // 16 : (e0 + HALF) // 16]))
 
-        w4_tiles = []
+        wq = [held([P, N], U32, "wq%d" % b) for b in range(PASSES)]
+        wq_s = [held([P, N], U8, "wq_s%d" % b) for b in range(PASSES)]
+
+        def cast_w():
+            w_bf = held([P, PASSES, N * PACK], BF16, "w_bf", tag="win2_1")
+            for b in range(PASSES):
+                nc.vector.tensor_copy(
+                    w_bf[:, b, :].rearrange("p (t m r) -> p m r t", t=PACK, r=PACK),
+                    w_raw[b][:].rearrange("p r (m t) -> p m r t", t=PACK),
+                )
+            return w_bf
 
         def deal_w4():
             w4 = held([P, PASSES * 2 * N], U8, "w4", tag="win1_0")
             w4_s = held([P, PASSES * N], U8, "w4_s", tag="win1_1")
-            deal(w4[:].bitcast(U16), w4_raw[:].bitcast(U16), 8)
-            deal(w4_s[:], w4_s_raw[:], 16)
-            w4_tiles.extend([w4, w4_s])
+            deal(w4[:].bitcast(U16), w4_raw[:].bitcast(U16), 2)
+            deal(w4_s[:], w4_s_raw[:], 1)
+            return w4, w4_s
 
-        wq = [held([P, N], U32, "wq%d" % b) for b in range(PASSES)]
-        wq_s = [held([P, N], U8, "wq_s%d" % b) for b in range(PASSES)]
-
-        w_bf = []
-
-        def cast_w():
-            both = held([P, PASSES * N * PACK], BF16, "w_bf", tag="win2_1")
-            w_bf.extend(both[:, b * N * PACK : (b + 1) * N * PACK] for b in range(PASSES))
+        def quantise_w(w_bf):
             for b in range(PASSES):
-                nc.vector.tensor_copy(
-                    w_bf[b].rearrange("p (t m r) -> p m t r", t=PACK, r=PACK),
-                    w_raw[b][:].rearrange("p r (m t) -> p m t r", t=PACK),
-                )
-
-        def quantise_w():
-            for b in range(PASSES):
-                nc.vector.quantize_mx(out=wq[b][:].bitcast(FP8X4), scales=wq_s[b][:], in_=w_bf[b])
+                nc.vector.quantize_mx(out=wq[b][:].bitcast(FP8X4), scales=wq_s[b][:], in_=w_bf[:, b, :])
 
         starts = [sum(CHUNKS[:c]) for c in range(len(CHUNKS))]
         groups = PASSES * len(CHUNKS)
-        sq, rs, inv, hb, hi, hq, hq_s, y, yi = {}, {}, {}, {}, {}, {}, {}, {}, {}
+        aff, sq, rs, partial, hb, hi, hq, hq_s = {}, {}, {}, {}, {}, {}, {}, {}
 
         def width(g):
             return CHUNKS[g // PASSES]
 
         def banks(jc):
             return PACK * jc // BANK
-
-        aff = {}
 
         def affinity(g, u, a):
             c, b = divmod(g, PASSES)
@@ -195,56 +186,48 @@ def tile_list_motif_promoter_activity_kernel(
                 )
 
         def square(g, u):
-            if u >= banks(width(g)):
-                return
-            if u == 0:
-                sq[g] = work.tile([P, PACK * width(g)], F32, name="sq", bufs=AHEAD)
             if (g, u) not in aff:
                 affinity(g, u, 0)
             affinity(g, u, 1)
-            nc.scalar.activation(sq[g][:, u * BANK : (u + 1) * BANK], aff[g, u][:], ACT.Square)
-
-        def pieces(g):
-            step = BANK if g == 0 else PACK * width(g)
-            return [slice(s0, s0 + step) for s0 in range(0, PACK * width(g), step)]
+            if u + 1 < banks(width(g)):
+                sq[g, u] = held([P, BANK], F32, "sq_%d" % g, tag="sq_%d" % g)
+            else:
+                sq[g, u] = work.tile([P, BANK], F32, name="sq", bufs=AHEAD)
+            nc.scalar.activation(sq[g, u][:], aff[g, u][:], ACT.Square)
 
         def root(g):
             rs[g] = held([P, PACK * width(g)], F32, "rs_%d" % g, tag="rs_%d" % g)
-            for cols in pieces(g):
-                nc.scalar.activation(rs[g][:, cols], sq[g][:, cols], ACT.Abs_reciprocal_sqrt, bias=unit[:])
-
-        def inverse(g):
-            inv[g] = work.tile([P, PACK * width(g)], F32, name="inv", bufs=AHEAD)
-            if on_scalar(g):
-                for cols in pieces(g):
-                    nc.scalar.activation(inv[g][:, cols], rs[g][:, cols], ACT.Square)
+            for u in range(banks(width(g))):
+                nc.scalar.activation(
+                    rs[g][:, u * BANK : (u + 1) * BANK], sq[g, u][:], ACT.Abs_reciprocal_sqrt, bias=unit[:]
+                )
 
         def weigh(g):
             jc, b = width(g), g % PASSES
-            if on_scalar(g):
-                hb[g] = work.tile([P, PACK * jc], BF16, name="hb", bufs=3)
+            partial[g] = work.tile([P, PACK * jc], F32, name="partial", bufs=AHEAD)
+            if g >= SQUARED_FROM:
+                nc.scalar.activation(partial[g][:], rs[g][:], ACT.Square)
+                hb[g] = work.tile([P, PACK * jc], BF16, name="hb")
+                dst, factor = hb[g], partial[g]
+            else:
+                dst, factor = partial[g], rs[g]
             for t in range(PACK):
                 cols = slice(t * jc, (t + 1) * jc)
-                scalar = ab[:, PACK * b + t : PACK * b + t + 1]
-                if on_scalar(g):
-                    nc.vector.scalar_tensor_tensor(hb[g][:, cols], sq[g][:, cols], scalar, inv[g][:, cols], ALU.mult, ALU.mult)
-                else:
-                    nc.vector.scalar_tensor_tensor(inv[g][:, cols], sq[g][:, cols], scalar, rs[g][:, cols], ALU.mult, ALU.mult)
+                u, c0 = divmod(t * jc, BANK)
+                square_t = sq[g, u][:, c0 : c0 + jc]
+                abundance = ab[:, PACK * b + t : PACK * b + t + 1]
+                nc.vector.scalar_tensor_tensor(dst[:, cols], square_t, abundance, factor[:, cols], ALU.mult, ALU.mult)
 
-        def weave(g):
-            hi[g] = work.tile([P, PACK * width(g)], BF16, name="hi", bufs=3, align_bytes=64)
-            if on_scalar(g):
-                interleave(nc.vector.tensor_copy, hi[g], hb[g])
+        def weave_h(g):
+            hi[g] = work.tile([P, PACK * width(g)], BF16, name="hi", align_bytes=64)
+            if g >= SQUARED_FROM:
+                nc.vector.tensor_copy(woven(hi[g], LINE), sliced(hb[g], LINE))
             else:
-                nc.vector.tensor_tensor(
-                    hi[g][:].rearrange("p (g i t) -> p g t i", i=PAIR, t=PACK),
-                    inv[g][:].rearrange("p (t g i) -> p g t i", i=PAIR, t=PACK),
-                    rs[g][:].rearrange("p (t g i) -> p g t i", i=PAIR, t=PACK),
-                    ALU.mult,
-                )
+                nc.vector.tensor_tensor(woven(hi[g], PAIR), sliced(partial[g], PAIR), sliced(rs[g], PAIR), ALU.mult)
 
         def quantise_h(g):
-            hq[g] = work.tile([P, width(g)], U32, name="hq", bufs=AHEAD + 1, align_bytes=64)
+            two_banks = g + 1 < groups and banks(width(g + 1)) > 1
+            hq[g] = held([P, width(g)], U32, "hq_%d" % g, tag="sq_%d" % (g + 1) if two_banks else "")
             hq_s[g] = work.tile([P, width(g)], U8, name="hq_s", bufs=AHEAD + 1, align_bytes=64)
             nc.vector.quantize_mx(out=hq[g][:].bitcast(FP8X4), scales=hq_s[g][:], in_=hi[g][:])
 
@@ -252,11 +235,10 @@ def tile_list_motif_promoter_activity_kernel(
         out_rows = out_0.rearrange("(p t) j -> p t j", t=PACK)
         out_words = out_1[0].rearrange("p m t -> p (m t)").bitcast(I32)
 
-        def pathways(c):
+        def finish(c, w4, w4_s):
             jc = CHUNKS[c]
             per_bank = BANK // jc
-            w4, w4_s = w4_tiles
-            y[c] = work.tile([P, PACK * jc], F32, name="y")
+            y = work.tile([P, PACK * jc], F32, name="y")
             behind = PASSES * c + COPY_LAG
             first = held([P, PACK * jc], F32, "first_%d" % c, tag="rs_%d" % behind if behind < groups else "")
             for u in range(banks(jc)):
@@ -288,52 +270,40 @@ def tile_list_motif_promoter_activity_kernel(
                             )
                 cols = slice(u * BANK, (u + 1) * BANK)
                 nc.scalar.copy(first[:, cols], p1[:])
-                nc.vector.tensor_tensor(y[c][:, cols], p2[:], first[:, cols], ALU.mult)
+                nc.vector.tensor_tensor(y[:, cols], p2[:], first[:, cols], ALU.mult)
             genes = slice(starts[c], starts[c] + jc)
-            nc.sync.dma_start(out_rows[:, :, genes], y[c][:].rearrange("p (t j) -> p t j", t=PACK))
-
-        def weave_y(c):
-            yi[c] = work.tile([P, PACK * CHUNKS[c]], BF16, name="yi", bufs=2, align_bytes=64)
-            interleave(nc.scalar.copy if c in Y_ON_SCALAR else nc.vector.tensor_copy, yi[c], y[c])
-
-        def quantise_y(c):
-            genes = slice(starts[c], starts[c] + CHUNKS[c])
-            yq = work.tile([P, CHUNKS[c]], U32, name="yq", bufs=2, align_bytes=64)
-            nc.vector.quantize_mx(out=yq[:].bitcast(FP8X4), scales=y_s[:, genes], in_=yi[c][:])
+            nc.sync.dma_start(out_rows[:, :, genes], y[:].rearrange("p (t j) -> p t j", t=PACK))
+            yi = work.tile([P, PACK * jc], BF16, name="yi", bufs=2, align_bytes=64)
+            copy = nc.scalar.copy if c in WOVEN_ON_SCALAR else nc.vector.tensor_copy
+            copy(woven(yi, LINE), sliced(y, LINE))
+            yq = work.tile([P, jc], U32, name="yq", bufs=2, align_bytes=64)
+            nc.vector.quantize_mx(out=yq[:].bitcast(FP8X4), scales=y_s[:, genes], in_=yi[:])
             nc.sync.dma_start(out_words[:, genes], yq[:].bitcast(I32))
-
-        def finish(c):
-            pathways(c)
-            weave_y(c)
-            quantise_y(c)
 
         for bank in range(AFF_BANKS):
             affinity(*divmod(bank, banks(CHUNKS[0])), 0)
-        for u in range(PACK):
+        for u in range(banks(width(0))):
             square(0, u)
-        for step in range(groups):
-            if step + 1 < groups:
-                square(step + 1, 0)
-            root(step)
-            if step + 1 < groups:
-                for u in range(1, PACK):
-                    square(step + 1, u)
-            inverse(step)
-            weigh(step)
-            if step >= 1:
-                quantise_h(step - 1)
-            weave(step)
-            if step == 1:
-                cast_w()
-            if step == 2:
-                deal_w4()
-                quantise_w()
-            if step >= COPY_LAG and (step - COPY_LAG) % PASSES == 0:
-                finish((step - COPY_LAG) // PASSES)
+        for g in range(groups):
+            if g + 1 < groups:
+                square(g + 1, 0)
+            root(g)
+            if g + 1 < groups:
+                for u in range(1, banks(width(g + 1))):
+                    square(g + 1, u)
+            weigh(g)
+            if g >= 1:
+                quantise_h(g - 1)
+            weave_h(g)
+            if g == PASSES - 1:
+                w_bf = cast_w()
+            if g == PASSES:
+                w4, w4_s = deal_w4()
+                quantise_w(w_bf)
+            if g >= COPY_LAG and (g - COPY_LAG) % PASSES == 0:
+                finish((g - COPY_LAG) // PASSES, w4, w4_s)
         quantise_h(groups - 1)
-        for c in range(len(CHUNKS)):
-            if c not in y:
-                finish(c)
+        finish(len(CHUNKS) - 1, w4, w4_s)
         for q in range(4):
             queue = nc.scalar if q % 2 else nc.sync
             queue.dma_start(out_2[0, 4 * q : 4 * q + 4, :].bitcast(I32), y_s[32 * q : 32 * q + 4, :].bitcast(I32))

@@ -26,7 +26,7 @@ LINE = 4
 PAIR = 2
 LINE_BYTES = 16
 CHUNKS = (256, 256, 256, 128, 128)
-ROW1, ROW2 = 0, 8
+ROWS = 16
 AHEAD = 5
 AFF_BANKS = 4
 SQUARED_FROM = 3
@@ -43,6 +43,10 @@ def tile_list_motif_promoter_activity_kernel(
         keep = ctx.enter_context(tc.tile_pool(name="keep", bufs=1))
         work = ctx.enter_context(tc.tile_pool(name="work", bufs=3))
         psum = ctx.enter_context(tc.psum_pool(name="psum", bufs=2))
+        big = ctx.enter_context(tc.tile_pool(name="big", bufs=1))
+
+        def placed(shape, dtype, name, offset):
+            return big.tile(shape, dtype, name=name, offset=offset, align_bytes=64)
 
         def held(shape, dtype, name, tag=""):
             return keep.tile(shape, dtype, name=name, tag=tag, align_bytes=64)
@@ -55,43 +59,40 @@ def tile_list_motif_promoter_activity_kernel(
 
         win1_s = held([P, T1], U8, "win1_s", tag="win1_s")
         win2_s = held([P, T2], U8, "win2_s", tag="win2_s")
+        for win in (win1_s, win2_s):
+            nc.vector.memset(win[32:64, :].bitcast(I32), 0)
+            nc.vector.memset(win[64:P, :].bitcast(I32), 0)
+        planes = [held([P, S1 + S2], U8, "plane%d" % a) for a in range(PASSES)]
         one = held([P, 1], F32, "one")
-        nc.vector.memset(win2_s[:].bitcast(I32), 0)
         nc.gpsimd.memset(one[:], 1.0)
-        nc.gpsimd.memset(win1_s[:].bitcast(I32), 0)
-        unit = held([P, 1], F32, "unit")
-        nc.scalar.activation(unit[:], one[:], ACT.Abs_reciprocal_sqrt)
+        nc.gpsimd.memset(planes[1][:].bitcast(I32), 0)
+        unit_row = held([P, 1], F32, "unit_row")
+        nc.scalar.activation(unit_row[:], one[:], ACT.Abs_reciprocal_sqrt)
+        unit = unit_row[:, 0:1]
 
         idx1 = keep.tile([P, S1 // 16], U16, name="idx1")
         idx2 = keep.tile([P, S2 // 16], U16, name="idx2")
         win1 = [held([P, T1], U32, "win1_%d" % a, tag="win1_%d" % a) for a in range(PASSES)]
-        win2 = [held([P, T2], U32, "win2_%d" % a, tag="win2_%d" % a) for a in range(PASSES)]
+        win2 = [placed([P, T2], U32, "win2_%d" % a, 4 * T2 * a) for a in range(PASSES)]
 
-        def load_words(dst, src, pieces):
-            words = src.rearrange("p n t -> p (n t)").bitcast(I32)
-            step = words.shape[1] // pieces
-            for c0 in range(0, words.shape[1], step):
-                nc.sync.dma_start(dst[:, c0 : c0 + step].bitcast(I32), words[:, c0 : c0 + step])
+        def load_words(dst, src):
+            nc.sync.dma_start(dst[:].bitcast(I32), src.rearrange("p n t -> p (n t)").bitcast(I32))
 
-        def load_scales(queue, win, src, row):
-            for q in range(4):
-                queue.dma_start(
-                    win[32 * q + row : 32 * q + row + 4 * PASSES, :].bitcast(I32),
-                    src[:, 4 * q : 4 * q + 4, :].bitcast(I32),
-                )
+        def load_scales(win, src):
+            nc.sync.dma_start(win[: PASSES * ROWS, :].bitcast(I32), src.rearrange("a q n -> (a q) n").bitcast(I32))
 
-        load_scales(nc.gpsimd, win2_s, tab2_scales, ROW2)
         nc.sync.dma_start(idx1[:], offs)
-        for a in range(PASSES):
-            load_words(win1[a], tab_words[a], 2)
+        load_scales(win1_s, tab_scales)
         nc.sync.dma_start(idx2[:], offs2)
+        load_scales(win2_s, tab2_scales)
+        for a in range(PASSES):
+            load_words(win1[a], tab_words[a])
         ab = held([P, PASSES * PACK], F32, "ab")
         nc.sync.dma_start(
             ab[:].rearrange("p (b t) -> p b t", b=PASSES), abund.rearrange("(b p t) -> p b t", b=PASSES, t=PACK)
         )
-        load_scales(nc.sync, win1_s, tab_scales, ROW1)
         for a in range(PASSES):
-            load_words(win2[a], tab2_words[a], 1)
+            load_words(win2[a], tab2_words[a])
 
         def deal(dst, src, column_bytes):
             per_line = LINE_BYTES // column_bytes
@@ -100,28 +101,44 @@ def tile_list_motif_promoter_activity_kernel(
                 src.rearrange("p (b x i t) -> p b x t i", b=PASSES, t=PACK, i=per_line),
             )
 
+        picked_s = held([P, S1], U8, "picked_s")
+        picked2_s = held([P, S2], U8, "picked2_s", tag="picked0")
         picked = [held([P, S1], U32, "picked%d" % a, tag="picked%d" % a) for a in range(PASSES)]
         v1 = [held([P, S1], U32, "v1_%d" % a) for a in range(PASSES)]
-        picked_s = held([P, S1], U8, "picked_s")
-        v1_s = held([P, S1], U8, "v1_s")
-        v2_s = held([P, S2], U8, "v2_s", tag="win1_s")
+        nc.vector.tensor_copy(picked_s[:], win1_s[:].indirect(idx1[:]))
+        nc.vector.tensor_copy(picked2_s[:], win2_s[:].indirect(idx2[:]))
+        deal(planes[0][:, :S1], picked_s[:], 1)
+        nc.vector.tensor_copy(planes[0][:, S1:].bitcast(I32), picked2_s[:].bitcast(I32))
+        for a in range(PASSES):
+            for q in range(4):
+                if a or q:
+                    src = ROWS * a + 4 * q
+                    nc.scalar.dma_start(
+                        planes[a][32 * q : 32 * q + 4, :].bitcast(I32), planes[0][src : src + 4, :].bitcast(I32)
+                    )
         for a in range(PASSES):
             nc.vector.tensor_copy(picked[a][:], win1[a][:].indirect(idx1[:]))
-        deal(v1[0][:], picked[0][:], 4)
-        nc.vector.tensor_copy(picked_s[:], win1_s[:].indirect(idx1[:]))
-        deal(v1[1][:], picked[1][:], 4)
-        nc.vector.tensor_copy(v2_s[:], win2_s[:].indirect(idx2[:]))
-        deal(v1_s[:], picked_s[:], 1)
+            deal(v1[a][:], picked[a][:], 4)
 
-        w_raw = [held([P, PACK, N], F32, "w_raw%d" % b, tag="win1_%d" % b) for b in range(PASSES)]
+        w_all = held([P, PASSES, PACK, N], F32, "w_all", tag="picked1")
+        w_raw = [w_all[:, b, :, :] for b in range(PASSES)]
         for b in range(PASSES):
-            nc.sync.dma_start(w_raw[b][:], w[b * PASS : (b + 1) * PASS, :].rearrange("(p r) n -> p r n", r=PACK))
-        w4_raw = held([P, PASSES * 2 * N], U8, "w4_raw", tag="picked0")
+            nc.sync.dma_start(w_raw[b], w[b * PASS : (b + 1) * PASS, :].rearrange("(p r) n -> p r n", r=PACK))
+        w4_raw = held([P, PASSES * 2 * N], U8, "w4_raw", tag="win1_1")
         nc.sync.dma_start(
             w4_raw[:].bitcast(I32).rearrange("p (b n) -> p b n", b=PASSES),
             w4_words.bitcast(I32).rearrange("b p n -> p b n"),
         )
-        w4_s_raw = held([P, PASSES * N], U8, "w4_s_raw", tag="picked1")
+
+        v2 = {}
+        for a, h in ((0, 0), (1, 0), (1, 1), (0, 1)):
+            if (a, h) == (0, 1):
+                v2[a, h] = placed([P, HALF], U32, "v2_01", 4 * T2)
+            else:
+                v2[a, h] = held([P, HALF], U32, "v2_%d%d" % (a, h))
+            nc.vector.tensor_copy(v2[a, h][:], win2[a][:].indirect(idx2[:, h * HALF // 16 : (h + 1) * HALF // 16]))
+
+        w4_s_raw = placed([P, PASSES * N], U8, "w4_s_raw", 0)
         nc.vector.memset(w4_s_raw[:].bitcast(I32), 0)
         for q in range(4):
             nc.sync.dma_start(
@@ -129,26 +146,21 @@ def tile_list_motif_promoter_activity_kernel(
                 w4_scales[:, 4 * q : 4 * q + 4, :].bitcast(I32).rearrange("b r n -> r b n"),
             )
 
-        v2 = [held([P, S2], U32, "v2_0", tag="win2_s"), held([P, S2], U32, "v2_1", tag="win2_0")]
-        nc.vector.tensor_copy(v2[0][:], win2[0][:].indirect(idx2[:]))
-        for e0 in range(0, S2, HALF):
-            nc.vector.tensor_copy(v2[1][:, e0 : e0 + HALF], win2[1][:].indirect(idx2[:, e0 // 16 : (e0 + HALF) // 16]))
-
         wq = [held([P, N], U32, "wq%d" % b) for b in range(PASSES)]
         wq_s = [held([P, N], U8, "wq_s%d" % b) for b in range(PASSES)]
 
         def cast_w():
-            w_bf = held([P, PASSES, N * PACK], BF16, "w_bf", tag="win2_1")
+            w_bf = placed([P, PASSES, N * PACK], BF16, "w_bf", 2048)
             for b in range(PASSES):
                 nc.vector.tensor_copy(
                     w_bf[:, b, :].rearrange("p (t m r) -> p m r t", t=PACK, r=PACK),
-                    w_raw[b][:].rearrange("p r (m t) -> p m r t", t=PACK),
+                    w_raw[b].rearrange("p r (m t) -> p m r t", t=PACK),
                 )
             return w_bf
 
         def deal_w4():
             w4 = held([P, PASSES * 2 * N], U8, "w4", tag="win1_0")
-            w4_s = held([P, PASSES * N], U8, "w4_s", tag="win1_1")
+            w4_s = held([P, PASSES * N], U8, "w4_s", tag="picked0")
             deal(w4[:].bitcast(U16), w4_raw[:].bitcast(U16), 2)
             deal(w4_s[:], w4_s_raw[:], 1)
             return w4, w4_s
@@ -178,9 +190,9 @@ def tile_list_motif_promoter_activity_kernel(
                 nc.tensor.matmul_mx(
                     out=aff[g, u][:, e * jc : (e + 1) * jc],
                     lhsT=v1[a][:, m0 : m0 + P].bitcast(FP8X4),
-                    lhsT_scale=v1_s[ROW1 + 4 * a :, m0 : m0 + P],
-                    rhs=v2[a][:, starts[c] : starts[c] + jc].bitcast(FP8X4),
-                    rhs_scale=v2_s[ROW2 + 4 * a :, starts[c] : starts[c] + jc],
+                    lhsT_scale=planes[a][:, m0 : m0 + P],
+                    rhs=v2[a, starts[c] // HALF][:, starts[c] % HALF : starts[c] % HALF + jc].bitcast(FP8X4),
+                    rhs_scale=planes[a][:, S1 + starts[c] : S1 + starts[c] + jc],
                     start=(a == 0 and e == 0),
                     stop=(a == PASSES - 1 and e == per_bank - 1),
                 )
@@ -199,7 +211,7 @@ def tile_list_motif_promoter_activity_kernel(
             rs[g] = held([P, PACK * width(g)], F32, "rs_%d" % g, tag="rs_%d" % g)
             for u in range(banks(width(g))):
                 nc.scalar.activation(
-                    rs[g][:, u * BANK : (u + 1) * BANK], sq[g, u][:], ACT.Abs_reciprocal_sqrt, bias=unit[:]
+                    rs[g][:, u * BANK : (u + 1) * BANK], sq[g, u][:], ACT.Abs_reciprocal_sqrt, bias=unit
                 )
 
         def weigh(g):

@@ -26,12 +26,18 @@ LINE = 4
 PAIR = 2
 LINE_BYTES = 16
 CHUNKS = (256, 256, 256, 128, 128)
+GROUPS = (
+    (0, 0, 256), (1, 0, 256), (0, 256, 256), (1, 256, 256), (0, 512, 256), (1, 512, 256),
+    (0, 768, 256), (1, 768, 128), (1, 896, 128),
+)
+BEHIND = (3, 5, 7, 8, 9)
+QUANT_HELD = 7
 ROWS = 16
 AHEAD = 5
 AFF_BANKS = 4
-SQUARED_FROM = 3
+SQUARED_FROM = 5
 COPY_LAG = 3
-WOVEN_ON_SCALAR = (2, 3)
+WOVEN_ON_SCALAR = (0, 1, 2, 3)
 
 
 def tile_list_motif_promoter_activity_kernel(
@@ -114,7 +120,7 @@ def tile_list_motif_promoter_activity_kernel(
                 if a or q:
                     src = ROWS * a + 4 * q
                     nc.scalar.dma_start(
-                        planes[a][32 * q : 32 * q + 4, :].bitcast(I32), planes[0][src : src + 4, :].bitcast(I32)
+                        planes[a][32 * q + 4 * a : 32 * q + 4 * a + 4, :].bitcast(I32), planes[0][src : src + 4, :].bitcast(I32)
                     )
         for a in range(PASSES):
             nc.vector.tensor_copy(picked[a][:], win1[a][:].indirect(idx1[:]))
@@ -170,18 +176,17 @@ def tile_list_motif_promoter_activity_kernel(
                 nc.vector.quantize_mx(out=wq[b][:].bitcast(FP8X4), scales=wq_s[b][:], in_=w_bf[:, b, :])
 
         starts = [sum(CHUNKS[:c]) for c in range(len(CHUNKS))]
-        groups = PASSES * len(CHUNKS)
+        groups = len(GROUPS)
         aff, sq, rs, partial, hb, hi, hq, hq_s = {}, {}, {}, {}, {}, {}, {}, {}
 
         def width(g):
-            return CHUNKS[g // PASSES]
+            return GROUPS[g][2]
 
         def banks(jc):
             return PACK * jc // BANK
 
         def affinity(g, u, a):
-            c, b = divmod(g, PASSES)
-            jc = CHUNKS[c]
+            b, j0, jc = GROUPS[g]
             per_bank = BANK // jc
             if a == 0:
                 aff[g, u] = psum.tile([P, BANK], F32, name="aff", bufs=AFF_BANKS)
@@ -190,9 +195,9 @@ def tile_list_motif_promoter_activity_kernel(
                 nc.tensor.matmul_mx(
                     out=aff[g, u][:, e * jc : (e + 1) * jc],
                     lhsT=v1[a][:, m0 : m0 + P].bitcast(FP8X4),
-                    lhsT_scale=planes[a][:, m0 : m0 + P],
-                    rhs=v2[a, starts[c] // HALF][:, starts[c] % HALF : starts[c] % HALF + jc].bitcast(FP8X4),
-                    rhs_scale=planes[a][:, S1 + starts[c] : S1 + starts[c] + jc],
+                    lhsT_scale=planes[a][4 * a :, m0 : m0 + P],
+                    rhs=v2[a, j0 // HALF][:, j0 % HALF : j0 % HALF + jc].bitcast(FP8X4),
+                    rhs_scale=planes[a][4 * a :, S1 + j0 : S1 + j0 + jc],
                     start=(a == 0 and e == 0),
                     stop=(a == PASSES - 1 and e == per_bank - 1),
                 )
@@ -201,21 +206,20 @@ def tile_list_motif_promoter_activity_kernel(
             if (g, u) not in aff:
                 affinity(g, u, 0)
             affinity(g, u, 1)
-            if u + 1 < banks(width(g)):
-                sq[g, u] = held([P, BANK], F32, "sq_%d" % g, tag="sq_%d" % g)
-            else:
-                sq[g, u] = work.tile([P, BANK], F32, name="sq", bufs=AHEAD)
-            nc.scalar.activation(sq[g, u][:], aff[g, u][:], ACT.Square)
+            if u == 0:
+                sq[g] = held([P, PACK * width(g)], F32, "sq_%d" % g, tag="sq_%d" % g)
+            nc.scalar.activation(sq[g][:, u * BANK : (u + 1) * BANK], aff[g, u][:], ACT.Square)
 
         def root(g):
             rs[g] = held([P, PACK * width(g)], F32, "rs_%d" % g, tag="rs_%d" % g)
-            for u in range(banks(width(g))):
+            step = BANK if g == 0 else PACK * width(g)
+            for c0 in range(0, PACK * width(g), step):
                 nc.scalar.activation(
-                    rs[g][:, u * BANK : (u + 1) * BANK], sq[g, u][:], ACT.Abs_reciprocal_sqrt, bias=unit
+                    rs[g][:, c0 : c0 + step], sq[g][:, c0 : c0 + step], ACT.Abs_reciprocal_sqrt, bias=unit
                 )
 
         def weigh(g):
-            jc, b = width(g), g % PASSES
+            b, j0, jc = GROUPS[g]
             partial[g] = work.tile([P, PACK * jc], F32, name="partial", bufs=AHEAD)
             if g >= SQUARED_FROM:
                 nc.scalar.activation(partial[g][:], rs[g][:], ACT.Square)
@@ -225,10 +229,10 @@ def tile_list_motif_promoter_activity_kernel(
                 dst, factor = partial[g], rs[g]
             for t in range(PACK):
                 cols = slice(t * jc, (t + 1) * jc)
-                u, c0 = divmod(t * jc, BANK)
-                square_t = sq[g, u][:, c0 : c0 + jc]
                 abundance = ab[:, PACK * b + t : PACK * b + t + 1]
-                nc.vector.scalar_tensor_tensor(dst[:, cols], square_t, abundance, factor[:, cols], ALU.mult, ALU.mult)
+                nc.vector.scalar_tensor_tensor(
+                    dst[:, cols], sq[g][:, cols], abundance, factor[:, cols], ALU.mult, ALU.mult
+                )
 
         def weave_h(g):
             hi[g] = work.tile([P, PACK * width(g)], BF16, name="hi", align_bytes=64)
@@ -238,10 +242,13 @@ def tile_list_motif_promoter_activity_kernel(
                 nc.vector.tensor_tensor(woven(hi[g], PAIR), sliced(partial[g], PAIR), sliced(rs[g], PAIR), ALU.mult)
 
         def quantise_h(g):
-            two_banks = g + 1 < groups and banks(width(g + 1)) > 1
-            hq[g] = held([P, width(g)], U32, "hq_%d" % g, tag="sq_%d" % (g + 1) if two_banks else "")
+            hold = g + 1 < QUANT_HELD
+            hq[g] = held([P, width(g)], U32, "hq_%d" % g, tag="sq_%d" % (g + 1) if hold else "")
             hq_s[g] = work.tile([P, width(g)], U8, name="hq_s", bufs=AHEAD + 1, align_bytes=64)
             nc.vector.quantize_mx(out=hq[g][:].bitcast(FP8X4), scales=hq_s[g][:], in_=hi[g][:])
+
+        def group_of(b, j):
+            return [g for g, (gb, j0, jc) in enumerate(GROUPS) if gb == b and j0 <= j < j0 + jc][0]
 
         y_s = held([P, S2], U8, "y_s")
         out_rows = out_0.rearrange("(p t) j -> p t j", t=PACK)
@@ -251,20 +258,22 @@ def tile_list_motif_promoter_activity_kernel(
             jc = CHUNKS[c]
             per_bank = BANK // jc
             y = work.tile([P, PACK * jc], F32, name="y")
-            behind = PASSES * c + COPY_LAG
+            behind = BEHIND[c]
             first = held([P, PACK * jc], F32, "first_%d" % c, tag="rs_%d" % behind if behind < groups else "")
             for u in range(banks(jc)):
                 p1 = psum.tile([P, BANK], F32, name="p1")
                 p2 = psum.tile([P, BANK], F32, name="p2")
                 for b in range(PASSES):
+                    g = group_of(b, starts[c])
+                    h0 = starts[c] - GROUPS[g][1]
                     for e in range(per_bank):
                         m = slice((per_bank * u + e) * P, (per_bank * u + e + 1) * P)
                         nc.tensor.matmul_mx(
                             out=p1[:, e * jc : (e + 1) * jc],
                             lhsT=wq[b][:, m].bitcast(FP8X4),
                             lhsT_scale=wq_s[b][:, m],
-                            rhs=hq[PASSES * c + b][:].bitcast(FP8X4),
-                            rhs_scale=hq_s[PASSES * c + b][:],
+                            rhs=hq[g][:, h0 : h0 + jc].bitcast(FP8X4),
+                            rhs_scale=hq_s[g][:, h0 : h0 + jc],
                             start=(b == 0 and e == 0),
                             stop=(b == PASSES - 1 and e == per_bank - 1),
                         )
@@ -275,8 +284,8 @@ def tile_list_motif_promoter_activity_kernel(
                                 out=p2[:, e * jc + j0 : e * jc + j0 + P],
                                 lhsT=w4[:, 2 * m0 : 2 * (m0 + P)].bitcast(FP4X4),
                                 lhsT_scale=w4_s[:, m0 : m0 + P],
-                                rhs=hq[PASSES * c + b][:, j0 : j0 + P].bitcast(FP8X4),
-                                rhs_scale=hq_s[PASSES * c + b][:, j0 : j0 + P],
+                                rhs=hq[g][:, h0 + j0 : h0 + j0 + P].bitcast(FP8X4),
+                                rhs_scale=hq_s[g][:, h0 + j0 : h0 + j0 + P],
                                 start=(b == 0 and e == 0 and j0 == 0),
                                 stop=(b == PASSES - 1 and e == per_bank - 1 and j0 == jc - P),
                             )
@@ -293,7 +302,7 @@ def tile_list_motif_promoter_activity_kernel(
             nc.sync.dma_start(out_words[:, genes], yq[:].bitcast(I32))
 
         for bank in range(AFF_BANKS):
-            affinity(*divmod(bank, banks(CHUNKS[0])), 0)
+            affinity(*divmod(bank, banks(width(0))), 0)
         for u in range(banks(width(0))):
             square(0, u)
         for g in range(groups):
@@ -312,10 +321,13 @@ def tile_list_motif_promoter_activity_kernel(
             if g == PASSES:
                 w4, w4_s = deal_w4()
                 quantise_w(w_bf)
-            if g >= COPY_LAG and (g - COPY_LAG) % PASSES == 0:
-                finish((g - COPY_LAG) // PASSES, w4, w4_s)
+            for c in range(len(CHUNKS)):
+                if BEHIND[c] == g:
+                    finish(c, w4, w4_s)
         quantise_h(groups - 1)
-        finish(len(CHUNKS) - 1, w4, w4_s)
+        for c in range(len(CHUNKS)):
+            if BEHIND[c] >= groups:
+                finish(c, w4, w4_s)
         for q in range(4):
             queue = nc.scalar if q % 2 else nc.sync
             queue.dma_start(out_2[0, 4 * q : 4 * q + 4, :].bitcast(I32), y_s[32 * q : 32 * q + 4, :].bitcast(I32))

@@ -65,13 +65,12 @@ def tile_list_motif_promoter_activity_kernel(
 
         win1_s = held([P, T1], U8, "win1_s", tag="win1_s")
         win2_s = held([P, T2], U8, "win2_s", tag="win2_s")
-        for win in (win1_s, win2_s):
-            nc.vector.memset(win[32:64, :].bitcast(I32), 0)
-            nc.vector.memset(win[64:P, :].bitcast(I32), 0)
-        planes = [held([P, S1 + S2], U8, "plane%d" % a) for a in range(PASSES)]
+        nc.vector.memset(win1_s[32:64, :].bitcast(I32), 0)
+        nc.vector.memset(win1_s[64:P, :].bitcast(I32), 0)
         one = held([P, 1], F32, "one")
         nc.gpsimd.memset(one[:], 1.0)
-        nc.gpsimd.memset(planes[1][:].bitcast(I32), 0)
+        nc.gpsimd.memset(win2_s[32:64, :].bitcast(I32), 0)
+        nc.gpsimd.memset(win2_s[64:P, :].bitcast(I32), 0)
         unit_row = held([P, 1], F32, "unit_row")
         nc.scalar.activation(unit_row[:], one[:], ACT.Abs_reciprocal_sqrt)
         unit = unit_row[:, 0:1]
@@ -80,6 +79,8 @@ def tile_list_motif_promoter_activity_kernel(
         idx2 = keep.tile([P, S2 // 16], U16, name="idx2")
         win1 = [held([P, T1], U32, "win1_%d" % a, tag="win1_%d" % a) for a in range(PASSES)]
         win2 = [placed([P, T2], U32, "win2_%d" % a, 4 * T2 * a) for a in range(PASSES)]
+
+        planes = [held([P, S1 + S2], U8, "plane%d" % a, tag="win1_1" if a else "") for a in range(PASSES)]
 
         def load_words(dst, src):
             nc.sync.dma_start(dst[:].bitcast(I32), src.rearrange("p n t -> p (n t)").bitcast(I32))
@@ -91,13 +92,12 @@ def tile_list_motif_promoter_activity_kernel(
         load_scales(win1_s, tab_scales)
         nc.sync.dma_start(idx2[:], offs2)
         load_scales(win2_s, tab2_scales)
-        for a in range(PASSES):
-            load_words(win1[a], tab_words[a])
         ab = held([P, PASSES * PACK], F32, "ab")
         nc.sync.dma_start(
             ab[:].rearrange("p (b t) -> p b t", b=PASSES), abund.rearrange("(b p t) -> p b t", b=PASSES, t=PACK)
         )
         for a in range(PASSES):
+            load_words(win1[a], tab_words[a])
             load_words(win2[a], tab2_words[a])
 
         def deal(dst, src, column_bytes):
@@ -109,28 +109,29 @@ def tile_list_motif_promoter_activity_kernel(
 
         picked_s = held([P, S1], U8, "picked_s")
         picked2_s = held([P, S2], U8, "picked2_s", tag="picked0")
-        picked = [held([P, S1], U32, "picked%d" % a, tag="picked%d" % a) for a in range(PASSES)]
+        picked = [held([P, S1], U32, "picked0", tag="picked0"), placed([P, S1], U32, "picked1", 8 * T2)]
         v1 = [held([P, S1], U32, "v1_%d" % a) for a in range(PASSES)]
         nc.vector.tensor_copy(picked_s[:], win1_s[:].indirect(idx1[:]))
         nc.vector.tensor_copy(picked2_s[:], win2_s[:].indirect(idx2[:]))
         deal(planes[0][:, :S1], picked_s[:], 1)
         nc.vector.tensor_copy(planes[0][:, S1:].bitcast(I32), picked2_s[:].bitcast(I32))
-        for a in range(PASSES):
-            for q in range(4):
-                if a or q:
-                    src = ROWS * a + 4 * q
-                    nc.scalar.dma_start(
-                        planes[a][32 * q + 4 * a : 32 * q + 4 * a + 4, :].bitcast(I32), planes[0][src : src + 4, :].bitcast(I32)
-                    )
+        for q in range(1, 4):
+            nc.scalar.dma_start(
+                planes[0][32 * q : 32 * q + 4, :].bitcast(I32), planes[0][4 * q : 4 * q + 4, :].bitcast(I32)
+            )
         for a in range(PASSES):
             nc.vector.tensor_copy(picked[a][:], win1[a][:].indirect(idx1[:]))
             deal(v1[a][:], picked[a][:], 4)
 
-        w_all = held([P, PASSES, PACK, N], F32, "w_all", tag="picked1")
+        for r in range(4):
+            nc.sync.dma_start(
+                planes[1][4 + r : P : 32, :].bitcast(I32), planes[0][ROWS + r : 2 * ROWS : 4, :].bitcast(I32)
+            )
+        w_all = placed([P, PASSES, PACK, N], F32, "w_all", 8 * T2 + 2048)
         w_raw = [w_all[:, b, :, :] for b in range(PASSES)]
         for b in range(PASSES):
             nc.sync.dma_start(w_raw[b], w[b * PASS : (b + 1) * PASS, :].rearrange("(p r) n -> p r n", r=PACK))
-        w4_raw = held([P, PASSES * 2 * N], U8, "w4_raw", tag="win1_1")
+        w4_raw = placed([P, PASSES * 2 * N], U8, "w4_raw", 8 * T2)
         nc.sync.dma_start(
             w4_raw[:].bitcast(I32).rearrange("p (b n) -> p b n", b=PASSES),
             w4_words.bitcast(I32).rearrange("b p n -> p b n"),

@@ -124,7 +124,7 @@ def tile_list_motif_promoter_activity_kernel(
             deal(v1[a][:], picked[a][:], 4)
 
         for r in range(4):
-            nc.sync.dma_start(
+            nc.scalar.dma_start(
                 planes[1][4 + r : P : 32, :].bitcast(I32), planes[0][ROWS + r : 2 * ROWS : 4, :].bitcast(I32)
             )
         w_all = placed([P, PASSES, PACK, N], F32, "w_all", 8 * T2 + 2048)

@@ -30,10 +30,12 @@ GROUPS = (
     (0, 0, 256), (1, 0, 256), (0, 256, 256), (1, 256, 256), (0, 512, 256), (1, 512, 256),
     (0, 768, 256), (1, 768, 128), (1, 896, 128),
 )
-BEHIND = (3, 5, 7, 8, 9)
+BEHIND = (4, 6, 7, 9, 10)
 QUANT_HELD = 7
+LATE = 3
+PLANES_AT = (6, 8, 9, 10, 11)
 ROWS = 16
-AHEAD = 5
+AHEAD = 4
 AFF_BANKS = 4
 SQUARED_FROM = 5
 COPY_LAG = 3
@@ -156,14 +158,15 @@ def tile_list_motif_promoter_activity_kernel(
         wq = [held([P, N], U32, "wq%d" % b) for b in range(PASSES)]
         wq_s = [held([P, N], U8, "wq_s%d" % b) for b in range(PASSES)]
 
-        def cast_w():
-            w_bf = placed([P, PASSES, N * PACK], BF16, "w_bf", 2048)
-            for b in range(PASSES):
-                nc.vector.tensor_copy(
-                    w_bf[:, b, :].rearrange("p (t m r) -> p m r t", t=PACK, r=PACK),
-                    w_raw[b].rearrange("p r (m t) -> p m r t", t=PACK),
-                )
-            return w_bf
+        w_bf = {}
+
+        def cast_w(b):
+            w_bf[b] = placed([P, N * PACK], BF16, "w_bf%d" % b, 2048 + 4096 * b)
+            copy = nc.vector.tensor_copy
+            copy(
+                w_bf[b][:].rearrange("p (t m r) -> p m r t", t=PACK, r=PACK),
+                w_raw[b].rearrange("p r (m t) -> p m r t", t=PACK),
+            )
 
         def deal_w4():
             w4 = held([P, PASSES * 2 * N], U8, "w4", tag="win1_0")
@@ -172,9 +175,9 @@ def tile_list_motif_promoter_activity_kernel(
             deal(w4_s[:], w4_s_raw[:], 1)
             return w4, w4_s
 
-        def quantise_w(w_bf):
+        def quantise_w():
             for b in range(PASSES):
-                nc.vector.quantize_mx(out=wq[b][:].bitcast(FP8X4), scales=wq_s[b][:], in_=w_bf[:, b, :])
+                nc.vector.quantize_mx(out=wq[b][:].bitcast(FP8X4), scales=wq_s[b][:], in_=w_bf[b][:])
 
         starts = [sum(CHUNKS[:c]) for c in range(len(CHUNKS))]
         groups = len(GROUPS)
@@ -251,6 +254,7 @@ def tile_list_motif_promoter_activity_kernel(
         def group_of(b, j):
             return [g for g, (gb, j0, jc) in enumerate(GROUPS) if gb == b and j0 <= j < j0 + jc][0]
 
+        ys = {}
         y_s = held([P, S2], U8, "y_s")
         out_rows = out_0.rearrange("(p t) j -> p t j", t=PACK)
         out_words = out_1[0].rearrange("p m t -> p (m t)").bitcast(I32)
@@ -258,12 +262,15 @@ def tile_list_motif_promoter_activity_kernel(
         def finish(c, w4, w4_s):
             jc = CHUNKS[c]
             per_bank = BANK // jc
-            y = work.tile([P, PACK * jc], F32, name="y")
-            behind = BEHIND[c]
-            first = held([P, PACK * jc], F32, "first_%d" % c, tag="rs_%d" % behind if behind < groups else "")
+            y = ys[c] = held([P, PACK * jc], F32, "y_%d" % c)
+            first = work.tile([P, PACK * jc], F32, name="first", bufs=2)
             for u in range(banks(jc)):
-                p1 = psum.tile([P, BANK], F32, name="p1")
-                p2 = psum.tile([P, BANK], F32, name="p2")
+                if c < LATE:
+                    p1 = psum.tile([P, BANK], F32, name="p1")
+                    p2 = psum.tile([P, BANK], F32, name="p2")
+                else:
+                    p1 = psum.tile([P, BANK], F32, name="aff", bufs=AFF_BANKS)
+                    p2 = psum.tile([P, BANK], F32, name="aff", bufs=AFF_BANKS)
                 for b in range(PASSES):
                     g = group_of(b, starts[c])
                     h0 = starts[c] - GROUPS[g][1]
@@ -295,6 +302,11 @@ def tile_list_motif_promoter_activity_kernel(
                 nc.vector.tensor_tensor(y[:, cols], p2[:], first[:, cols], ALU.mult)
             genes = slice(starts[c], starts[c] + jc)
             nc.sync.dma_start(out_rows[:, :, genes], y[:].rearrange("p (t j) -> p t j", t=PACK))
+
+        def finish_planes(c):
+            jc = CHUNKS[c]
+            y = ys[c]
+            genes = slice(starts[c], starts[c] + jc)
             yi = work.tile([P, PACK * jc], BF16, name="yi", bufs=2, align_bytes=64)
             copy = nc.scalar.copy if c in WOVEN_ON_SCALAR else nc.vector.tensor_copy
             copy(woven(yi, LINE), sliced(y, LINE))
@@ -318,17 +330,23 @@ def tile_list_motif_promoter_activity_kernel(
                 quantise_h(g - 1)
             weave_h(g)
             if g == PASSES - 1:
-                w_bf = cast_w()
+                cast_w(0)
             if g == PASSES:
                 w4, w4_s = deal_w4()
-                quantise_w(w_bf)
+                cast_w(1)
+                quantise_w()
             for c in range(len(CHUNKS)):
                 if BEHIND[c] == g:
                     finish(c, w4, w4_s)
+                if PLANES_AT[c] == g:
+                    finish_planes(c)
         quantise_h(groups - 1)
-        for c in range(len(CHUNKS)):
-            if BEHIND[c] >= groups:
-                finish(c, w4, w4_s)
+        for g in range(groups, 12):
+            for c in range(len(CHUNKS)):
+                if BEHIND[c] == g:
+                    finish(c, w4, w4_s)
+                if PLANES_AT[c] == g:
+                    finish_planes(c)
         for q in range(4):
             queue = nc.scalar if q % 2 else nc.sync
             queue.dma_start(out_2[0, 4 * q : 4 * q + 4, :].bitcast(I32), y_s[32 * q : 32 * q + 4, :].bitcast(I32))

@@ -25,21 +25,18 @@ BANK = 512
 LINE = 4
 PAIR = 2
 LINE_BYTES = 16
-CHUNKS = (256, 256, 256, 128, 128)
-GROUPS = (
-    (0, 0, 256), (1, 0, 256), (0, 256, 256), (1, 256, 256), (0, 512, 256), (1, 512, 256),
-    (0, 768, 256), (1, 768, 128), (1, 896, 128),
-)
-BEHIND = (4, 6, 7, 9, 10)
-QUANT_HELD = 7
-LATE = 3
-PLANES_AT = (6, 8, 9, 10, 11)
 ROWS = 16
+WIDE, SHORT = 256, 128
+CHUNKS = (WIDE, WIDE, WIDE, SHORT, SHORT)
+GROUPS = tuple((b, j0, WIDE) for j0 in range(0, S2, WIDE) for b in range(PASSES))[:-1] + (
+    (PASSES - 1, S2 - WIDE, SHORT),
+    (PASSES - 1, S2 - SHORT, SHORT),
+)
 AHEAD = 4
 AFF_BANKS = 4
+MOVES_AHEAD = 3
 SQUARED_FROM = 5
-COPY_LAG = 3
-WOVEN_ON_SCALAR = (0, 1, 2, 3)
+LAG_TWO_PRODUCTS, LAG_SQUARED = 3, 2
 
 
 def tile_list_motif_promoter_activity_kernel(
@@ -51,10 +48,10 @@ def tile_list_motif_promoter_activity_kernel(
         keep = ctx.enter_context(tc.tile_pool(name="keep", bufs=1))
         work = ctx.enter_context(tc.tile_pool(name="work", bufs=3))
         psum = ctx.enter_context(tc.psum_pool(name="psum", bufs=2))
-        big = ctx.enter_context(tc.tile_pool(name="big", bufs=1))
+        table2 = ctx.enter_context(tc.tile_pool(name="table2", bufs=1))
 
         def placed(shape, dtype, name, offset):
-            return big.tile(shape, dtype, name=name, offset=offset, align_bytes=64)
+            return table2.tile(shape, dtype, name=name, offset=offset, align_bytes=64)
 
         def held(shape, dtype, name, tag=""):
             return keep.tile(shape, dtype, name=name, tag=tag, align_bytes=64)
@@ -69,6 +66,8 @@ def tile_list_motif_promoter_activity_kernel(
         win2_s = held([P, T2], U8, "win2_s", tag="win2_s")
         nc.vector.memset(win1_s[32:64, :].bitcast(I32), 0)
         nc.vector.memset(win1_s[64:P, :].bitcast(I32), 0)
+        w4_s_raw = held([P, PASSES * N], U8, "w4_s_raw")
+        nc.vector.memset(w4_s_raw[:].bitcast(I32), 0)
         one = held([P, 1], F32, "one")
         nc.gpsimd.memset(one[:], 1.0)
         nc.gpsimd.memset(win2_s[32:64, :].bitcast(I32), 0)
@@ -82,7 +81,7 @@ def tile_list_motif_promoter_activity_kernel(
         win1 = [held([P, T1], U32, "win1_%d" % a, tag="win1_%d" % a) for a in range(PASSES)]
         win2 = [placed([P, T2], U32, "win2_%d" % a, 4 * T2 * a) for a in range(PASSES)]
 
-        planes = [held([P, S1 + S2], U8, "plane%d" % a, tag="win1_1" if a else "") for a in range(PASSES)]
+        planes = [held([P, S1 + S2], U8, "plane%d" % a, tag="win1_s" if a else "") for a in range(PASSES)]
 
         def load_words(dst, src):
             nc.sync.dma_start(dst[:].bitcast(I32), src.rearrange("p n t -> p (n t)").bitcast(I32))
@@ -98,9 +97,9 @@ def tile_list_motif_promoter_activity_kernel(
         nc.sync.dma_start(
             ab[:].rearrange("p (b t) -> p b t", b=PASSES), abund.rearrange("(b p t) -> p b t", b=PASSES, t=PACK)
         )
-        for a in range(PASSES):
-            load_words(win1[a], tab_words[a])
-            load_words(win2[a], tab2_words[a])
+        load_words(win1[0], tab_words[0])
+        load_words(win2[0], tab2_words[0])
+        load_words(win1[1], tab_words[1])
 
         def deal(dst, src, column_bytes):
             per_line = LINE_BYTES // column_bytes
@@ -111,29 +110,36 @@ def tile_list_motif_promoter_activity_kernel(
 
         picked_s = held([P, S1], U8, "picked_s")
         picked2_s = held([P, S2], U8, "picked2_s", tag="picked0")
-        picked = [held([P, S1], U32, "picked0", tag="picked0"), placed([P, S1], U32, "picked1", 8 * T2)]
+        picked = [held([P, S1], U32, "picked0", tag="picked0"), held([P, S1], U32, "picked1")]
         v1 = [held([P, S1], U32, "v1_%d" % a) for a in range(PASSES)]
         nc.vector.tensor_copy(picked_s[:], win1_s[:].indirect(idx1[:]))
         nc.vector.tensor_copy(picked2_s[:], win2_s[:].indirect(idx2[:]))
         deal(planes[0][:, :S1], picked_s[:], 1)
         nc.vector.tensor_copy(planes[0][:, S1:].bitcast(I32), picked2_s[:].bitcast(I32))
         for q in range(1, 4):
-            nc.scalar.dma_start(
+            nc.sync.dma_start(
                 planes[0][32 * q : 32 * q + 4, :].bitcast(I32), planes[0][4 * q : 4 * q + 4, :].bitcast(I32)
             )
+
+        def move_row(r):
+            nc.sync.dma_start(
+                planes[1][4 + r : P : 32, :].bitcast(I32), planes[0][ROWS + r : 2 * ROWS : 4, :].bitcast(I32)
+            )
+
+        for r in range(MOVES_AHEAD):
+            move_row(r)
+        load_words(win2[1], tab2_words[1])
+        for r in range(MOVES_AHEAD, 4):
+            move_row(r)
         for a in range(PASSES):
             nc.vector.tensor_copy(picked[a][:], win1[a][:].indirect(idx1[:]))
             deal(v1[a][:], picked[a][:], 4)
 
-        for r in range(4):
-            nc.scalar.dma_start(
-                planes[1][4 + r : P : 32, :].bitcast(I32), planes[0][ROWS + r : 2 * ROWS : 4, :].bitcast(I32)
-            )
-        w_all = placed([P, PASSES, PACK, N], F32, "w_all", 8 * T2 + 2048)
+        w_all = held([P, PASSES, PACK, N], F32, "w_all")
         w_raw = [w_all[:, b, :, :] for b in range(PASSES)]
         for b in range(PASSES):
             nc.sync.dma_start(w_raw[b], w[b * PASS : (b + 1) * PASS, :].rearrange("(p r) n -> p r n", r=PACK))
-        w4_raw = placed([P, PASSES * 2 * N], U8, "w4_raw", 8 * T2)
+        w4_raw = held([P, PASSES * 2 * N], U8, "w4_raw")
         nc.sync.dma_start(
             w4_raw[:].bitcast(I32).rearrange("p (b n) -> p b n", b=PASSES),
             w4_words.bitcast(I32).rearrange("b p n -> p b n"),
@@ -147,8 +153,6 @@ def tile_list_motif_promoter_activity_kernel(
                 v2[a, h] = held([P, HALF], U32, "v2_%d%d" % (a, h))
             nc.vector.tensor_copy(v2[a, h][:], win2[a][:].indirect(idx2[:, h * HALF // 16 : (h + 1) * HALF // 16]))
 
-        w4_s_raw = placed([P, PASSES * N], U8, "w4_s_raw", 0)
-        nc.vector.memset(w4_s_raw[:].bitcast(I32), 0)
         for q in range(4):
             nc.sync.dma_start(
                 w4_s_raw[32 * q : 32 * q + 4, :].bitcast(I32).rearrange("r (b n) -> r b n", b=PASSES),
@@ -157,13 +161,11 @@ def tile_list_motif_promoter_activity_kernel(
 
         wq = [held([P, N], U32, "wq%d" % b) for b in range(PASSES)]
         wq_s = [held([P, N], U8, "wq_s%d" % b) for b in range(PASSES)]
-
         w_bf = {}
 
         def cast_w(b):
-            w_bf[b] = placed([P, N * PACK], BF16, "w_bf%d" % b, 2048 + 4096 * b)
-            copy = nc.vector.tensor_copy
-            copy(
+            w_bf[b] = placed([P, N * PACK], BF16, "w_bf%d" % b, 2 * N * PACK * b)
+            nc.vector.tensor_copy(
                 w_bf[b][:].rearrange("p (t m r) -> p m r t", t=PACK, r=PACK),
                 w_raw[b].rearrange("p r (m t) -> p m r t", t=PACK),
             )
@@ -246,7 +248,7 @@ def tile_list_motif_promoter_activity_kernel(
                 nc.vector.tensor_tensor(woven(hi[g], PAIR), sliced(partial[g], PAIR), sliced(rs[g], PAIR), ALU.mult)
 
         def quantise_h(g):
-            hold = g + 1 < QUANT_HELD
+            hold = g + 1 < groups and width(g + 1) == WIDE
             hq[g] = held([P, width(g)], U32, "hq_%d" % g, tag="sq_%d" % (g + 1) if hold else "")
             hq_s[g] = work.tile([P, width(g)], U8, name="hq_s", bufs=AHEAD + 1, align_bytes=64)
             nc.vector.quantize_mx(out=hq[g][:].bitcast(FP8X4), scales=hq_s[g][:], in_=hi[g][:])
@@ -259,13 +261,13 @@ def tile_list_motif_promoter_activity_kernel(
         out_rows = out_0.rearrange("(p t) j -> p t j", t=PACK)
         out_words = out_1[0].rearrange("p m t -> p (m t)").bitcast(I32)
 
-        def finish(c, w4, w4_s):
+        def pathways(c, w4, w4_s):
             jc = CHUNKS[c]
             per_bank = BANK // jc
             y = ys[c] = held([P, PACK * jc], F32, "y_%d" % c)
             first = work.tile([P, PACK * jc], F32, name="first", bufs=2)
             for u in range(banks(jc)):
-                if c < LATE:
+                if jc == WIDE:
                     p1 = psum.tile([P, BANK], F32, name="p1")
                     p2 = psum.tile([P, BANK], F32, name="p2")
                 else:
@@ -303,16 +305,27 @@ def tile_list_motif_promoter_activity_kernel(
             genes = slice(starts[c], starts[c] + jc)
             nc.sync.dma_start(out_rows[:, :, genes], y[:].rearrange("p (t j) -> p t j", t=PACK))
 
-        def finish_planes(c):
+        def quantise_out(c):
             jc = CHUNKS[c]
             y = ys[c]
             genes = slice(starts[c], starts[c] + jc)
             yi = work.tile([P, PACK * jc], BF16, name="yi", bufs=2, align_bytes=64)
-            copy = nc.scalar.copy if c in WOVEN_ON_SCALAR else nc.vector.tensor_copy
+            copy = nc.scalar.copy if c + 1 < len(CHUNKS) else nc.vector.tensor_copy
             copy(woven(yi, LINE), sliced(y, LINE))
             yq = work.tile([P, jc], U32, name="yq", bufs=2, align_bytes=64)
             nc.vector.quantize_mx(out=yq[:].bitcast(FP8X4), scales=y_s[:, genes], in_=yi[:])
             nc.sync.dma_start(out_words[:, genes], yq[:].bitcast(I32))
+
+        last_group = [group_of(PASSES - 1, j0) for j0 in starts]
+        pathways_at = [g + (LAG_TWO_PRODUCTS if g < SQUARED_FROM else LAG_SQUARED) for g in last_group]
+        codes_at = [pathways_at[c] + banks(jc) for c, jc in enumerate(CHUNKS)]
+
+        def finish(step, w4, w4_s):
+            for c in range(len(CHUNKS)):
+                if pathways_at[c] == step:
+                    pathways(c, w4, w4_s)
+                if codes_at[c] == step:
+                    quantise_out(c)
 
         for bank in range(AFF_BANKS):
             affinity(*divmod(bank, banks(width(0))), 0)
@@ -335,18 +348,11 @@ def tile_list_motif_promoter_activity_kernel(
                 w4, w4_s = deal_w4()
                 cast_w(1)
                 quantise_w()
-            for c in range(len(CHUNKS)):
-                if BEHIND[c] == g:
-                    finish(c, w4, w4_s)
-                if PLANES_AT[c] == g:
-                    finish_planes(c)
+            if g >= PASSES:
+                finish(g, w4, w4_s)
         quantise_h(groups - 1)
-        for g in range(groups, 12):
-            for c in range(len(CHUNKS)):
-                if BEHIND[c] == g:
-                    finish(c, w4, w4_s)
-                if PLANES_AT[c] == g:
-                    finish_planes(c)
+        for step in range(groups, codes_at[-1] + 1):
+            finish(step, w4, w4_s)
         for q in range(4):
             queue = nc.scalar if q % 2 else nc.sync
             queue.dma_start(out_2[0, 4 * q : 4 * q + 4, :].bitcast(I32), y_s[32 * q : 32 * q + 4, :].bitcast(I32))

@@ -34,8 +34,7 @@ GROUPS = tuple((b, j0, WIDE) for j0 in range(0, S2, WIDE) for b in range(PASSES)
 )
 AHEAD = 4
 AFF_BANKS = 4
-MOVES_AHEAD = 3
-SQUARED_FROM = 5
+SQUARED_FROM = 4
 LAG_TWO_PRODUCTS, LAG_SQUARED = 3, 2
 
 
@@ -48,10 +47,10 @@ def tile_list_motif_promoter_activity_kernel(
         keep = ctx.enter_context(tc.tile_pool(name="keep", bufs=1))
         work = ctx.enter_context(tc.tile_pool(name="work", bufs=3))
         psum = ctx.enter_context(tc.psum_pool(name="psum", bufs=2))
-        table2 = ctx.enter_context(tc.tile_pool(name="table2", bufs=1))
+        by_offset = ctx.enter_context(tc.tile_pool(name="by_offset", bufs=1))
 
         def placed(shape, dtype, name, offset):
-            return table2.tile(shape, dtype, name=name, offset=offset, align_bytes=64)
+            return by_offset.tile(shape, dtype, name=name, offset=offset, align_bytes=64)
 
         def held(shape, dtype, name, tag=""):
             return keep.tile(shape, dtype, name=name, tag=tag, align_bytes=64)
@@ -66,8 +65,6 @@ def tile_list_motif_promoter_activity_kernel(
         win2_s = held([P, T2], U8, "win2_s", tag="win2_s")
         nc.vector.memset(win1_s[32:64, :].bitcast(I32), 0)
         nc.vector.memset(win1_s[64:P, :].bitcast(I32), 0)
-        w4_s_raw = held([P, PASSES * N], U8, "w4_s_raw")
-        nc.vector.memset(w4_s_raw[:].bitcast(I32), 0)
         one = held([P, 1], F32, "one")
         nc.gpsimd.memset(one[:], 1.0)
         nc.gpsimd.memset(win2_s[32:64, :].bitcast(I32), 0)
@@ -81,7 +78,7 @@ def tile_list_motif_promoter_activity_kernel(
         win1 = [held([P, T1], U32, "win1_%d" % a, tag="win1_%d" % a) for a in range(PASSES)]
         win2 = [placed([P, T2], U32, "win2_%d" % a, 4 * T2 * a) for a in range(PASSES)]
 
-        planes = [held([P, S1 + S2], U8, "plane%d" % a, tag="win1_s" if a else "") for a in range(PASSES)]
+        planes = [held([P, S1 + S2], U8, "plane%d" % a, tag="win1_1" if a else "") for a in range(PASSES)]
 
         def load_words(dst, src):
             nc.sync.dma_start(dst[:].bitcast(I32), src.rearrange("p n t -> p (n t)").bitcast(I32))
@@ -97,9 +94,9 @@ def tile_list_motif_promoter_activity_kernel(
         nc.sync.dma_start(
             ab[:].rearrange("p (b t) -> p b t", b=PASSES), abund.rearrange("(b p t) -> p b t", b=PASSES, t=PACK)
         )
-        load_words(win1[0], tab_words[0])
-        load_words(win2[0], tab2_words[0])
-        load_words(win1[1], tab_words[1])
+        for a in range(PASSES):
+            load_words(win1[a], tab_words[a])
+            load_words(win2[a], tab2_words[a])
 
         def deal(dst, src, column_bytes):
             per_line = LINE_BYTES // column_bytes
@@ -109,37 +106,32 @@ def tile_list_motif_promoter_activity_kernel(
             )
 
         picked_s = held([P, S1], U8, "picked_s")
+        behind_tables = PASSES * 4 * T2
         picked2_s = held([P, S2], U8, "picked2_s", tag="picked0")
-        picked = [held([P, S1], U32, "picked0", tag="picked0"), held([P, S1], U32, "picked1")]
+        picked = [held([P, S1], U32, "picked0", tag="picked0"), placed([P, S1], U32, "picked1", behind_tables)]
         v1 = [held([P, S1], U32, "v1_%d" % a) for a in range(PASSES)]
         nc.vector.tensor_copy(picked_s[:], win1_s[:].indirect(idx1[:]))
         nc.vector.tensor_copy(picked2_s[:], win2_s[:].indirect(idx2[:]))
         deal(planes[0][:, :S1], picked_s[:], 1)
         nc.vector.tensor_copy(planes[0][:, S1:].bitcast(I32), picked2_s[:].bitcast(I32))
         for q in range(1, 4):
-            nc.sync.dma_start(
+            nc.scalar.dma_start(
                 planes[0][32 * q : 32 * q + 4, :].bitcast(I32), planes[0][4 * q : 4 * q + 4, :].bitcast(I32)
             )
-
-        def move_row(r):
-            nc.sync.dma_start(
-                planes[1][4 + r : P : 32, :].bitcast(I32), planes[0][ROWS + r : 2 * ROWS : 4, :].bitcast(I32)
-            )
-
-        for r in range(MOVES_AHEAD):
-            move_row(r)
-        load_words(win2[1], tab2_words[1])
-        for r in range(MOVES_AHEAD, 4):
-            move_row(r)
         for a in range(PASSES):
             nc.vector.tensor_copy(picked[a][:], win1[a][:].indirect(idx1[:]))
             deal(v1[a][:], picked[a][:], 4)
 
-        w_all = held([P, PASSES, PACK, N], F32, "w_all")
+        for r in range(4):
+            nc.scalar.dma_start(
+                planes[1][4 + r : P : 32, :].bitcast(I32), planes[0][ROWS + r : 2 * ROWS : 4, :].bitcast(I32)
+            )
+        w4_bytes = PASSES * 2 * N
+        w_all = placed([P, PASSES, PACK, N], F32, "w_all", behind_tables + w4_bytes)
         w_raw = [w_all[:, b, :, :] for b in range(PASSES)]
         for b in range(PASSES):
             nc.sync.dma_start(w_raw[b], w[b * PASS : (b + 1) * PASS, :].rearrange("(p r) n -> p r n", r=PACK))
-        w4_raw = held([P, PASSES * 2 * N], U8, "w4_raw")
+        w4_raw = placed([P, w4_bytes], U8, "w4_raw", behind_tables)
         nc.sync.dma_start(
             w4_raw[:].bitcast(I32).rearrange("p (b n) -> p b n", b=PASSES),
             w4_words.bitcast(I32).rearrange("b p n -> p b n"),
@@ -153,6 +145,8 @@ def tile_list_motif_promoter_activity_kernel(
                 v2[a, h] = held([P, HALF], U32, "v2_%d%d" % (a, h))
             nc.vector.tensor_copy(v2[a, h][:], win2[a][:].indirect(idx2[:, h * HALF // 16 : (h + 1) * HALF // 16]))
 
+        w4_s_raw = placed([P, PASSES * N], U8, "w4_s_raw", 0)
+        nc.vector.memset(w4_s_raw[:].bitcast(I32), 0)
         for q in range(4):
             nc.sync.dma_start(
                 w4_s_raw[32 * q : 32 * q + 4, :].bitcast(I32).rearrange("r (b n) -> r b n", b=PASSES),
@@ -164,7 +158,7 @@ def tile_list_motif_promoter_activity_kernel(
         w_bf = {}
 
         def cast_w(b):
-            w_bf[b] = placed([P, N * PACK], BF16, "w_bf%d" % b, 2 * N * PACK * b)
+            w_bf[b] = placed([P, N * PACK], BF16, "w_bf%d" % b, 2 * N * PACK * (b + 1))
             nc.vector.tensor_copy(
                 w_bf[b][:].rearrange("p (t m r) -> p m r t", t=PACK, r=PACK),
                 w_raw[b].rearrange("p r (m t) -> p m r t", t=PACK),

@@ -26,6 +26,7 @@ LINE = 4
 PAIR = 2
 LINE_BYTES = 16
 ROWS = 16
+LAST_PIECES = (256, 256, 512)
 WIDE, SHORT = 256, 128
 CHUNKS = (WIDE, WIDE, WIDE, SHORT, SHORT)
 GROUPS = tuple((b, j0, WIDE) for j0 in range(0, S2, WIDE) for b in range(PASSES))[:-1] + (
@@ -138,12 +139,18 @@ def tile_list_motif_promoter_activity_kernel(
         )
 
         v2 = {}
-        for a, h in ((0, 0), (1, 0), (1, 1), (0, 1)):
-            if (a, h) == (0, 1):
-                v2[a, h] = placed([P, HALF], U32, "v2_01", 4 * T2)
-            else:
-                v2[a, h] = held([P, HALF], U32, "v2_%d%d" % (a, h))
-            nc.vector.tensor_copy(v2[a, h][:], win2[a][:].indirect(idx2[:, h * HALF // 16 : (h + 1) * HALF // 16]))
+
+        def gather_genes(a, j0, genes, tile):
+            nc.vector.tensor_copy(tile[:], win2[a][:].indirect(idx2[:, j0 // 16 : (j0 + genes) // 16]))
+            for j in range(0, genes, SHORT):
+                v2[a, j0 + j] = (tile, j)
+
+        gather_genes(0, 0, HALF, held([P, HALF], U32, "v2_00"))
+        j0 = 0
+        for n, piece in enumerate(LAST_PIECES):
+            gather_genes(1, j0, piece, held([P, piece], U32, "v2_1%d" % n))
+            j0 = j0 + piece
+        gather_genes(0, HALF, HALF, placed([P, HALF], U32, "v2_01", 4 * T2))
 
         w4_s_raw = placed([P, PASSES * N], U8, "w4_s_raw", 0)
         nc.vector.memset(w4_s_raw[:].bitcast(I32), 0)
@@ -196,7 +203,7 @@ def tile_list_motif_promoter_activity_kernel(
                     out=aff[g, u][:, e * jc : (e + 1) * jc],
                     lhsT=v1[a][:, m0 : m0 + P].bitcast(FP8X4),
                     lhsT_scale=planes[a][4 * a :, m0 : m0 + P],
-                    rhs=v2[a, j0 // HALF][:, j0 % HALF : j0 % HALF + jc].bitcast(FP8X4),
+                    rhs=v2[a, j0][0][:, v2[a, j0][1] : v2[a, j0][1] + jc].bitcast(FP8X4),
                     rhs_scale=planes[a][4 * a :, S1 + j0 : S1 + j0 + jc],
                     start=(a == 0 and e == 0),
                     stop=(a == PASSES - 1 and e == per_bank - 1),
@@ -321,7 +328,7 @@ def tile_list_motif_promoter_activity_kernel(
                 if codes_at[c] == step:
                     quantise_out(c)
 
-        for bank in range(AFF_BANKS):
+        for bank in range(banks(width(0))):
             affinity(*divmod(bank, banks(width(0))), 0)
         for u in range(banks(width(0))):
             square(0, u)

@@ -26,6 +26,8 @@ LINE = 4
 PAIR = 2
 LINE_BYTES = 16
 ROWS = 16
+ROW0 = P - PASSES * ROWS
+PLANE_ROW = (12, 4)
 LAST_PIECES = (256, 256, 512)
 WIDE, SHORT = 256, 128
 CHUNKS = (WIDE, WIDE, WIDE, SHORT, SHORT)
@@ -64,28 +66,27 @@ def tile_list_motif_promoter_activity_kernel(
 
         win1_s = held([P, T1], U8, "win1_s", tag="win1_s")
         win2_s = held([P, T2], U8, "win2_s", tag="win2_s")
-        nc.vector.memset(win1_s[32:64, :].bitcast(I32), 0)
-        nc.vector.memset(win1_s[64:P, :].bitcast(I32), 0)
+        nc.vector.memset(win1_s[:ROW0, :].bitcast(I32), 0)
+        nc.vector.memset(win2_s[:ROW0, :].bitcast(I32), 0)
         one = held([P, 1], F32, "one")
         nc.gpsimd.memset(one[:], 1.0)
-        nc.gpsimd.memset(win2_s[32:64, :].bitcast(I32), 0)
-        nc.gpsimd.memset(win2_s[64:P, :].bitcast(I32), 0)
         unit_row = held([P, 1], F32, "unit_row")
         nc.scalar.activation(unit_row[:], one[:], ACT.Abs_reciprocal_sqrt)
         unit = unit_row[:, 0:1]
 
         idx1 = keep.tile([P, S1 // 16], U16, name="idx1")
         idx2 = keep.tile([P, S2 // 16], U16, name="idx2")
-        win1 = [held([P, T1], U32, "win1_%d" % a, tag="win1_%d" % a) for a in range(PASSES)]
+        last_factors = PASSES * 4 * T2 + PASSES * 2 * N + PASSES * 4 * PACK * N
+        win1 = [held([P, T1], U32, "win1_0", tag="win1_0"), placed([P, T1], U32, "win1_1", last_factors)]
         win2 = [placed([P, T2], U32, "win2_%d" % a, 4 * T2 * a) for a in range(PASSES)]
 
-        planes = [held([P, S1 + S2], U8, "plane%d" % a, tag="win1_1" if a else "") for a in range(PASSES)]
+        planes = [held([P, S1 + S2], U8, "plane0"), placed([P, S1 + S2], U8, "plane1", last_factors)]
 
         def load_words(dst, src):
             nc.sync.dma_start(dst[:].bitcast(I32), src.rearrange("p n t -> p (n t)").bitcast(I32))
 
         def load_scales(win, src):
-            nc.sync.dma_start(win[: PASSES * ROWS, :].bitcast(I32), src.rearrange("a q n -> (a q) n").bitcast(I32))
+            nc.sync.dma_start(win[ROW0:, :].bitcast(I32), src.rearrange("a q n -> (a q) n").bitcast(I32))
 
         nc.sync.dma_start(idx1[:], offs)
         load_scales(win1_s, tab_scales)
@@ -115,17 +116,16 @@ def tile_list_motif_promoter_activity_kernel(
         nc.vector.tensor_copy(picked2_s[:], win2_s[:].indirect(idx2[:]))
         deal(planes[0][:, :S1], picked_s[:], 1)
         nc.vector.tensor_copy(planes[0][:, S1:].bitcast(I32), picked2_s[:].bitcast(I32))
-        for q in range(1, 4):
-            nc.scalar.dma_start(
-                planes[0][32 * q : 32 * q + 4, :].bitcast(I32), planes[0][4 * q : 4 * q + 4, :].bitcast(I32)
-            )
+        for q in range(3):
+            to, at = 32 * q + PLANE_ROW[0], ROW0 + 4 * q
+            nc.scalar.dma_start(planes[0][to : to + 4, :].bitcast(I32), planes[0][at : at + 4, :].bitcast(I32))
         for a in range(PASSES):
             nc.vector.tensor_copy(picked[a][:], win1[a][:].indirect(idx1[:]))
             deal(v1[a][:], picked[a][:], 4)
 
         for r in range(4):
             nc.scalar.dma_start(
-                planes[1][4 + r : P : 32, :].bitcast(I32), planes[0][ROWS + r : 2 * ROWS : 4, :].bitcast(I32)
+                planes[1][4 + r : P : 32, :].bitcast(I32), planes[0][ROW0 + ROWS + r : P : 4, :].bitcast(I32)
             )
         w4_bytes = PASSES * 2 * N
         w_all = placed([P, PASSES, PACK, N], F32, "w_all", behind_tables + w4_bytes)
@@ -145,7 +145,7 @@ def tile_list_motif_promoter_activity_kernel(
             for j in range(0, genes, SHORT):
                 v2[a, j0 + j] = (tile, j)
 
-        gather_genes(0, 0, HALF, held([P, HALF], U32, "v2_00"))
+        gather_genes(0, 0, HALF, placed([P, HALF], U32, "v2_00", last_factors + S1 + S2))
         j0 = 0
         for n, piece in enumerate(LAST_PIECES):
             gather_genes(1, j0, piece, held([P, piece], U32, "v2_1%d" % n))
@@ -202,9 +202,9 @@ def tile_list_motif_promoter_activity_kernel(
                 nc.tensor.matmul_mx(
                     out=aff[g, u][:, e * jc : (e + 1) * jc],
                     lhsT=v1[a][:, m0 : m0 + P].bitcast(FP8X4),
-                    lhsT_scale=planes[a][4 * a :, m0 : m0 + P],
+                    lhsT_scale=planes[a][PLANE_ROW[a] :, m0 : m0 + P],
                     rhs=v2[a, j0][0][:, v2[a, j0][1] : v2[a, j0][1] + jc].bitcast(FP8X4),
-                    rhs_scale=planes[a][4 * a :, S1 + j0 : S1 + j0 + jc],
+                    rhs_scale=planes[a][PLANE_ROW[a] :, S1 + j0 : S1 + j0 + jc],
                     start=(a == 0 and e == 0),
                     stop=(a == PASSES - 1 and e == per_bank - 1),
                 )
@@ -300,9 +300,11 @@ def tile_list_motif_promoter_activity_kernel(
                                 start=(b == 0 and e == 0 and j0 == 0),
                                 stop=(b == PASSES - 1 and e == per_bank - 1 and j0 == jc - P),
                             )
-                cols = slice(u * BANK, (u + 1) * BANK)
-                nc.scalar.copy(first[:, cols], p1[:])
-                nc.vector.tensor_tensor(y[:, cols], p2[:], first[:, cols], ALU.mult)
+                step = BANK // 2 if c + 1 == len(CHUNKS) else BANK
+                for c0 in range(0, BANK, step):
+                    part = slice(u * BANK + c0, u * BANK + c0 + step)
+                    nc.scalar.copy(first[:, part], p1[:, c0 : c0 + step])
+                    nc.vector.tensor_tensor(y[:, part], p2[:, c0 : c0 + step], first[:, part], ALU.mult)
             genes = slice(starts[c], starts[c] + jc)
             nc.sync.dma_start(out_rows[:, :, genes], y[:].rearrange("p (t j) -> p t j", t=PACK))
 
@@ -310,10 +312,10 @@ def tile_list_motif_promoter_activity_kernel(
             jc = CHUNKS[c]
             y = ys[c]
             genes = slice(starts[c], starts[c] + jc)
-            yi = work.tile([P, PACK * jc], BF16, name="yi", bufs=2, align_bytes=64)
+            yi = held([P, PACK * jc], BF16, "yi_%d" % c)
             copy = nc.scalar.copy if c + 1 < len(CHUNKS) else nc.vector.tensor_copy
             copy(woven(yi, LINE), sliced(y, LINE))
-            yq = work.tile([P, jc], U32, name="yq", bufs=2, align_bytes=64)
+            yq = held([P, jc], U32, "yq_%d" % c)
             nc.vector.quantize_mx(out=yq[:].bitcast(FP8X4), scales=y_s[:, genes], in_=yi[:])
             nc.sync.dma_start(out_words[:, genes], yq[:].bitcast(I32))
 

@@ -76,14 +76,12 @@ def tile_list_motif_promoter_activity_kernel(
 
         idx1 = keep.tile([P, S1 // 16], U16, name="idx1")
         idx2 = keep.tile([P, S2 // 16], U16, name="idx2")
-        last_factors = PASSES * 4 * T2 + PASSES * 2 * N + PASSES * 4 * PACK * N
-        win1 = [held([P, T1], U32, "win1_0", tag="win1_0"), placed([P, T1], U32, "win1_1", last_factors)]
+        win1 = [held([P, T1], U32, "win1_%d" % a, tag="win1_%d" % a) for a in range(PASSES)]
         win2 = [placed([P, T2], U32, "win2_%d" % a, 4 * T2 * a) for a in range(PASSES)]
+        planes = [held([P, S1 + S2], U8, "plane%d" % a, tag="win2_s" if a else "") for a in range(PASSES)]
 
-        planes = [held([P, S1 + S2], U8, "plane0"), placed([P, S1 + S2], U8, "plane1", last_factors)]
-
-        def load_words(dst, src):
-            nc.sync.dma_start(dst[:].bitcast(I32), src.rearrange("p n t -> p (n t)").bitcast(I32))
+        def load_words(dst, src, cols):
+            nc.sync.dma_start(dst[:, cols].bitcast(I32), src.rearrange("p n t -> p (n t)").bitcast(I32)[:, cols])
 
         def load_scales(win, src):
             nc.sync.dma_start(win[ROW0:, :].bitcast(I32), src.rearrange("a q n -> (a q) n").bitcast(I32))
@@ -96,69 +94,76 @@ def tile_list_motif_promoter_activity_kernel(
         nc.sync.dma_start(
             ab[:].rearrange("p (b t) -> p b t", b=PASSES), abund.rearrange("(b p t) -> p b t", b=PASSES, t=PACK)
         )
-        for a in range(PASSES):
-            load_words(win1[a], tab_words[a])
-            load_words(win2[a], tab2_words[a])
+        load_words(win1[0], tab_words[0], slice(0, T1))
+        load_words(win2[0], tab2_words[0], slice(0, T2))
+        load_words(win1[1], tab_words[1], slice(0, T1))
+        load_words(win2[1], tab2_words[1], slice(0, T2))
 
         def deal(dst, src, column_bytes):
             per_line = LINE_BYTES // column_bytes
             nc.vector.tensor_copy(
-                dst.rearrange("p (b t x i) -> p b x t i", b=PASSES, t=PACK, i=per_line),
-                src.rearrange("p (b x i t) -> p b x t i", b=PASSES, t=PACK, i=per_line),
+                dst.rearrange("p (b t x i) -> p b x t i", x=P // per_line, t=PACK, i=per_line),
+                src.rearrange("p (b x i t) -> p b x t i", x=P // per_line, t=PACK, i=per_line),
             )
 
         picked_s = held([P, S1], U8, "picked_s")
-        behind_tables = PASSES * 4 * T2
         picked2_s = held([P, S2], U8, "picked2_s", tag="picked0")
-        picked = [held([P, S1], U32, "picked0", tag="picked0"), placed([P, S1], U32, "picked1", behind_tables)]
-        v1 = [held([P, S1], U32, "v1_%d" % a) for a in range(PASSES)]
         nc.vector.tensor_copy(picked_s[:], win1_s[:].indirect(idx1[:]))
         nc.vector.tensor_copy(picked2_s[:], win2_s[:].indirect(idx2[:]))
         deal(planes[0][:, :S1], picked_s[:], 1)
         nc.vector.tensor_copy(planes[0][:, S1:].bitcast(I32), picked2_s[:].bitcast(I32))
-        for q in range(3):
-            to, at = 32 * q + PLANE_ROW[0], ROW0 + 4 * q
-            nc.scalar.dma_start(planes[0][to : to + 4, :].bitcast(I32), planes[0][at : at + 4, :].bitcast(I32))
-        for a in range(PASSES):
-            nc.vector.tensor_copy(picked[a][:], win1[a][:].indirect(idx1[:]))
-            deal(v1[a][:], picked[a][:], 4)
 
-        for r in range(4):
-            nc.scalar.dma_start(
+        def move_row(r):
+            nc.sync.dma_start(
                 planes[1][4 + r : P : 32, :].bitcast(I32), planes[0][ROW0 + ROWS + r : P : 4, :].bitcast(I32)
             )
-        w4_bytes = PASSES * 2 * N
-        w_all = placed([P, PASSES, PACK, N], F32, "w_all", behind_tables + w4_bytes)
-        w_raw = [w_all[:, b, :, :] for b in range(PASSES)]
+
+        for r in range(4):
+            move_row(r)
+        for q in range(3):
+            to, at = 32 * q + PLANE_ROW[0], ROW0 + 4 * q
+            nc.sync.dma_start(planes[0][to : to + 4, :].bitcast(I32), planes[0][at : at + 4, :].bitcast(I32))
+        w_raw = [held([P, PACK, N], F32, "w_raw%d" % b) for b in range(PASSES)]
         for b in range(PASSES):
-            nc.sync.dma_start(w_raw[b], w[b * PASS : (b + 1) * PASS, :].rearrange("(p r) n -> p r n", r=PACK))
-        w4_raw = placed([P, w4_bytes], U8, "w4_raw", behind_tables)
+            nc.sync.dma_start(w_raw[b][:], w[b * PASS : (b + 1) * PASS, :].rearrange("(p r) n -> p r n", r=PACK))
+        w4_raw = held([P, PASSES * 2 * N], U8, "w4_raw")
         nc.sync.dma_start(
             w4_raw[:].bitcast(I32).rearrange("p (b n) -> p b n", b=PASSES),
             w4_words.bitcast(I32).rearrange("b p n -> p b n"),
         )
-
-        v2 = {}
-
-        def gather_genes(a, j0, genes, tile):
-            nc.vector.tensor_copy(tile[:], win2[a][:].indirect(idx2[:, j0 // 16 : (j0 + genes) // 16]))
-            for j in range(0, genes, SHORT):
-                v2[a, j0 + j] = (tile, j)
-
-        gather_genes(0, 0, HALF, placed([P, HALF], U32, "v2_00", last_factors + S1 + S2))
-        j0 = 0
-        for n, piece in enumerate(LAST_PIECES):
-            gather_genes(1, j0, piece, held([P, piece], U32, "v2_1%d" % n))
-            j0 = j0 + piece
-        gather_genes(0, HALF, HALF, placed([P, HALF], U32, "v2_01", 4 * T2))
-
-        w4_s_raw = placed([P, PASSES * N], U8, "w4_s_raw", 0)
+        w4_s_raw = held([P, PASSES * N], U8, "w4_s_raw")
         nc.vector.memset(w4_s_raw[:].bitcast(I32), 0)
         for q in range(4):
             nc.sync.dma_start(
                 w4_s_raw[32 * q : 32 * q + 4, :].bitcast(I32).rearrange("r (b n) -> r b n", b=PASSES),
                 w4_scales[:, 4 * q : 4 * q + 4, :].bitcast(I32).rearrange("b r n -> r b n"),
             )
+
+        v1, v2 = {}, {}
+
+        def gather_factors(a, b0, runs, picked):
+            entries = runs * PASS
+            nc.vector.tensor_copy(
+                picked[:], win1[a][:].indirect(idx1[:, b0 * PASS // 16 : (b0 * PASS + entries) // 16])
+            )
+            dealt = held([P, entries], U32, "v1_%d%d" % (a, b0))
+            deal(dealt[:], picked[:], 4)
+            for b in range(runs):
+                v1[a, b0 + b] = (dealt, b * PASS)
+
+        def gather_genes(a, j0, genes, tile):
+            nc.vector.tensor_copy(tile[:], win2[a][:].indirect(idx2[:, j0 // 16 : (j0 + genes) // 16]))
+            for j in range(0, genes, SHORT):
+                v2[a, j0 + j] = (tile, j)
+
+        gather_factors(0, 0, PASSES, held([P, S1], U32, "picked0", tag="picked0"))
+        gather_genes(0, 0, HALF, held([P, HALF], U32, "v2_00"))
+        gather_factors(1, 0, PASSES, held([P, S1], U32, "picked1"))
+        j0 = 0
+        for n, piece in enumerate(LAST_PIECES):
+            gather_genes(1, j0, piece, held([P, piece], U32, "v2_1%d" % n))
+            j0 = j0 + piece
+        gather_genes(0, HALF, HALF, placed([P, HALF], U32, "v2_01", 4 * T2))
 
         wq = [held([P, N], U32, "wq%d" % b) for b in range(PASSES)]
         wq_s = [held([P, N], U8, "wq_s%d" % b) for b in range(PASSES)]
@@ -168,7 +173,7 @@ def tile_list_motif_promoter_activity_kernel(
             w_bf[b] = placed([P, N * PACK], BF16, "w_bf%d" % b, 2 * N * PACK * (b + 1))
             nc.vector.tensor_copy(
                 w_bf[b][:].rearrange("p (t m r) -> p m r t", t=PACK, r=PACK),
-                w_raw[b].rearrange("p r (m t) -> p m r t", t=PACK),
+                w_raw[b][:].rearrange("p r (m t) -> p m r t", t=PACK),
             )
 
         def deal_w4():
@@ -195,24 +200,24 @@ def tile_list_motif_promoter_activity_kernel(
         def affinity(g, u, a):
             b, j0, jc = GROUPS[g]
             per_bank = BANK // jc
-            if a == 0:
+            opens = (g, u) not in aff
+            if opens:
                 aff[g, u] = psum.tile([P, BANK], F32, name="aff", bufs=AFF_BANKS)
             for e in range(per_bank):
                 m0 = b * PASS + (per_bank * u + e) * P
                 nc.tensor.matmul_mx(
                     out=aff[g, u][:, e * jc : (e + 1) * jc],
-                    lhsT=v1[a][:, m0 : m0 + P].bitcast(FP8X4),
+                    lhsT=v1[a, b][0][:, m0 : m0 + P].bitcast(FP8X4),
                     lhsT_scale=planes[a][PLANE_ROW[a] :, m0 : m0 + P],
                     rhs=v2[a, j0][0][:, v2[a, j0][1] : v2[a, j0][1] + jc].bitcast(FP8X4),
                     rhs_scale=planes[a][PLANE_ROW[a] :, S1 + j0 : S1 + j0 + jc],
-                    start=(a == 0 and e == 0),
-                    stop=(a == PASSES - 1 and e == per_bank - 1),
+                    start=(opens and e == 0),
+                    stop=(not opens and e == per_bank - 1),
                 )
 
         def square(g, u):
-            if (g, u) not in aff:
-                affinity(g, u, 0)
-            affinity(g, u, 1)
+            for a in (1, 0) if (g, u) == (0, 0) else (0, 1):
+                affinity(g, u, a)
             if u == 0:
                 sq[g] = held([P, PACK * width(g)], F32, "sq_%d" % g, tag="sq_%d" % g)
             nc.scalar.activation(sq[g][:, u * BANK : (u + 1) * BANK], aff[g, u][:], ACT.Square)
@@ -330,8 +335,6 @@ def tile_list_motif_promoter_activity_kernel(
                 if codes_at[c] == step:
                     quantise_out(c)
 
-        for bank in range(banks(width(0))):
-            affinity(*divmod(bank, banks(width(0))), 0)
         for u in range(banks(width(0))):
             square(0, u)
         for g in range(groups):

@@ -64,6 +64,14 @@ def tile_list_motif_promoter_activity_kernel(
         def sliced(src, run):
             return src[:].rearrange("p (t x i) -> p x t i", i=run, t=PACK)
 
+        def woven_genes(dst, j0, run):
+            return dst[:, PACK * j0 : PACK * (j0 + run)].rearrange("p (x i t) -> p x t i", i=LINE, t=PACK)
+
+        def sliced_genes(src, j0, run):
+            return src[:].rearrange("p (t j) -> p t j", t=PACK)[:, :, j0 : j0 + run].rearrange(
+                "p t (x i) -> p x t i", i=LINE
+            )
+
         win1_s = held([P, T1], U8, "win1_s", tag="win1_s")
         win2_s = held([P, T2], U8, "win2_s", tag="win2_s")
         nc.vector.memset(win1_s[:ROW0, :].bitcast(I32), 0)
@@ -94,6 +102,11 @@ def tile_list_motif_promoter_activity_kernel(
         nc.sync.dma_start(
             ab[:].rearrange("p (b t) -> p b t", b=PASSES), abund.rearrange("(b p t) -> p b t", b=PASSES, t=PACK)
         )
+        ab_second = {}
+        for g in range(1, len(GROUPS)):
+            ab_second[g] = held([P, 1], F32, "ab_%d" % g, tag="codes_%d" % (g - 1))
+            column = PACK * GROUPS[g][0] + 1
+            nc.scalar.copy(ab_second[g][:], ab[:, column : column + 1])
         load_words(win1[0], tab_words[0], slice(0, T1))
         load_words(win2[0], tab2_words[0], slice(0, T2))
         load_words(win1[1], tab_words[1], slice(0, T1))
@@ -107,7 +120,7 @@ def tile_list_motif_promoter_activity_kernel(
             )
 
         picked_s = held([P, S1], U8, "picked_s")
-        picked2_s = held([P, S2], U8, "picked2_s", tag="picked0")
+        picked2_s = held([P, S2], U8, "picked2_s")
         nc.vector.tensor_copy(picked_s[:], win1_s[:].indirect(idx1[:]))
         nc.vector.tensor_copy(picked2_s[:], win2_s[:].indirect(idx2[:]))
         deal(planes[0][:, :S1], picked_s[:], 1)
@@ -123,7 +136,7 @@ def tile_list_motif_promoter_activity_kernel(
         for q in range(3):
             to, at = 32 * q + PLANE_ROW[0], ROW0 + 4 * q
             nc.sync.dma_start(planes[0][to : to + 4, :].bitcast(I32), planes[0][at : at + 4, :].bitcast(I32))
-        w_raw = [held([P, PACK, N], F32, "w_raw%d" % b) for b in range(PASSES)]
+        w_raw = [held([P, PACK, N], F32, "w_raw%d" % b, tag="w_raw%d" % b) for b in range(PASSES)]
         for b in range(PASSES):
             nc.sync.dma_start(w_raw[b][:], w[b * PASS : (b + 1) * PASS, :].rearrange("(p r) n -> p r n", r=PACK))
         w4_raw = held([P, PASSES * 2 * N], U8, "w4_raw")
@@ -141,24 +154,24 @@ def tile_list_motif_promoter_activity_kernel(
 
         v1, v2 = {}, {}
 
-        def gather_factors(a, b0, runs, picked):
-            entries = runs * PASS
-            nc.vector.tensor_copy(
-                picked[:], win1[a][:].indirect(idx1[:, b0 * PASS // 16 : (b0 * PASS + entries) // 16])
-            )
-            dealt = held([P, entries], U32, "v1_%d%d" % (a, b0))
-            deal(dealt[:], picked[:], 4)
-            for b in range(runs):
-                v1[a, b0 + b] = (dealt, b * PASS)
+        def gather_factors(a):
+            picked = [held([P, PASS], U32, "picked%d%d" % (a, b), tag="picked%d%d" % (a, b)) for b in range(PASSES)]
+            for b in range(PASSES):
+                nc.vector.tensor_copy(
+                    picked[b][:], win1[a][:].indirect(idx1[:, b * PASS // 16 : (b + 1) * PASS // 16])
+                )
+            for b in range(PASSES):
+                v1[a, b] = held([P, PASS], U32, "v1_%d%d" % (a, b))
+                deal(v1[a, b][:], picked[b][:], 4)
 
         def gather_genes(a, j0, genes, tile):
             nc.vector.tensor_copy(tile[:], win2[a][:].indirect(idx2[:, j0 // 16 : (j0 + genes) // 16]))
             for j in range(0, genes, SHORT):
                 v2[a, j0 + j] = (tile, j)
 
-        gather_factors(0, 0, PASSES, held([P, S1], U32, "picked0", tag="picked0"))
+        gather_factors(0)
         gather_genes(0, 0, HALF, held([P, HALF], U32, "v2_00"))
-        gather_factors(1, 0, PASSES, held([P, S1], U32, "picked1"))
+        gather_factors(1)
         j0 = 0
         for n, piece in enumerate(LAST_PIECES):
             gather_genes(1, j0, piece, held([P, piece], U32, "v2_1%d" % n))
@@ -170,22 +183,28 @@ def tile_list_motif_promoter_activity_kernel(
         w_bf = {}
 
         def cast_w(b):
-            w_bf[b] = placed([P, N * PACK], BF16, "w_bf%d" % b, 2 * N * PACK * (b + 1))
-            nc.vector.tensor_copy(
-                w_bf[b][:].rearrange("p (t m r) -> p m r t", t=PACK, r=PACK),
-                w_raw[b][:].rearrange("p r (m t) -> p m r t", t=PACK),
-            )
+            w_bf[b] = held([P, N * PACK], BF16, "w_bf%d" % b, tag="win1_%d" % b)
+            for t0 in range(0, PACK, 2):
+                nc.vector.tensor_copy(
+                    w_bf[b][:].rearrange("p (t m r) -> p m r t", t=PACK, r=PACK)[:, :, :, t0 : t0 + 2],
+                    w_raw[b][:].rearrange("p r (m t) -> p m r t", t=PACK)[:, :, :, t0 : t0 + 2],
+                )
 
         def deal_w4():
-            w4 = held([P, PASSES * 2 * N], U8, "w4", tag="win1_0")
-            w4_s = held([P, PASSES * N], U8, "w4_s", tag="picked0")
+            w4 = held([P, PASSES * 2 * N], U8, "w4", tag="picked01")
+            w4_s = held([P, PASSES * N], U8, "w4_s", tag="picked00")
             deal(w4[:].bitcast(U16), w4_raw[:].bitcast(U16), 2)
             deal(w4_s[:], w4_s_raw[:], 1)
             return w4, w4_s
 
         def quantise_w():
             for b in range(PASSES):
-                nc.vector.quantize_mx(out=wq[b][:].bitcast(FP8X4), scales=wq_s[b][:], in_=w_bf[b][:])
+                for n0 in range(0, N, N // 2):
+                    nc.vector.quantize_mx(
+                        out=wq[b][:, n0 : n0 + N // 2].bitcast(FP8X4),
+                        scales=wq_s[b][:, n0 : n0 + N // 2],
+                        in_=w_bf[b][:, PACK * n0 : PACK * (n0 + N // 2)],
+                    )
 
         starts = [sum(CHUNKS[:c]) for c in range(len(CHUNKS))]
         groups = len(GROUPS)
@@ -207,7 +226,7 @@ def tile_list_motif_promoter_activity_kernel(
                 m0 = b * PASS + (per_bank * u + e) * P
                 nc.tensor.matmul_mx(
                     out=aff[g, u][:, e * jc : (e + 1) * jc],
-                    lhsT=v1[a, b][0][:, m0 : m0 + P].bitcast(FP8X4),
+                    lhsT=v1[a, b][:, m0 - b * PASS : m0 - b * PASS + P].bitcast(FP8X4),
                     lhsT_scale=planes[a][PLANE_ROW[a] :, m0 : m0 + P],
                     rhs=v2[a, j0][0][:, v2[a, j0][1] : v2[a, j0][1] + jc].bitcast(FP8X4),
                     rhs_scale=planes[a][PLANE_ROW[a] :, S1 + j0 : S1 + j0 + jc],
@@ -230,11 +249,14 @@ def tile_list_motif_promoter_activity_kernel(
                     rs[g][:, c0 : c0 + step], sq[g][:, c0 : c0 + step], ACT.Abs_reciprocal_sqrt, bias=unit
                 )
 
-        def weigh(g):
-            b, j0, jc = GROUPS[g]
-            partial[g] = work.tile([P, PACK * jc], F32, name="partial", bufs=AHEAD)
+        def square_root(g):
+            partial[g] = work.tile([P, PACK * width(g)], F32, name="partial", bufs=AHEAD)
             if g >= SQUARED_FROM:
                 nc.scalar.activation(partial[g][:], rs[g][:], ACT.Square)
+
+        def weigh(g):
+            b, j0, jc = GROUPS[g]
+            if g >= SQUARED_FROM:
                 hb[g] = work.tile([P, PACK * jc], BF16, name="hb")
                 dst, factor = hb[g], partial[g]
             else:
@@ -242,6 +264,8 @@ def tile_list_motif_promoter_activity_kernel(
             for t in range(PACK):
                 cols = slice(t * jc, (t + 1) * jc)
                 abundance = ab[:, PACK * b + t : PACK * b + t + 1]
+                if t == 1 and g in ab_second:
+                    abundance = ab_second[g][:]
                 nc.vector.scalar_tensor_tensor(
                     dst[:, cols], sq[g][:, cols], abundance, factor[:, cols], ALU.mult, ALU.mult
                 )
@@ -249,15 +273,22 @@ def tile_list_motif_promoter_activity_kernel(
         def weave_h(g):
             hi[g] = work.tile([P, PACK * width(g)], BF16, name="hi", align_bytes=64)
             if g >= SQUARED_FROM:
-                nc.vector.tensor_copy(woven(hi[g], LINE), sliced(hb[g], LINE))
+                run = width(g) if g + 1 < groups else width(g) // 2
+                for j0 in range(0, width(g), run):
+                    nc.vector.tensor_copy(woven_genes(hi[g], j0, run), sliced_genes(hb[g], j0, run))
             else:
                 nc.vector.tensor_tensor(woven(hi[g], PAIR), sliced(partial[g], PAIR), sliced(rs[g], PAIR), ALU.mult)
 
         def quantise_h(g):
-            hold = g + 1 < groups and width(g + 1) == WIDE
-            hq[g] = held([P, width(g)], U32, "hq_%d" % g, tag="sq_%d" % (g + 1) if hold else "")
+            hq[g] = held([P, width(g)], U32, "hq_%d" % g, tag="codes_%d" % g)
             hq_s[g] = work.tile([P, width(g)], U8, name="hq_s", bufs=AHEAD + 1, align_bytes=64)
-            nc.vector.quantize_mx(out=hq[g][:].bitcast(FP8X4), scales=hq_s[g][:], in_=hi[g][:])
+            run = width(g) if g + 1 < groups else width(g) // 2
+            for j0 in range(0, width(g), run):
+                nc.vector.quantize_mx(
+                    out=hq[g][:, j0 : j0 + run].bitcast(FP8X4),
+                    scales=hq_s[g][:, j0 : j0 + run],
+                    in_=hi[g][:, PACK * j0 : PACK * (j0 + run)],
+                )
 
         def group_of(b, j):
             return [g for g, (gb, j0, jc) in enumerate(GROUPS) if gb == b and j0 <= j < j0 + jc][0]
@@ -270,7 +301,7 @@ def tile_list_motif_promoter_activity_kernel(
         def pathways(c, w4, w4_s):
             jc = CHUNKS[c]
             per_bank = BANK // jc
-            y = ys[c] = held([P, PACK * jc], F32, "y_%d" % c)
+            y = ys[c] = held([P, PACK * jc], F32, "y_%d" % c, tag="w_raw%d" % c if c < PASSES else "")
             first = work.tile([P, PACK * jc], F32, name="first", bufs=2)
             for u in range(banks(jc)):
                 if jc == WIDE:
@@ -305,11 +336,15 @@ def tile_list_motif_promoter_activity_kernel(
                                 start=(b == 0 and e == 0 and j0 == 0),
                                 stop=(b == PASSES - 1 and e == per_bank - 1 and j0 == jc - P),
                             )
-                step = BANK // 2 if c + 1 == len(CHUNKS) else BANK
-                for c0 in range(0, BANK, step):
-                    part = slice(u * BANK + c0, u * BANK + c0 + step)
-                    nc.scalar.copy(first[:, part], p1[:, c0 : c0 + step])
-                    nc.vector.tensor_tensor(y[:, part], p2[:, c0 : c0 + step], first[:, part], ALU.mult)
+                cols = slice(u * BANK, (u + 1) * BANK)
+                run = jc // 2 if c + 1 == len(CHUNKS) else jc
+                for j0 in range(0, jc, run):
+                    views = [
+                        ap.rearrange("p (e j) -> p e j", e=per_bank)[:, :, j0 : j0 + run]
+                        for ap in (y[:, cols], p1[:], p2[:], first[:, cols])
+                    ]
+                    nc.scalar.copy(views[3], views[1])
+                    nc.vector.tensor_tensor(views[0], views[2], views[3], ALU.mult)
             genes = slice(starts[c], starts[c] + jc)
             nc.sync.dma_start(out_rows[:, :, genes], y[:].rearrange("p (t j) -> p t j", t=PACK))
 
@@ -319,9 +354,16 @@ def tile_list_motif_promoter_activity_kernel(
             genes = slice(starts[c], starts[c] + jc)
             yi = held([P, PACK * jc], BF16, "yi_%d" % c)
             copy = nc.scalar.copy if c + 1 < len(CHUNKS) else nc.vector.tensor_copy
-            copy(woven(yi, LINE), sliced(y, LINE))
             yq = held([P, jc], U32, "yq_%d" % c)
-            nc.vector.quantize_mx(out=yq[:].bitcast(FP8X4), scales=y_s[:, genes], in_=yi[:])
+            run = jc if c + 1 < len(CHUNKS) else jc // 2
+            for j0 in range(0, jc, run):
+                copy(woven_genes(yi, j0, run), sliced_genes(y, j0, run))
+            for j0 in range(0, jc, run):
+                nc.vector.quantize_mx(
+                    out=yq[:, j0 : j0 + run].bitcast(FP8X4),
+                    scales=y_s[:, starts[c] + j0 : starts[c] + j0 + run],
+                    in_=yi[:, PACK * j0 : PACK * (j0 + run)],
+                )
             nc.sync.dma_start(out_words[:, genes], yq[:].bitcast(I32))
 
         last_group = [group_of(PASSES - 1, j0) for j0 in starts]
@@ -337,13 +379,18 @@ def tile_list_motif_promoter_activity_kernel(
 
         for u in range(banks(width(0))):
             square(0, u)
+        ahead = [(g, u) for g in range(1, groups) for u in range(banks(width(g)))]
         for g in range(groups):
-            if g + 1 < groups:
-                square(g + 1, 0)
-            root(g)
-            if g + 1 < groups:
-                for u in range(1, banks(width(g + 1))):
-                    square(g + 1, u)
+            if 2 * g < len(ahead):
+                square(*ahead[2 * g])
+                root(g)
+                square(*ahead[2 * g + 1])
+                square_root(g)
+            elif g + 1 < groups:
+                root(g)
+                root(g + 1)
+                square_root(g)
+                square_root(g + 1)
             weigh(g)
             if g >= 1:
                 quantise_h(g - 1)

@@ -26,6 +26,7 @@ LINE = 4
 PAIR = 2
 LINE_BYTES = 16
 ROWS = 16
+QUADRANT = 32
 ROW0 = P - PASSES * ROWS
 PLANE_ROW = (12, 4)
 LAST_PIECES = (256, 256, 512)
@@ -72,7 +73,7 @@ def tile_list_motif_promoter_activity_kernel(
                 "p t (x i) -> p x t i", i=LINE
             )
 
-        win1_s = held([P, T1], U8, "win1_s", tag="win1_s")
+        win1_s = held([P, T1], U8, "win1_s")
         win2_s = held([P, T2], U8, "win2_s", tag="win2_s")
         nc.vector.memset(win1_s[:ROW0, :].bitcast(I32), 0)
         nc.vector.memset(win2_s[:ROW0, :].bitcast(I32), 0)
@@ -88,8 +89,8 @@ def tile_list_motif_promoter_activity_kernel(
         win2 = [placed([P, T2], U32, "win2_%d" % a, 4 * T2 * a) for a in range(PASSES)]
         planes = [held([P, S1 + S2], U8, "plane%d" % a, tag="win2_s" if a else "") for a in range(PASSES)]
 
-        def load_words(dst, src, cols):
-            nc.sync.dma_start(dst[:, cols].bitcast(I32), src.rearrange("p n t -> p (n t)").bitcast(I32)[:, cols])
+        def load_words(dst, src):
+            nc.sync.dma_start(dst[:].bitcast(I32), src.rearrange("p n t -> p (n t)").bitcast(I32))
 
         def load_scales(win, src):
             nc.sync.dma_start(win[ROW0:, :].bitcast(I32), src.rearrange("a q n -> (a q) n").bitcast(I32))
@@ -107,10 +108,9 @@ def tile_list_motif_promoter_activity_kernel(
             ab_second[g] = held([P, 1], F32, "ab_%d" % g, tag="codes_%d" % (g - 1))
             column = PACK * GROUPS[g][0] + 1
             nc.scalar.copy(ab_second[g][:], ab[:, column : column + 1])
-        load_words(win1[0], tab_words[0], slice(0, T1))
-        load_words(win2[0], tab2_words[0], slice(0, T2))
-        load_words(win1[1], tab_words[1], slice(0, T1))
-        load_words(win2[1], tab2_words[1], slice(0, T2))
+        for a in range(PASSES):
+            load_words(win1[a], tab_words[a])
+            load_words(win2[a], tab2_words[a])
 
         def deal(dst, src, column_bytes):
             per_line = LINE_BYTES // column_bytes
@@ -125,16 +125,13 @@ def tile_list_motif_promoter_activity_kernel(
         nc.vector.tensor_copy(picked2_s[:], win2_s[:].indirect(idx2[:]))
         deal(planes[0][:, :S1], picked_s[:], 1)
         nc.vector.tensor_copy(planes[0][:, S1:].bitcast(I32), picked2_s[:].bitcast(I32))
-
-        def move_row(r):
-            nc.sync.dma_start(
-                planes[1][4 + r : P : 32, :].bitcast(I32), planes[0][ROW0 + ROWS + r : P : 4, :].bitcast(I32)
-            )
-
         for r in range(4):
-            move_row(r)
+            nc.sync.dma_start(
+                planes[1][PLANE_ROW[1] + r : P : QUADRANT, :].bitcast(I32),
+                planes[0][ROW0 + ROWS + r : P : 4, :].bitcast(I32),
+            )
         for q in range(3):
-            to, at = 32 * q + PLANE_ROW[0], ROW0 + 4 * q
+            to, at = QUADRANT * q + PLANE_ROW[0], ROW0 + 4 * q
             nc.sync.dma_start(planes[0][to : to + 4, :].bitcast(I32), planes[0][at : at + 4, :].bitcast(I32))
         w_raw = [held([P, PACK, N], F32, "w_raw%d" % b, tag="w_raw%d" % b) for b in range(PASSES)]
         for b in range(PASSES):
@@ -148,7 +145,7 @@ def tile_list_motif_promoter_activity_kernel(
         nc.vector.memset(w4_s_raw[:].bitcast(I32), 0)
         for q in range(4):
             nc.sync.dma_start(
-                w4_s_raw[32 * q : 32 * q + 4, :].bitcast(I32).rearrange("r (b n) -> r b n", b=PASSES),
+                w4_s_raw[QUADRANT * q : QUADRANT * q + 4, :].bitcast(I32).rearrange("r (b n) -> r b n", b=PASSES),
                 w4_scales[:, 4 * q : 4 * q + 4, :].bitcast(I32).rearrange("b r n -> r b n"),
             )
 
@@ -208,6 +205,7 @@ def tile_list_motif_promoter_activity_kernel(
 
         starts = [sum(CHUNKS[:c]) for c in range(len(CHUNKS))]
         groups = len(GROUPS)
+        hi_pooled = {}
         aff, sq, rs, partial, hb, hi, hq, hq_s = {}, {}, {}, {}, {}, {}, {}, {}
 
         def width(g):
@@ -219,16 +217,17 @@ def tile_list_motif_promoter_activity_kernel(
         def affinity(g, u, a):
             b, j0, jc = GROUPS[g]
             per_bank = BANK // jc
+            genes, at = v2[a, j0]
             opens = (g, u) not in aff
             if opens:
                 aff[g, u] = psum.tile([P, BANK], F32, name="aff", bufs=AFF_BANKS)
             for e in range(per_bank):
-                m0 = b * PASS + (per_bank * u + e) * P
+                m0 = (per_bank * u + e) * P
                 nc.tensor.matmul_mx(
                     out=aff[g, u][:, e * jc : (e + 1) * jc],
-                    lhsT=v1[a, b][:, m0 - b * PASS : m0 - b * PASS + P].bitcast(FP8X4),
-                    lhsT_scale=planes[a][PLANE_ROW[a] :, m0 : m0 + P],
-                    rhs=v2[a, j0][0][:, v2[a, j0][1] : v2[a, j0][1] + jc].bitcast(FP8X4),
+                    lhsT=v1[a, b][:, m0 : m0 + P].bitcast(FP8X4),
+                    lhsT_scale=planes[a][PLANE_ROW[a] :, b * PASS + m0 : b * PASS + m0 + P],
+                    rhs=genes[:, at : at + jc].bitcast(FP8X4),
                     rhs_scale=planes[a][PLANE_ROW[a] :, S1 + j0 : S1 + j0 + jc],
                     start=(opens and e == 0),
                     stop=(not opens and e == per_bank - 1),
@@ -270,9 +269,30 @@ def tile_list_motif_promoter_activity_kernel(
                     dst[:, cols], sq[g][:, cols], abundance, factor[:, cols], ALU.mult, ALU.mult
                 )
 
+        def pooled_genes(g):
+            return width(g) // 2 if g in pathways_at and g >= SQUARED_FROM and width(g) == WIDE else 0
+
+        def weave_pooled(g):
+            n = pooled_genes(g)
+            hi_pooled[g] = held([P, PACK * n], BF16, "hi_pooled_%d" % g, tag="hi_%d" % (g - 1))
+            nc.gpsimd.tensor_scalar(
+                hi_pooled[g][:].rearrange("p (j t) -> p j t", t=PACK),
+                hb[g][:].rearrange("p (t j) -> p j t", t=PACK)[:, width(g) - n :, :],
+                1.0,
+                -0.0,
+                ALU.mult,
+                ALU.add,
+            )
+
         def weave_h(g):
-            hi[g] = work.tile([P, PACK * width(g)], BF16, name="hi", align_bytes=64)
-            if g >= SQUARED_FROM:
+            if g + 1 < groups and pooled_genes(g + 1):
+                hi[g] = held([P, PACK * width(g)], BF16, "hi_%d" % g, tag="hi_%d" % g)
+            else:
+                hi[g] = work.tile([P, PACK * width(g)], BF16, name="hi", align_bytes=64, bufs=2)
+            if pooled_genes(g):
+                n = width(g) - pooled_genes(g)
+                nc.vector.tensor_copy(woven_genes(hi[g], 0, n), sliced_genes(hb[g], 0, n))
+            elif g >= SQUARED_FROM:
                 run = width(g) if g + 1 < groups else width(g) // 2
                 for j0 in range(0, width(g), run):
                     nc.vector.tensor_copy(woven_genes(hi[g], j0, run), sliced_genes(hb[g], j0, run))
@@ -282,12 +302,11 @@ def tile_list_motif_promoter_activity_kernel(
         def quantise_h(g):
             hq[g] = held([P, width(g)], U32, "hq_%d" % g, tag="codes_%d" % g)
             hq_s[g] = work.tile([P, width(g)], U8, name="hq_s", bufs=AHEAD + 1, align_bytes=64)
-            run = width(g) if g + 1 < groups else width(g) // 2
+            run = width(g) if g + 1 < groups and not pooled_genes(g) else width(g) // 2
             for j0 in range(0, width(g), run):
+                source = hi_pooled[g][:] if j0 and pooled_genes(g) else hi[g][:, PACK * j0 : PACK * (j0 + run)]
                 nc.vector.quantize_mx(
-                    out=hq[g][:, j0 : j0 + run].bitcast(FP8X4),
-                    scales=hq_s[g][:, j0 : j0 + run],
-                    in_=hi[g][:, PACK * j0 : PACK * (j0 + run)],
+                    out=hq[g][:, j0 : j0 + run].bitcast(FP8X4), scales=hq_s[g][:, j0 : j0 + run], in_=source
                 )
 
         def group_of(b, j):
@@ -301,7 +320,7 @@ def tile_list_motif_promoter_activity_kernel(
         def pathways(c, w4, w4_s):
             jc = CHUNKS[c]
             per_bank = BANK // jc
-            y = ys[c] = held([P, PACK * jc], F32, "y_%d" % c, tag="w_raw%d" % c if c < PASSES else "")
+            y = ys[c] = held([P, PACK * jc], F32, "y_%d" % c, tag="sq_%d" % pathways_at[c] if c < PASSES else "")
             first = work.tile([P, PACK * jc], F32, name="first", bufs=2)
             for u in range(banks(jc)):
                 if jc == WIDE:
@@ -339,12 +358,12 @@ def tile_list_motif_promoter_activity_kernel(
                 cols = slice(u * BANK, (u + 1) * BANK)
                 run = jc // 2 if c + 1 == len(CHUNKS) else jc
                 for j0 in range(0, jc, run):
-                    views = [
+                    y_run, p1_run, p2_run, first_run = [
                         ap.rearrange("p (e j) -> p e j", e=per_bank)[:, :, j0 : j0 + run]
                         for ap in (y[:, cols], p1[:], p2[:], first[:, cols])
                     ]
-                    nc.scalar.copy(views[3], views[1])
-                    nc.vector.tensor_tensor(views[0], views[2], views[3], ALU.mult)
+                    nc.scalar.copy(first_run, p1_run)
+                    nc.vector.tensor_tensor(y_run, p2_run, first_run, ALU.mult)
             genes = slice(starts[c], starts[c] + jc)
             nc.sync.dma_start(out_rows[:, :, genes], y[:].rearrange("p (t j) -> p t j", t=PACK))
 
@@ -392,9 +411,14 @@ def tile_list_motif_promoter_activity_kernel(
                 square_root(g)
                 square_root(g + 1)
             weigh(g)
-            if g >= 1:
+            if pooled_genes(g):
+                weave_h(g)
                 quantise_h(g - 1)
-            weave_h(g)
+                weave_pooled(g)
+            else:
+                if g >= 1:
+                    quantise_h(g - 1)
+                weave_h(g)
             if g == PASSES - 1:
                 cast_w(0)
             if g == PASSES:
@@ -408,4 +432,4 @@ def tile_list_motif_promoter_activity_kernel(
             finish(step, w4, w4_s)
         for q in range(4):
             queue = nc.scalar if q % 2 else nc.sync
-            queue.dma_start(out_2[0, 4 * q : 4 * q + 4, :].bitcast(I32), y_s[32 * q : 32 * q + 4, :].bitcast(I32))
+            queue.dma_start(out_2[0, 4 * q : 4 * q + 4, :].bitcast(I32), y_s[QUADRANT * q : QUADRANT * q + 4, :].bitcast(I32))

@@ -20,7 +20,7 @@ P = 128
 PACK = 4
 PASS = P * PACK
 PASSES = 2
-HALF = 512
+HALF = 1024
 BANK = 512
 LINE = 4
 PAIR = 2
@@ -30,6 +30,7 @@ QUADRANT = 32
 ROW0 = P - PASSES * ROWS
 PLANE_ROW = (12, 4)
 LAST_PIECES = (256, 256, 512)
+W_PIECES = ((0, 0, N // 2), (0, N // 2, N), (1, 0, N))
 WIDE, SHORT = 256, 128
 CHUNKS = (WIDE, WIDE, WIDE, SHORT, SHORT)
 GROUPS = tuple((b, j0, WIDE) for j0 in range(0, S2, WIDE) for b in range(PASSES))[:-1] + (
@@ -38,7 +39,7 @@ GROUPS = tuple((b, j0, WIDE) for j0 in range(0, S2, WIDE) for b in range(PASSES)
 )
 AHEAD = 4
 AFF_BANKS = 4
-SQUARED_FROM = 4
+SQUARED = (4, 6, 7, 8)
 LAG_TWO_PRODUCTS, LAG_SQUARED = 3, 2
 
 
@@ -77,12 +78,6 @@ def tile_list_motif_promoter_activity_kernel(
         win2_s = held([P, T2], U8, "win2_s", tag="win2_s")
         nc.vector.memset(win1_s[:ROW0, :].bitcast(I32), 0)
         nc.vector.memset(win2_s[:ROW0, :].bitcast(I32), 0)
-        one = held([P, 1], F32, "one")
-        nc.gpsimd.memset(one[:], 1.0)
-        unit_row = held([P, 1], F32, "unit_row")
-        nc.scalar.activation(unit_row[:], one[:], ACT.Abs_reciprocal_sqrt)
-        unit = unit_row[:, 0:1]
-
         idx1 = keep.tile([P, S1 // 16], U16, name="idx1")
         idx2 = keep.tile([P, S2 // 16], U16, name="idx2")
         win1 = [held([P, T1], U32, "win1_%d" % a, tag="win1_%d" % a) for a in range(PASSES)]
@@ -93,31 +88,45 @@ def tile_list_motif_promoter_activity_kernel(
             nc.sync.dma_start(dst[:].bitcast(I32), src.rearrange("p n t -> p (n t)").bitcast(I32))
 
         def load_scales(win, src):
-            nc.sync.dma_start(win[ROW0:, :].bitcast(I32), src.rearrange("a q n -> (a q) n").bitcast(I32))
+            nc.scalar.dma_start(win[ROW0:, :].bitcast(I32), src.rearrange("a q n -> (a q) n").bitcast(I32))
 
         nc.sync.dma_start(idx1[:], offs)
         load_scales(win1_s, tab_scales)
         nc.sync.dma_start(idx2[:], offs2)
         load_scales(win2_s, tab2_scales)
         ab = held([P, PASSES * PACK], F32, "ab")
-        nc.sync.dma_start(
+        nc.scalar.dma_start(
             ab[:].rearrange("p (b t) -> p b t", b=PASSES), abund.rearrange("(b p t) -> p b t", b=PASSES, t=PACK)
         )
+        one = held([P, 1], F32, "one")
+        nc.gpsimd.memset(one[:], 1.0)
+        unit_row = held([P, 1], F32, "unit_row")
+        nc.scalar.activation(unit_row[:], one[:], ACT.Abs_reciprocal_sqrt)
+        unit = unit_row[:, 0:1]
         ab_second = {}
         for g in range(1, len(GROUPS)):
             ab_second[g] = held([P, 1], F32, "ab_%d" % g, tag="codes_%d" % (g - 1))
             column = PACK * GROUPS[g][0] + 1
             nc.scalar.copy(ab_second[g][:], ab[:, column : column + 1])
+        w4_raw = held([P, PASSES * 2 * N], U8, "w4_raw")
         for a in range(PASSES):
             load_words(win1[a], tab_words[a])
+            if a + 1 == PASSES:
+                nc.sync.dma_start(
+                    w4_raw[:].bitcast(I32).rearrange("p (b n) -> p b n", b=PASSES),
+                    w4_words.bitcast(I32).rearrange("b p n -> p b n"),
+                )
             load_words(win2[a], tab2_words[a])
 
-        def deal(dst, src, column_bytes):
+        def deal(dst, src, column_bytes, copy=nc.vector.tensor_copy):
             per_line = LINE_BYTES // column_bytes
-            nc.vector.tensor_copy(
+            copy(
                 dst.rearrange("p (b t x i) -> p b x t i", x=P // per_line, t=PACK, i=per_line),
                 src.rearrange("p (b x i t) -> p b x t i", x=P // per_line, t=PACK, i=per_line),
             )
+
+        w4 = held([P, PASSES * 2 * N], U8, "w4")
+        deal(w4[:].bitcast(U16), w4_raw[:].bitcast(U16), 2, nc.scalar.copy)
 
         picked_s = held([P, S1], U8, "picked_s")
         picked2_s = held([P, S2], U8, "picked2_s")
@@ -133,14 +142,12 @@ def tile_list_motif_promoter_activity_kernel(
         for q in range(3):
             to, at = QUADRANT * q + PLANE_ROW[0], ROW0 + 4 * q
             nc.sync.dma_start(planes[0][to : to + 4, :].bitcast(I32), planes[0][at : at + 4, :].bitcast(I32))
-        w_raw = [held([P, PACK, N], F32, "w_raw%d" % b, tag="w_raw%d" % b) for b in range(PASSES)]
-        for b in range(PASSES):
-            nc.sync.dma_start(w_raw[b][:], w[b * PASS : (b + 1) * PASS, :].rearrange("(p r) n -> p r n", r=PACK))
-        w4_raw = held([P, PASSES * 2 * N], U8, "w4_raw")
-        nc.sync.dma_start(
-            w4_raw[:].bitcast(I32).rearrange("p (b n) -> p b n", b=PASSES),
-            w4_words.bitcast(I32).rearrange("b p n -> p b n"),
-        )
+        w_raw = {}
+        for b, n0, n1 in W_PIECES:
+            w_raw[b, n0] = held([P, PACK, n1 - n0], F32, "w_raw%d_%d" % (b, n0), tag="w_raw%d_%d" % (b, n0))
+            nc.sync.dma_start(
+                w_raw[b, n0][:], w[b * PASS : (b + 1) * PASS, n0:n1].rearrange("(p r) n -> p r n", r=PACK)
+            )
         w4_s_raw = held([P, PASSES * N], U8, "w4_s_raw")
         nc.vector.memset(w4_s_raw[:].bitcast(I32), 0)
         for q in range(4):
@@ -173,7 +180,6 @@ def tile_list_motif_promoter_activity_kernel(
         for n, piece in enumerate(LAST_PIECES):
             gather_genes(1, j0, piece, held([P, piece], U32, "v2_1%d" % n))
             j0 = j0 + piece
-        gather_genes(0, HALF, HALF, placed([P, HALF], U32, "v2_01", 4 * T2))
 
         wq = [held([P, N], U32, "wq%d" % b) for b in range(PASSES)]
         wq_s = [held([P, N], U8, "wq_s%d" % b) for b in range(PASSES)]
@@ -181,18 +187,18 @@ def tile_list_motif_promoter_activity_kernel(
 
         def cast_w(b):
             w_bf[b] = held([P, N * PACK], BF16, "w_bf%d" % b, tag="win1_%d" % b)
-            for t0 in range(0, PACK, 2):
-                nc.vector.tensor_copy(
-                    w_bf[b][:].rearrange("p (t m r) -> p m r t", t=PACK, r=PACK)[:, :, :, t0 : t0 + 2],
-                    w_raw[b][:].rearrange("p r (m t) -> p m r t", t=PACK)[:, :, :, t0 : t0 + 2],
-                )
+            dealt = w_bf[b][:].rearrange("p (t m r) -> p m r t", t=PACK, r=PACK)
+            for n0, n1 in [piece[1:] for piece in W_PIECES if piece[0] == b]:
+                for t0 in range(0, PACK, 2):
+                    nc.vector.tensor_copy(
+                        dealt[:, n0 // PACK : n1 // PACK, :, t0 : t0 + 2],
+                        w_raw[b, n0][:].rearrange("p r (m t) -> p m r t", t=PACK)[:, :, :, t0 : t0 + 2],
+                    )
 
         def deal_w4():
-            w4 = held([P, PASSES * 2 * N], U8, "w4", tag="picked01")
             w4_s = held([P, PASSES * N], U8, "w4_s", tag="picked00")
-            deal(w4[:].bitcast(U16), w4_raw[:].bitcast(U16), 2)
             deal(w4_s[:], w4_s_raw[:], 1)
-            return w4, w4_s
+            return w4_s
 
         def quantise_w():
             for b in range(PASSES):
@@ -214,15 +220,22 @@ def tile_list_motif_promoter_activity_kernel(
         def banks(jc):
             return PACK * jc // BANK
 
+        def slices_of(g):
+            if g == 0:
+                return [(0, 1), (1, 2), (2, PACK)]
+            per_bank = BANK // width(g)
+            return [(t, t + per_bank) for t in range(0, PACK, per_bank)]
+
         def affinity(g, u, a):
             b, j0, jc = GROUPS[g]
-            per_bank = BANK // jc
+            t0, t1 = slices_of(g)[u]
+            per_bank = t1 - t0
             genes, at = v2[a, j0]
             opens = (g, u) not in aff
             if opens:
                 aff[g, u] = psum.tile([P, BANK], F32, name="aff", bufs=AFF_BANKS)
             for e in range(per_bank):
-                m0 = (per_bank * u + e) * P
+                m0 = (t0 + e) * P
                 nc.tensor.matmul_mx(
                     out=aff[g, u][:, e * jc : (e + 1) * jc],
                     lhsT=v1[a, b][:, m0 : m0 + P].bitcast(FP8X4),
@@ -238,24 +251,24 @@ def tile_list_motif_promoter_activity_kernel(
                 affinity(g, u, a)
             if u == 0:
                 sq[g] = held([P, PACK * width(g)], F32, "sq_%d" % g, tag="sq_%d" % g)
-            nc.scalar.activation(sq[g][:, u * BANK : (u + 1) * BANK], aff[g, u][:], ACT.Square)
+            t0, t1 = slices_of(g)[u]
+            jc = width(g)
+            nc.scalar.activation(sq[g][:, t0 * jc : t1 * jc], aff[g, u][:, : (t1 - t0) * jc], ACT.Square)
 
-        def root(g):
-            rs[g] = held([P, PACK * width(g)], F32, "rs_%d" % g, tag="rs_%d" % g)
-            step = BANK if g == 0 else PACK * width(g)
-            for c0 in range(0, PACK * width(g), step):
-                nc.scalar.activation(
-                    rs[g][:, c0 : c0 + step], sq[g][:, c0 : c0 + step], ACT.Abs_reciprocal_sqrt, bias=unit
-                )
+        def root(g, t0=0, t1=PACK):
+            if t0 == 0:
+                rs[g] = held([P, PACK * width(g)], F32, "rs_%d" % g, tag="rs_%d" % g)
+            cols = slice(t0 * width(g), t1 * width(g))
+            nc.scalar.activation(rs[g][:, cols], sq[g][:, cols], ACT.Abs_reciprocal_sqrt, bias=unit)
 
         def square_root(g):
             partial[g] = work.tile([P, PACK * width(g)], F32, name="partial", bufs=AHEAD)
-            if g >= SQUARED_FROM:
+            if g in SQUARED:
                 nc.scalar.activation(partial[g][:], rs[g][:], ACT.Square)
 
         def weigh(g):
             b, j0, jc = GROUPS[g]
-            if g >= SQUARED_FROM:
+            if g in SQUARED:
                 hb[g] = work.tile([P, PACK * jc], BF16, name="hb")
                 dst, factor = hb[g], partial[g]
             else:
@@ -270,7 +283,7 @@ def tile_list_motif_promoter_activity_kernel(
                 )
 
         def pooled_genes(g):
-            return width(g) // 2 if g in pathways_at and g >= SQUARED_FROM and width(g) == WIDE else 0
+            return width(g) // 2 if g in pathways_at and g in SQUARED and width(g) == WIDE else 0
 
         def weave_pooled(g):
             n = pooled_genes(g)
@@ -292,7 +305,7 @@ def tile_list_motif_promoter_activity_kernel(
             if pooled_genes(g):
                 n = width(g) - pooled_genes(g)
                 nc.vector.tensor_copy(woven_genes(hi[g], 0, n), sliced_genes(hb[g], 0, n))
-            elif g >= SQUARED_FROM:
+            elif g in SQUARED:
                 run = width(g) if g + 1 < groups else width(g) // 2
                 for j0 in range(0, width(g), run):
                     nc.vector.tensor_copy(woven_genes(hi[g], j0, run), sliced_genes(hb[g], j0, run))
@@ -371,7 +384,7 @@ def tile_list_motif_promoter_activity_kernel(
             jc = CHUNKS[c]
             y = ys[c]
             genes = slice(starts[c], starts[c] + jc)
-            yi = held([P, PACK * jc], BF16, "yi_%d" % c)
+            yi = held([P, PACK * jc], BF16, "yi_%d" % c, tag="picked1%d" % c if c < PASSES else "")
             copy = nc.scalar.copy if c + 1 < len(CHUNKS) else nc.vector.tensor_copy
             yq = held([P, jc], U32, "yq_%d" % c)
             run = jc if c + 1 < len(CHUNKS) else jc // 2
@@ -386,7 +399,7 @@ def tile_list_motif_promoter_activity_kernel(
             nc.sync.dma_start(out_words[:, genes], yq[:].bitcast(I32))
 
         last_group = [group_of(PASSES - 1, j0) for j0 in starts]
-        pathways_at = [g + (LAG_TWO_PRODUCTS if g < SQUARED_FROM else LAG_SQUARED) for g in last_group]
+        pathways_at = [g + (LAG_TWO_PRODUCTS if g < 4 else LAG_SQUARED) for g in last_group]
         codes_at = [pathways_at[c] + banks(jc) for c, jc in enumerate(CHUNKS)]
 
         def finish(step, w4, w4_s):
@@ -396,13 +409,16 @@ def tile_list_motif_promoter_activity_kernel(
                 if codes_at[c] == step:
                     quantise_out(c)
 
-        for u in range(banks(width(0))):
+        first_banks = slices_of(0)
+        for u in range(len(first_banks)):
             square(0, u)
+            if u:
+                root(0, *first_banks[u - 1])
         ahead = [(g, u) for g in range(1, groups) for u in range(banks(width(g)))]
         for g in range(groups):
             if 2 * g < len(ahead):
                 square(*ahead[2 * g])
-                root(g)
+                root(g, *(first_banks[-1] if g == 0 else ()))
                 square(*ahead[2 * g + 1])
                 square_root(g)
             elif g + 1 < groups:
@@ -422,7 +438,7 @@ def tile_list_motif_promoter_activity_kernel(
             if g == PASSES - 1:
                 cast_w(0)
             if g == PASSES:
-                w4, w4_s = deal_w4()
+                w4_s = deal_w4()
                 cast_w(1)
                 quantise_w()
             if g >= PASSES:

@@ -283,7 +283,7 @@ def tile_list_motif_promoter_activity_kernel(
                 )
 
         def pooled_genes(g):
-            return width(g) // 2 if g in pathways_at and g in SQUARED and width(g) == WIDE else 0
+            return SHORT if g in pathways_at and g in SQUARED else 0
 
         def weave_pooled(g):
             n = pooled_genes(g)
@@ -315,9 +315,10 @@ def tile_list_motif_promoter_activity_kernel(
         def quantise_h(g):
             hq[g] = held([P, width(g)], U32, "hq_%d" % g, tag="codes_%d" % g)
             hq_s[g] = work.tile([P, width(g)], U8, name="hq_s", bufs=AHEAD + 1, align_bytes=64)
-            run = width(g) if g + 1 < groups and not pooled_genes(g) else width(g) // 2
+            run = pooled_genes(g) or (width(g) if g + 1 < groups else width(g) // 2)
             for j0 in range(0, width(g), run):
-                source = hi_pooled[g][:] if j0 and pooled_genes(g) else hi[g][:, PACK * j0 : PACK * (j0 + run)]
+                last = j0 + run == width(g)
+                source = hi_pooled[g][:] if last and pooled_genes(g) else hi[g][:, PACK * j0 : PACK * (j0 + run)]
                 nc.vector.quantize_mx(
                     out=hq[g][:, j0 : j0 + run].bitcast(FP8X4), scales=hq_s[g][:, j0 : j0 + run], in_=source
                 )
@@ -325,7 +326,7 @@ def tile_list_motif_promoter_activity_kernel(
         def group_of(b, j):
             return [g for g, (gb, j0, jc) in enumerate(GROUPS) if gb == b and j0 <= j < j0 + jc][0]
 
-        ys = {}
+        ys, yqs = {}, {}
         y_s = held([P, S2], U8, "y_s")
         out_rows = out_0.rearrange("(p t) j -> p t j", t=PACK)
         out_words = out_1[0].rearrange("p m t -> p (m t)").bitcast(I32)
@@ -333,10 +334,10 @@ def tile_list_motif_promoter_activity_kernel(
         def pathways(c, w4, w4_s):
             jc = CHUNKS[c]
             per_bank = BANK // jc
-            y = ys[c] = held([P, PACK * jc], F32, "y_%d" % c, tag="sq_%d" % pathways_at[c] if c < PASSES else "")
+            y = ys[c] = held([P, PACK * jc], F32, "y_%d" % c, tag="sq_%d" % pathways_at[c] if jc == WIDE else "")
             first = work.tile([P, PACK * jc], F32, name="first", bufs=2)
             for u in range(banks(jc)):
-                if jc == WIDE:
+                if c != PASSES:
                     p1 = psum.tile([P, BANK], F32, name="p1")
                     p2 = psum.tile([P, BANK], F32, name="p2")
                 else:
@@ -377,35 +378,46 @@ def tile_list_motif_promoter_activity_kernel(
                     ]
                     nc.scalar.copy(first_run, p1_run)
                     nc.vector.tensor_tensor(y_run, p2_run, first_run, ALU.mult)
-            genes = slice(starts[c], starts[c] + jc)
-            nc.sync.dma_start(out_rows[:, :, genes], y[:].rearrange("p (t j) -> p t j", t=PACK))
+                nc.sync.dma_start(
+                    out_rows[:, per_bank * u : per_bank * (u + 1), starts[c] : starts[c] + jc],
+                    y[:, cols].rearrange("p (e j) -> p e j", e=per_bank),
+                )
 
         def quantise_out(c):
             jc = CHUNKS[c]
             y = ys[c]
-            genes = slice(starts[c], starts[c] + jc)
-            yi = held([P, PACK * jc], BF16, "yi_%d" % c, tag="picked1%d" % c if c < PASSES else "")
-            copy = nc.scalar.copy if c + 1 < len(CHUNKS) else nc.vector.tensor_copy
-            yq = held([P, jc], U32, "yq_%d" % c)
+            yi = held([P, PACK * jc], BF16, "yi_%d" % c, tag=("picked10", "picked11", "picked01", "", "")[c])
+            if jc == WIDE or CHUNKS[c - 1] == WIDE:
+                yqs[c] = (held([P, WIDE], U32, "yq_%d" % c), starts[c])
+            else:
+                yqs[c] = yqs[c - 1]
+            yq, base = yqs[c]
+            at = starts[c] - base
             run = jc if c + 1 < len(CHUNKS) else jc // 2
             for j0 in range(0, jc, run):
+                copy = nc.vector.tensor_copy if j0 else nc.scalar.copy
                 copy(woven_genes(yi, j0, run), sliced_genes(y, j0, run))
             for j0 in range(0, jc, run):
                 nc.vector.quantize_mx(
-                    out=yq[:, j0 : j0 + run].bitcast(FP8X4),
+                    out=yq[:, at + j0 : at + j0 + run].bitcast(FP8X4),
                     scales=y_s[:, starts[c] + j0 : starts[c] + j0 + run],
                     in_=yi[:, PACK * j0 : PACK * (j0 + run)],
                 )
-            nc.sync.dma_start(out_words[:, genes], yq[:].bitcast(I32))
+            if at + jc == WIDE:
+                nc.sync.dma_start(out_words[:, base : base + WIDE], yq[:].bitcast(I32))
 
         last_group = [group_of(PASSES - 1, j0) for j0 in starts]
         pathways_at = [g + (LAG_TWO_PRODUCTS if g < 4 else LAG_SQUARED) for g in last_group]
+        pathways_at[2] = groups - 1
         codes_at = [pathways_at[c] + banks(jc) for c, jc in enumerate(CHUNKS)]
+
+        codes_at[0] = codes_at[1] = groups
 
         def finish(step, w4, w4_s):
             for c in range(len(CHUNKS)):
                 if pathways_at[c] == step:
                     pathways(c, w4, w4_s)
+            for c in range(len(CHUNKS)):
                 if codes_at[c] == step:
                     quantise_out(c)
 
@@ -428,7 +440,8 @@ def tile_list_motif_promoter_activity_kernel(
                 square_root(g + 1)
             weigh(g)
             if pooled_genes(g):
-                weave_h(g)
+                if pooled_genes(g) < width(g):
+                    weave_h(g)
                 quantise_h(g - 1)
                 weave_pooled(g)
             else:

@@ -31,6 +31,8 @@ ROW0 = P - PASSES * ROWS
 PLANE_ROW = (12, 4)
 LAST_PIECES = (256, 256, 512)
 W_PIECES = ((0, 0, N // 2), (0, N // 2, N), (1, 0, N))
+POOLED = 160
+POOLED_OUT = 64
 WIDE, SHORT = 256, 128
 CHUNKS = (WIDE, WIDE, WIDE, SHORT, SHORT)
 GROUPS = tuple((b, j0, WIDE) for j0 in range(0, S2, WIDE) for b in range(PASSES))[:-1] + (
@@ -211,7 +213,6 @@ def tile_list_motif_promoter_activity_kernel(
 
         starts = [sum(CHUNKS[:c]) for c in range(len(CHUNKS))]
         groups = len(GROUPS)
-        hi_pooled = {}
         aff, sq, rs, partial, hb, hi, hq, hq_s = {}, {}, {}, {}, {}, {}, {}, {}
 
         def width(g):
@@ -261,10 +262,12 @@ def tile_list_motif_promoter_activity_kernel(
             cols = slice(t0 * width(g), t1 * width(g))
             nc.scalar.activation(rs[g][:, cols], sq[g][:, cols], ACT.Abs_reciprocal_sqrt, bias=unit)
 
-        def square_root(g):
-            partial[g] = work.tile([P, PACK * width(g)], F32, name="partial", bufs=AHEAD)
+        def square_root(g, t0=0, t1=PACK):
+            if t0 == 0:
+                partial[g] = work.tile([P, PACK * width(g)], F32, name="partial", bufs=AHEAD)
             if g in SQUARED:
-                nc.scalar.activation(partial[g][:], rs[g][:], ACT.Square)
+                cols = slice(t0 * width(g), t1 * width(g))
+                nc.scalar.activation(partial[g][:, cols], rs[g][:, cols], ACT.Square)
 
         def weigh(g):
             b, j0, jc = GROUPS[g]
@@ -283,45 +286,38 @@ def tile_list_motif_promoter_activity_kernel(
                 )
 
         def pooled_genes(g):
-            return SHORT if g in pathways_at and g in SQUARED else 0
+            return min(POOLED, width(g)) if g in pathways_at and g in SQUARED else 0
 
-        def weave_pooled(g):
-            n = pooled_genes(g)
-            hi_pooled[g] = held([P, PACK * n], BF16, "hi_pooled_%d" % g, tag="hi_%d" % (g - 1))
+        def pool_weave(dst, src, genes, n):
             nc.gpsimd.tensor_scalar(
-                hi_pooled[g][:].rearrange("p (j t) -> p j t", t=PACK),
-                hb[g][:].rearrange("p (t j) -> p j t", t=PACK)[:, width(g) - n :, :],
+                dst[:].rearrange("p (j t) -> p j t", t=PACK)[:, genes - n :, :],
+                src[:].rearrange("p (t j) -> p j t", t=PACK)[:, genes - n :, :],
                 1.0,
                 -0.0,
                 ALU.mult,
                 ALU.add,
             )
 
+        def weave_pooled(g):
+            n = pooled_genes(g)
+            hi[g] = held([P, PACK * width(g)], BF16, "hi_%d" % g, tag="hi_%d" % (g - 1))
+            pool_weave(hi[g], hb[g], width(g), n)
+
         def weave_h(g):
-            if g + 1 < groups and pooled_genes(g + 1):
+            if pooled_genes(g + 1):
                 hi[g] = held([P, PACK * width(g)], BF16, "hi_%d" % g, tag="hi_%d" % g)
-            else:
+            elif not pooled_genes(g):
                 hi[g] = work.tile([P, PACK * width(g)], BF16, name="hi", align_bytes=64, bufs=2)
-            if pooled_genes(g):
+            if g in SQUARED:
                 n = width(g) - pooled_genes(g)
                 nc.vector.tensor_copy(woven_genes(hi[g], 0, n), sliced_genes(hb[g], 0, n))
-            elif g in SQUARED:
-                run = width(g) if g + 1 < groups else width(g) // 2
-                for j0 in range(0, width(g), run):
-                    nc.vector.tensor_copy(woven_genes(hi[g], j0, run), sliced_genes(hb[g], j0, run))
             else:
                 nc.vector.tensor_tensor(woven(hi[g], PAIR), sliced(partial[g], PAIR), sliced(rs[g], PAIR), ALU.mult)
 
         def quantise_h(g):
             hq[g] = held([P, width(g)], U32, "hq_%d" % g, tag="codes_%d" % g)
             hq_s[g] = work.tile([P, width(g)], U8, name="hq_s", bufs=AHEAD + 1, align_bytes=64)
-            run = pooled_genes(g) or (width(g) if g + 1 < groups else width(g) // 2)
-            for j0 in range(0, width(g), run):
-                last = j0 + run == width(g)
-                source = hi_pooled[g][:] if last and pooled_genes(g) else hi[g][:, PACK * j0 : PACK * (j0 + run)]
-                nc.vector.quantize_mx(
-                    out=hq[g][:, j0 : j0 + run].bitcast(FP8X4), scales=hq_s[g][:, j0 : j0 + run], in_=source
-                )
+            nc.vector.quantize_mx(out=hq[g][:].bitcast(FP8X4), scales=hq_s[g][:], in_=hi[g][:])
 
         def group_of(b, j):
             return [g for g, (gb, j0, jc) in enumerate(GROUPS) if gb == b and j0 <= j < j0 + jc][0]
@@ -386,25 +382,29 @@ def tile_list_motif_promoter_activity_kernel(
         def quantise_out(c):
             jc = CHUNKS[c]
             y = ys[c]
-            yi = held([P, PACK * jc], BF16, "yi_%d" % c, tag=("picked10", "picked11", "picked01", "", "")[c])
-            if jc == WIDE or CHUNKS[c - 1] == WIDE:
-                yqs[c] = (held([P, WIDE], U32, "yq_%d" % c), starts[c])
+            yi = held([P, PACK * jc], BF16, "yi_%d" % c, tag=("picked10", "picked11", "hi_%d" % (groups - 2), "", "")[c])
+            genes = 2 * jc if c < PASSES else jc
+            if c != 1:
+                yqs[c] = (held([P, genes], U32, "yq_%d" % c), starts[c])
             else:
                 yqs[c] = yqs[c - 1]
             yq, base = yqs[c]
             at = starts[c] - base
             run = jc if c + 1 < len(CHUNKS) else jc // 2
+            pooled = POOLED_OUT if c == 2 else 0
+            if pooled:
+                pool_weave(yi, y, jc, pooled)
             for j0 in range(0, jc, run):
                 copy = nc.vector.tensor_copy if j0 else nc.scalar.copy
-                copy(woven_genes(yi, j0, run), sliced_genes(y, j0, run))
+                copy(woven_genes(yi, j0, run - pooled), sliced_genes(y, j0, run - pooled))
             for j0 in range(0, jc, run):
                 nc.vector.quantize_mx(
                     out=yq[:, at + j0 : at + j0 + run].bitcast(FP8X4),
                     scales=y_s[:, starts[c] + j0 : starts[c] + j0 + run],
                     in_=yi[:, PACK * j0 : PACK * (j0 + run)],
                 )
-            if at + jc == WIDE:
-                nc.sync.dma_start(out_words[:, base : base + WIDE], yq[:].bitcast(I32))
+            if at + jc == genes:
+                nc.sync.dma_start(out_words[:, base : base + genes], yq[:].bitcast(I32))
 
         last_group = [group_of(PASSES - 1, j0) for j0 in starts]
         pathways_at = [g + (LAG_TWO_PRODUCTS if g < 4 else LAG_SQUARED) for g in last_group]
@@ -428,7 +428,13 @@ def tile_list_motif_promoter_activity_kernel(
                 root(0, *first_banks[u - 1])
         ahead = [(g, u) for g in range(1, groups) for u in range(banks(width(g)))]
         for g in range(groups):
-            if 2 * g < len(ahead):
+            if g in SQUARED and width(g) == WIDE:
+                square(*ahead[2 * g])
+                for step in (root, square_root):
+                    for t0 in range(0, PACK, PAIR):
+                        step(g, t0, t0 + PAIR)
+                square(*ahead[2 * g + 1])
+            elif 2 * g < len(ahead):
                 square(*ahead[2 * g])
                 root(g, *(first_banks[-1] if g == 0 else ()))
                 square(*ahead[2 * g + 1])
@@ -440,8 +446,6 @@ def tile_list_motif_promoter_activity_kernel(
                 square_root(g + 1)
             weigh(g)
             if pooled_genes(g):
-                if pooled_genes(g) < width(g):
-                    weave_h(g)
                 quantise_h(g - 1)
                 weave_pooled(g)
             else:
@@ -456,6 +460,8 @@ def tile_list_motif_promoter_activity_kernel(
                 quantise_w()
             if g >= PASSES:
                 finish(g, w4, w4_s)
+            if 0 < pooled_genes(g) < width(g):
+                weave_h(g)
         quantise_h(groups - 1)
         for step in range(groups, codes_at[-1] + 1):
             finish(step, w4, w4_s)

@@ -68,12 +68,12 @@ def tile_list_motif_promoter_activity_kernel(
         def sliced(src, run):
             return src[:].rearrange("p (t x i) -> p x t i", i=run, t=PACK)
 
-        def woven_genes(dst, j0, run):
-            return dst[:, PACK * j0 : PACK * (j0 + run)].rearrange("p (x i t) -> p x t i", i=LINE, t=PACK)
+        def woven_genes(dst, j0, run, near=LINE):
+            return dst[:, PACK * j0 : PACK * (j0 + run)].rearrange("p (x i t) -> p x t i", i=near, t=PACK)
 
-        def sliced_genes(src, j0, run):
+        def sliced_genes(src, j0, run, near=LINE):
             return src[:].rearrange("p (t j) -> p t j", t=PACK)[:, :, j0 : j0 + run].rearrange(
-                "p t (x i) -> p x t i", i=LINE
+                "p t (x i) -> p x t i", i=near
             )
 
         win1_s = held([P, T1], U8, "win1_s")
@@ -396,7 +396,7 @@ def tile_list_motif_promoter_activity_kernel(
                 pool_weave(yi, y, jc, pooled)
             for j0 in range(0, jc, run):
                 copy = nc.vector.tensor_copy if j0 else nc.scalar.copy
-                copy(woven_genes(yi, j0, run - pooled), sliced_genes(y, j0, run - pooled))
+                copy(woven_genes(yi, j0, run - pooled, PAIR), sliced_genes(y, j0, run - pooled, PAIR))
             for j0 in range(0, jc, run):
                 nc.vector.quantize_mx(
                     out=yq[:, at + j0 : at + j0 + run].bitcast(FP8X4),

@@ -118,7 +118,8 @@ def tile_list_motif_promoter_activity_kernel(
                     w4_raw[:].bitcast(I32).rearrange("p (b n) -> p b n", b=PASSES),
                     w4_words.bitcast(I32).rearrange("b p n -> p b n"),
                 )
-            load_words(win2[a], tab2_words[a])
+            else:
+                load_words(win2[a], tab2_words[a])
 
         def deal(dst, src, column_bytes, copy=nc.vector.tensor_copy):
             per_line = LINE_BYTES // column_bytes
@@ -141,6 +142,8 @@ def tile_list_motif_promoter_activity_kernel(
                 planes[1][PLANE_ROW[1] + r : P : QUADRANT, :].bitcast(I32),
                 planes[0][ROW0 + ROWS + r : P : 4, :].bitcast(I32),
             )
+            if r == 0:
+                load_words(win2[1], tab2_words[1])
         for q in range(3):
             to, at = QUADRANT * q + PLANE_ROW[0], ROW0 + 4 * q
             nc.sync.dma_start(planes[0][to : to + 4, :].bitcast(I32), planes[0][at : at + 4, :].bitcast(I32))

@@ -137,16 +137,15 @@ def tile_list_motif_promoter_activity_kernel(
         nc.vector.tensor_copy(picked2_s[:], win2_s[:].indirect(idx2[:]))
         deal(planes[0][:, :S1], picked_s[:], 1)
         nc.vector.tensor_copy(planes[0][:, S1:].bitcast(I32), picked2_s[:].bitcast(I32))
+        for q in range(3):
+            to, at = QUADRANT * q + PLANE_ROW[0], ROW0 + 4 * q
+            nc.sync.dma_start(planes[0][to : to + 4, :].bitcast(I32), planes[0][at : at + 4, :].bitcast(I32))
+        load_words(win2[1], tab2_words[1])
         for r in range(4):
             nc.sync.dma_start(
                 planes[1][PLANE_ROW[1] + r : P : QUADRANT, :].bitcast(I32),
                 planes[0][ROW0 + ROWS + r : P : 4, :].bitcast(I32),
             )
-            if r == 0:
-                load_words(win2[1], tab2_words[1])
-        for q in range(3):
-            to, at = QUADRANT * q + PLANE_ROW[0], ROW0 + 4 * q
-            nc.sync.dma_start(planes[0][to : to + 4, :].bitcast(I32), planes[0][at : at + 4, :].bitcast(I32))
         w_raw = {}
         for b, n0, n1 in W_PIECES:
             w_raw[b, n0] = held([P, PACK, n1 - n0], F32, "w_raw%d_%d" % (b, n0), tag="w_raw%d_%d" % (b, n0))
@@ -251,7 +250,7 @@ def tile_list_motif_promoter_activity_kernel(
                 )
 
         def square(g, u):
-            for a in (1, 0) if (g, u) == (0, 0) else (0, 1):
+            for a in (1,) if (g, u) in aff else (0, 1):
                 affinity(g, u, a)
             if u == 0:
                 sq[g] = held([P, PACK * width(g)], F32, "sq_%d" % g, tag="sq_%d" % g)
@@ -425,6 +424,9 @@ def tile_list_motif_promoter_activity_kernel(
                     quantise_out(c)
 
         first_banks = slices_of(0)
+        for u in range(len(first_banks)):
+            affinity(0, u, 0)
+        affinity(1, 0, 0)
         for u in range(len(first_banks)):
             square(0, u)
             if u:

@@ -111,7 +111,13 @@ def tile_list_motif_promoter_activity_kernel(
             column = PACK * GROUPS[g][0] + 1
             nc.scalar.copy(ab_second[g][:], ab[:, column : column + 1])
         w4_raw = held([P, PASSES * 2 * N], U8, "w4_raw")
+        w4_s_raw = held([P, N], U8, "w4_s_raw")
+        nc.vector.memset(w4_s_raw[:ROW0, :].bitcast(I32), 0)
         for a in range(PASSES):
+            if a:
+                nc.sync.dma_start(
+                    w4_s_raw[ROW0:, :].bitcast(I32), w4_scales.rearrange("a q n -> (a q) n").bitcast(I32)
+                )
             load_words(win1[a], tab_words[a])
             if a + 1 == PASSES:
                 nc.sync.dma_start(
@@ -152,14 +158,6 @@ def tile_list_motif_promoter_activity_kernel(
             nc.sync.dma_start(
                 w_raw[b, n0][:], w[b * PASS : (b + 1) * PASS, n0:n1].rearrange("(p r) n -> p r n", r=PACK)
             )
-        w4_s_raw = held([P, PASSES * N], U8, "w4_s_raw")
-        nc.vector.memset(w4_s_raw[:].bitcast(I32), 0)
-        for q in range(4):
-            nc.sync.dma_start(
-                w4_s_raw[QUADRANT * q : QUADRANT * q + 4, :].bitcast(I32).rearrange("r (b n) -> r b n", b=PASSES),
-                w4_scales[:, 4 * q : 4 * q + 4, :].bitcast(I32).rearrange("b r n -> r b n"),
-            )
-
         v1, v2 = {}, {}
 
         def gather_factors(a):
@@ -180,6 +178,16 @@ def tile_list_motif_promoter_activity_kernel(
         gather_factors(0)
         gather_genes(0, 0, HALF, held([P, HALF], U32, "v2_00"))
         gather_factors(1)
+        dealt = held([P, N], U8, "w4_s_dealt", tag="picked10")
+        deal(dealt[:], w4_s_raw[:], 1)
+        w4_s = held([P, PASSES * N], U8, "w4_s", tag="picked01")
+        for b in range(PASSES):
+            for q in range(4):
+                at = ROW0 + ROWS * b + 4 * q
+                nc.sync.dma_start(
+                    w4_s[QUADRANT * q : QUADRANT * q + 4, b * N : (b + 1) * N].bitcast(I32),
+                    dealt[at : at + 4, :].bitcast(I32),
+                )
         j0 = 0
         for n, piece in enumerate(LAST_PIECES):
             gather_genes(1, j0, piece, held([P, piece], U32, "v2_1%d" % n))
@@ -198,11 +206,6 @@ def tile_list_motif_promoter_activity_kernel(
                         dealt[:, n0 // PACK : n1 // PACK, :, t0 : t0 + 2],
                         w_raw[b, n0][:].rearrange("p r (m t) -> p m r t", t=PACK)[:, :, :, t0 : t0 + 2],
                     )
-
-        def deal_w4():
-            w4_s = held([P, PASSES * N], U8, "w4_s", tag="picked00")
-            deal(w4_s[:], w4_s_raw[:], 1)
-            return w4_s
 
         def quantise_w():
             for b in range(PASSES):
@@ -384,9 +387,9 @@ def tile_list_motif_promoter_activity_kernel(
         def quantise_out(c):
             jc = CHUNKS[c]
             y = ys[c]
-            yi = held([P, PACK * jc], BF16, "yi_%d" % c, tag=("picked10", "picked11", "hi_%d" % (groups - 2), "", "")[c])
-            genes = 2 * jc if c < PASSES else jc
-            if c != 1:
+            yi = held([P, PACK * jc], BF16, "yi_%d" % c, tag=("picked00", "picked11", "hi_%d" % (groups - 2), "", "")[c])
+            genes = sum(CHUNKS[c // 2 * 2 : c // 2 * 2 + 2])
+            if c % 2 == 0:
                 yqs[c] = (held([P, genes], U32, "yq_%d" % c), starts[c])
             else:
                 yqs[c] = yqs[c - 1]
@@ -397,7 +400,7 @@ def tile_list_motif_promoter_activity_kernel(
             if pooled:
                 pool_weave(yi, y, jc, pooled)
             for j0 in range(0, jc, run):
-                copy = nc.vector.tensor_copy if j0 else nc.scalar.copy
+                copy = nc.vector.tensor_copy if c + 1 == len(CHUNKS) else nc.scalar.copy
                 copy(woven_genes(yi, j0, run - pooled, PAIR), sliced_genes(y, j0, run - pooled, PAIR))
             for j0 in range(0, jc, run):
                 nc.vector.quantize_mx(
@@ -460,7 +463,6 @@ def tile_list_motif_promoter_activity_kernel(
             if g == PASSES - 1:
                 cast_w(0)
             if g == PASSES:
-                w4_s = deal_w4()
                 cast_w(1)
                 quantise_w()
             if g >= PASSES:

@@ -25,6 +25,7 @@ BANK = 512
 LINE = 4
 PAIR = 2
 LINE_BYTES = 16
+ROW_ALIGN = 256
 ROWS = 16
 QUADRANT = 32
 ROW0 = P - PASSES * ROWS
@@ -57,10 +58,10 @@ def tile_list_motif_promoter_activity_kernel(
         by_offset = ctx.enter_context(tc.tile_pool(name="by_offset", bufs=1))
 
         def placed(shape, dtype, name, offset):
-            return by_offset.tile(shape, dtype, name=name, offset=offset, align_bytes=64)
+            return by_offset.tile(shape, dtype, name=name, offset=offset, align_bytes=ROW_ALIGN)
 
-        def held(shape, dtype, name, tag=""):
-            return keep.tile(shape, dtype, name=name, tag=tag, align_bytes=64)
+        def held(shape, dtype, name, tag="", align=64):
+            return keep.tile(shape, dtype, name=name, tag=tag, align_bytes=align)
 
         def woven(dst, run):
             return dst[:].rearrange("p (x i t) -> p x t i", i=run, t=PACK)
@@ -76,15 +77,15 @@ def tile_list_motif_promoter_activity_kernel(
                 "p t (x i) -> p x t i", i=near
             )
 
-        win1_s = held([P, T1], U8, "win1_s")
-        win2_s = held([P, T2], U8, "win2_s", tag="win2_s")
+        win1_s = held([P, T1], U8, "win1_s", align=ROW_ALIGN)
+        win2_s = held([P, T2], U8, "win2_s", tag="win2_s", align=ROW_ALIGN)
         nc.vector.memset(win1_s[:ROW0, :].bitcast(I32), 0)
         nc.vector.memset(win2_s[:ROW0, :].bitcast(I32), 0)
         idx1 = keep.tile([P, S1 // 16], U16, name="idx1")
         idx2 = keep.tile([P, S2 // 16], U16, name="idx2")
-        win1 = [held([P, T1], U32, "win1_%d" % a, tag="win1_%d" % a) for a in range(PASSES)]
+        win1 = [held([P, T1], U32, "win1_%d" % a, tag="win1_%d" % a, align=ROW_ALIGN) for a in range(PASSES)]
         win2 = [placed([P, T2], U32, "win2_%d" % a, 4 * T2 * a) for a in range(PASSES)]
-        planes = [held([P, S1 + S2], U8, "plane%d" % a, tag="win2_s" if a else "") for a in range(PASSES)]
+        planes = [held([P, S1 + S2], U8, "plane%d" % a, tag="win2_s" if a else "", align=ROW_ALIGN) for a in range(PASSES)]
 
         def load_words(dst, src):
             nc.sync.dma_start(dst[:].bitcast(I32), src.rearrange("p n t -> p (n t)").bitcast(I32))
@@ -110,7 +111,7 @@ def tile_list_motif_promoter_activity_kernel(
             ab_second[g] = held([P, 1], F32, "ab_%d" % g, tag="codes_%d" % (g - 1))
             column = PACK * GROUPS[g][0] + 1
             nc.scalar.copy(ab_second[g][:], ab[:, column : column + 1])
-        w4_raw = held([P, PASSES * 2 * N], U8, "w4_raw")
+        w4_raw = held([P, PASSES * 2 * N], U8, "w4_raw", align=ROW_ALIGN)
         w4_s_raw = held([P, N], U8, "w4_s_raw")
         nc.vector.memset(w4_s_raw[:ROW0, :].bitcast(I32), 0)
         for a in range(PASSES):
@@ -154,7 +155,7 @@ def tile_list_motif_promoter_activity_kernel(
             )
         w_raw = {}
         for b, n0, n1 in W_PIECES:
-            w_raw[b, n0] = held([P, PACK, n1 - n0], F32, "w_raw%d_%d" % (b, n0), tag="w_raw%d_%d" % (b, n0))
+            w_raw[b, n0] = held([P, PACK, n1 - n0], F32, "w_raw%d_%d" % (b, n0), align=ROW_ALIGN)
             nc.sync.dma_start(
                 w_raw[b, n0][:], w[b * PASS : (b + 1) * PASS, n0:n1].rearrange("(p r) n -> p r n", r=PACK)
             )
@@ -198,7 +199,7 @@ def tile_list_motif_promoter_activity_kernel(
         w_bf = {}
 
         def cast_w(b):
-            w_bf[b] = held([P, N * PACK], BF16, "w_bf%d" % b, tag="win1_%d" % b)
+            w_bf[b] = held([P, N * PACK], BF16, "w_bf%d" % b, tag="win1_%d" % b, align=ROW_ALIGN)
             dealt = w_bf[b][:].rearrange("p (t m r) -> p m r t", t=PACK, r=PACK)
             for n0, n1 in [piece[1:] for piece in W_PIECES if piece[0] == b]:
                 for t0 in range(0, PACK, 2):

@@ -304,16 +304,20 @@ def tile_list_motif_promoter_activity_kernel(
                 ALU.add,
             )
 
+        def open_woven(g):
+            if g + 1 == groups:
+                hi[g] = held([P, PACK * width(g)], BF16, "hi_last", tag="hi_last")
+            else:
+                hi[g] = work.tile([P, PACK * width(g)], BF16, name="hi", align_bytes=64, bufs=2)
+
         def weave_pooled(g):
             n = pooled_genes(g)
-            hi[g] = held([P, PACK * width(g)], BF16, "hi_%d" % g, tag="hi_%d" % (g - 1))
+            open_woven(g)
             pool_weave(hi[g], hb[g], width(g), n)
 
         def weave_h(g):
-            if pooled_genes(g + 1):
-                hi[g] = held([P, PACK * width(g)], BF16, "hi_%d" % g, tag="hi_%d" % g)
-            elif not pooled_genes(g):
-                hi[g] = work.tile([P, PACK * width(g)], BF16, name="hi", align_bytes=64, bufs=2)
+            if not pooled_genes(g):
+                open_woven(g)
             if g in SQUARED:
                 n = width(g) - pooled_genes(g)
                 nc.vector.tensor_copy(woven_genes(hi[g], 0, n), sliced_genes(hb[g], 0, n))
@@ -388,7 +392,7 @@ def tile_list_motif_promoter_activity_kernel(
         def quantise_out(c):
             jc = CHUNKS[c]
             y = ys[c]
-            yi = held([P, PACK * jc], BF16, "yi_%d" % c, tag=("picked00", "picked11", "hi_%d" % (groups - 2), "", "")[c])
+            yi = held([P, PACK * jc], BF16, "yi_%d" % c, tag=("picked00", "picked11", "hi_last", "", "")[c])
             genes = sum(CHUNKS[c // 2 * 2 : c // 2 * 2 + 2])
             if c % 2 == 0:
                 yqs[c] = (held([P, genes], U32, "yq_%d" % c), starts[c])

@@ -257,7 +257,7 @@ def tile_list_motif_promoter_activity_kernel(
             for a in (1,) if (g, u) in aff else (0, 1):
                 affinity(g, u, a)
             if u == 0:
-                sq[g] = held([P, PACK * width(g)], F32, "sq_%d" % g, tag="sq_%d" % g)
+                sq[g] = held([P, PACK * width(g)], F32, "sq_%d" % g, tag="sq_%d" % g, align=ROW_ALIGN)
             t0, t1 = slices_of(g)[u]
             jc = width(g)
             nc.scalar.activation(sq[g][:, t0 * jc : t1 * jc], aff[g, u][:, : (t1 - t0) * jc], ACT.Square)
@@ -333,14 +333,15 @@ def tile_list_motif_promoter_activity_kernel(
             return [g for g, (gb, j0, jc) in enumerate(GROUPS) if gb == b and j0 <= j < j0 + jc][0]
 
         ys, yqs = {}, {}
-        y_s = held([P, S2], U8, "y_s")
+        y_s = held([P, S2], U8, "y_s", align=ROW_ALIGN)
         out_rows = out_0.rearrange("(p t) j -> p t j", t=PACK)
         out_words = out_1[0].rearrange("p m t -> p (m t)").bitcast(I32)
 
         def pathways(c, w4, w4_s):
             jc = CHUNKS[c]
             per_bank = BANK // jc
-            y = ys[c] = held([P, PACK * jc], F32, "y_%d" % c, tag="sq_%d" % pathways_at[c] if jc == WIDE else "")
+            bytes_of = "sq_%d" % pathways_at[c] if jc == WIDE else ""
+            y = ys[c] = held([P, PACK * jc], F32, "y_%d" % c, tag=bytes_of, align=ROW_ALIGN)
             first = work.tile([P, PACK * jc], F32, name="first", bufs=2)
             for u in range(banks(jc)):
                 if c != PASSES:
@@ -395,7 +396,7 @@ def tile_list_motif_promoter_activity_kernel(
             yi = held([P, PACK * jc], BF16, "yi_%d" % c, tag=("picked00", "picked11", "hi_last", "", "")[c])
             genes = sum(CHUNKS[c // 2 * 2 : c // 2 * 2 + 2])
             if c % 2 == 0:
-                yqs[c] = (held([P, genes], U32, "yq_%d" % c), starts[c])
+                yqs[c] = (held([P, genes], U32, "yq_%d" % c, align=ROW_ALIGN), starts[c])
             else:
                 yqs[c] = yqs[c - 1]
             yq, base = yqs[c]

@@ -77,26 +77,27 @@ def tile_list_motif_promoter_activity_kernel(
                 "p t (x i) -> p x t i", i=near
             )
 
-        win1_s = held([P, T1], U8, "win1_s", align=ROW_ALIGN)
+        win1_s = held([P, T1], U8, "win1_s", tag="win1_s", align=ROW_ALIGN)
         win2_s = held([P, T2], U8, "win2_s", tag="win2_s", align=ROW_ALIGN)
         nc.vector.memset(win1_s[:ROW0, :].bitcast(I32), 0)
-        nc.vector.memset(win2_s[:ROW0, :].bitcast(I32), 0)
+        nc.vector.memset(win2_s[QUADRANT : 2 * QUADRANT, :].bitcast(I32), 0)
+        nc.gpsimd.memset(win2_s[2 * QUADRANT :, :].bitcast(I32), 0)
         idx1 = keep.tile([P, S1 // 16], U16, name="idx1")
         idx2 = keep.tile([P, S2 // 16], U16, name="idx2")
         win1 = [held([P, T1], U32, "win1_%d" % a, tag="win1_%d" % a, align=ROW_ALIGN) for a in range(PASSES)]
         win2 = [placed([P, T2], U32, "win2_%d" % a, 4 * T2 * a) for a in range(PASSES)]
-        planes = [held([P, S1 + S2], U8, "plane%d" % a, tag="win2_s" if a else "", align=ROW_ALIGN) for a in range(PASSES)]
+        planes = [held([P, S1 + S2], U8, "plane%d" % a, tag=("win1_s", "win2_s")[a], align=ROW_ALIGN) for a in range(PASSES)]
 
         def load_words(dst, src):
             nc.sync.dma_start(dst[:].bitcast(I32), src.rearrange("p n t -> p (n t)").bitcast(I32))
 
-        def load_scales(win, src):
-            nc.scalar.dma_start(win[ROW0:, :].bitcast(I32), src.rearrange("a q n -> (a q) n").bitcast(I32))
+        def load_scales(win, row, src):
+            nc.scalar.dma_start(win[row : row + QUADRANT, :].bitcast(I32), src.rearrange("a q n -> (a q) n").bitcast(I32))
 
         nc.sync.dma_start(idx1[:], offs)
-        load_scales(win1_s, tab_scales)
+        load_scales(win1_s, ROW0, tab_scales)
         nc.sync.dma_start(idx2[:], offs2)
-        load_scales(win2_s, tab2_scales)
+        load_scales(win2_s, 0, tab2_scales)
         ab = held([P, PASSES * PACK], F32, "ab")
         nc.scalar.dma_start(
             ab[:].rearrange("p (b t) -> p b t", b=PASSES), abund.rearrange("(b p t) -> p b t", b=PASSES, t=PACK)
@@ -143,10 +144,13 @@ def tile_list_motif_promoter_activity_kernel(
         nc.vector.tensor_copy(picked_s[:], win1_s[:].indirect(idx1[:]))
         nc.vector.tensor_copy(picked2_s[:], win2_s[:].indirect(idx2[:]))
         deal(planes[0][:, :S1], picked_s[:], 1)
-        nc.vector.tensor_copy(planes[0][:, S1:].bitcast(I32), picked2_s[:].bitcast(I32))
-        for q in range(3):
-            to, at = QUADRANT * q + PLANE_ROW[0], ROW0 + 4 * q
-            nc.sync.dma_start(planes[0][to : to + 4, :].bitcast(I32), planes[0][at : at + 4, :].bitcast(I32))
+        nc.vector.tensor_copy(planes[0][ROW0:, S1:].bitcast(I32), picked2_s[:QUADRANT, :].bitcast(I32))
+        def move_first_pass(cols):
+            for q in range(3):
+                to, at = QUADRANT * q + PLANE_ROW[0], ROW0 + 4 * q
+                nc.sync.dma_start(planes[0][to : to + 4, cols].bitcast(I32), planes[0][at : at + 4, cols].bitcast(I32))
+
+        move_first_pass(slice(0, S1 + PASS))
         load_words(win2[1], tab2_words[1])
         for r in range(4):
             nc.sync.dma_start(
@@ -159,6 +163,8 @@ def tile_list_motif_promoter_activity_kernel(
             nc.sync.dma_start(
                 w_raw[b, n0][:], w[b * PASS : (b + 1) * PASS, n0:n1].rearrange("(p r) n -> p r n", r=PACK)
             )
+            if b + 1 == PASSES:
+                move_first_pass(slice(S1 + PASS, S1 + S2))
         v1, v2 = {}, {}
 
         def gather_factors(a):

@@ -185,9 +185,9 @@ def tile_list_motif_promoter_activity_kernel(
         gather_factors(0)
         gather_genes(0, 0, HALF, held([P, HALF], U32, "v2_00"))
         gather_factors(1)
-        dealt = held([P, N], U8, "w4_s_dealt", tag="picked10")
-        deal(dealt[:], w4_s_raw[:], 1)
-        w4_s = held([P, PASSES * N], U8, "w4_s", tag="picked01")
+        dealt = held([P, N], U8, "w4_s_dealt", tag="picked01")
+        deal(dealt[:], w4_s_raw[:], 1, nc.gpsimd.tensor_copy)
+        w4_s = held([P, PASSES * N], U8, "w4_s", tag="picked10")
         for b in range(PASSES):
             for q in range(4):
                 at = ROW0 + ROWS * b + 4 * q

@@ -31,11 +31,12 @@ QUADRANT = 32
 ROW0 = P - PASSES * ROWS
 PLANE_ROW = (12, 4)
 LAST_PIECES = (256, 256, 512)
-W_PIECES = ((0, 0, N // 2), (0, N // 2, N), (1, 0, N))
-POOLED = 160
+W_PIECES = ((0, 0, N // 4), (0, N // 4, N), (1, 0, N))
+POOLED = 208
 POOLED_OUT = 64
 WIDE, SHORT = 256, 128
 CHUNKS = (WIDE, WIDE, WIDE, SHORT, SHORT)
+CODE_STORES = ((0, 2), (2, 3), (3, 5))
 GROUPS = tuple((b, j0, WIDE) for j0 in range(0, S2, WIDE) for b in range(PASSES))[:-1] + (
     (PASSES - 1, S2 - WIDE, SHORT),
     (PASSES - 1, S2 - SHORT, SHORT),
@@ -208,6 +209,16 @@ def tile_list_motif_promoter_activity_kernel(
             w_bf[b] = held([P, N * PACK], BF16, "w_bf%d" % b, tag="win1_%d" % b, align=ROW_ALIGN)
             dealt = w_bf[b][:].rearrange("p (t m r) -> p m r t", t=PACK, r=PACK)
             for n0, n1 in [piece[1:] for piece in W_PIECES if piece[0] == b]:
+                if (b, n0) == (0, 0):
+                    nc.gpsimd.tensor_scalar(
+                        w_bf[b][:].rearrange("p (t m r) -> p t m r", t=PACK, r=PACK)[:, :, : n1 // PACK, :],
+                        w_raw[b, n0][:].rearrange("p r (m t) -> p t m r", t=PACK),
+                        1.0,
+                        -0.0,
+                        ALU.mult,
+                        ALU.add,
+                    )
+                    continue
                 for t0 in range(0, PACK, 2):
                     nc.vector.tensor_copy(
                         dealt[:, n0 // PACK : n1 // PACK, :, t0 : t0 + 2],
@@ -389,7 +400,11 @@ def tile_list_motif_promoter_activity_kernel(
                         ap.rearrange("p (e j) -> p e j", e=per_bank)[:, :, j0 : j0 + run]
                         for ap in (y[:, cols], p1[:], p2[:], first[:, cols])
                     ]
-                    nc.scalar.copy(first_run, p1_run)
+                    if (c, u) == (0, 0):
+                        nc.vector.tensor_copy(first_run[:, 0, :], p1_run[:, 0, :])
+                        nc.scalar.copy(first_run[:, 1, :], p1_run[:, 1, :])
+                    else:
+                        nc.scalar.copy(first_run, p1_run)
                     nc.vector.tensor_tensor(y_run, p2_run, first_run, ALU.mult)
                 nc.sync.dma_start(
                     out_rows[:, per_bank * u : per_bank * (u + 1), starts[c] : starts[c] + jc],
@@ -400,8 +415,9 @@ def tile_list_motif_promoter_activity_kernel(
             jc = CHUNKS[c]
             y = ys[c]
             yi = held([P, PACK * jc], BF16, "yi_%d" % c, tag=("picked00", "picked11", "hi_last", "", "")[c])
-            genes = sum(CHUNKS[c // 2 * 2 : c // 2 * 2 + 2])
-            if c % 2 == 0:
+            first, end = [run for run in CODE_STORES if run[0] <= c < run[1]][0]
+            genes = sum(CHUNKS[first:end])
+            if c == first:
                 yqs[c] = (held([P, genes], U32, "yq_%d" % c, align=ROW_ALIGN), starts[c])
             else:
                 yqs[c] = yqs[c - 1]
@@ -411,9 +427,10 @@ def tile_list_motif_promoter_activity_kernel(
             pooled = POOLED_OUT if c == 2 else 0
             if pooled:
                 pool_weave(yi, y, jc, pooled)
-            for j0 in range(0, jc, run):
+            piece = (jc - pooled) // 2 if pooled else run
+            for j0 in range(0, jc - pooled, piece):
                 copy = nc.vector.tensor_copy if c + 1 == len(CHUNKS) else nc.scalar.copy
-                copy(woven_genes(yi, j0, run - pooled, PAIR), sliced_genes(y, j0, run - pooled, PAIR))
+                copy(woven_genes(yi, j0, piece, PAIR), sliced_genes(y, j0, piece, PAIR))
             for j0 in range(0, jc, run):
                 nc.vector.quantize_mx(
                     out=yq[:, at + j0 : at + j0 + run].bitcast(FP8X4),

@@ -31,7 +31,7 @@ QUADRANT = 32
 ROW0 = P - PASSES * ROWS
 PLANE_ROW = (12, 4)
 LAST_PIECES = (256, 256, 512)
-W_PIECES = ((0, 0, N // 4), (0, N // 4, N), (1, 0, N))
+W_PIECES = ((0, 0, N // 2), (0, N // 2, N), (1, 0, N))
 POOLED = 208
 POOLED_OUT = 64
 WIDE, SHORT = 256, 128
@@ -209,16 +209,6 @@ def tile_list_motif_promoter_activity_kernel(
             w_bf[b] = held([P, N * PACK], BF16, "w_bf%d" % b, tag="win1_%d" % b, align=ROW_ALIGN)
             dealt = w_bf[b][:].rearrange("p (t m r) -> p m r t", t=PACK, r=PACK)
             for n0, n1 in [piece[1:] for piece in W_PIECES if piece[0] == b]:
-                if (b, n0) == (0, 0):
-                    nc.gpsimd.tensor_scalar(
-                        w_bf[b][:].rearrange("p (t m r) -> p t m r", t=PACK, r=PACK)[:, :, : n1 // PACK, :],
-                        w_raw[b, n0][:].rearrange("p r (m t) -> p t m r", t=PACK),
-                        1.0,
-                        -0.0,
-                        ALU.mult,
-                        ALU.add,
-                    )
-                    continue
                 for t0 in range(0, PACK, 2):
                     nc.vector.tensor_copy(
                         dealt[:, n0 // PACK : n1 // PACK, :, t0 : t0 + 2],
@@ -400,11 +390,7 @@ def tile_list_motif_promoter_activity_kernel(
                         ap.rearrange("p (e j) -> p e j", e=per_bank)[:, :, j0 : j0 + run]
                         for ap in (y[:, cols], p1[:], p2[:], first[:, cols])
                     ]
-                    if (c, u) == (0, 0):
-                        nc.vector.tensor_copy(first_run[:, 0, :], p1_run[:, 0, :])
-                        nc.scalar.copy(first_run[:, 1, :], p1_run[:, 1, :])
-                    else:
-                        nc.scalar.copy(first_run, p1_run)
+                    nc.scalar.copy(first_run, p1_run)
                     nc.vector.tensor_tensor(y_run, p2_run, first_run, ALU.mult)
                 nc.sync.dma_start(
                     out_rows[:, per_bank * u : per_bank * (u + 1), starts[c] : starts[c] + jc],

from contextlib import ExitStack

import concourse.mybir as mybir

K, T1, T2, S1, S2, N = 1024, 2048, 4096, 1024, 1024, 512
FLOPS = 2 * K * S1 * S2 + 2 * 2 * S1 * N * S2

F32 = mybir.dt.float32
BF16 = mybir.dt.bfloat16
I32 = mybir.dt.int32
U32 = mybir.dt.uint32
U16 = mybir.dt.uint16
U8 = mybir.dt.uint8
FP8X4 = mybir.dt.float8_e4m3fn_x4
FP4X4 = mybir.dt.float4_e2m1fn_x4
ACT = mybir.ActivationFunctionType
ALU = mybir.AluOpType

P = 128
PACK = 4
PASS = P * PACK
PASSES = 2
HALF = 1024
BANK = 512
LINE = 4
PAIR = 2
LINE_BYTES = 16
ROW_ALIGN = 256
ROWS = 16
QUADRANT = 32
ROW0 = P - PASSES * ROWS
PLANE_ROW = (12, 4)
LAST_PIECES = (256, 256, 512)
W_PIECES = ((0, 0, N // 2), (0, N // 2, N), (1, 0, N))
POOLED = 208
POOLED_OUT = 64
WIDE, SHORT = 256, 128
CHUNKS = (WIDE, WIDE, WIDE, SHORT, SHORT)
CODE_STORES = ((0, 2), (2, 3), (3, 5))
GROUPS = tuple((b, j0, WIDE) for j0 in range(0, S2, WIDE) for b in range(PASSES))[:-1] + (
    (PASSES - 1, S2 - WIDE, SHORT),
    (PASSES - 1, S2 - SHORT, SHORT),
)
AHEAD = 4
AFF_BANKS = 4
SQUARED = (4, 6, 7, 8)
LAG_TWO_PRODUCTS, LAG_SQUARED = 3, 2


def tile_list_motif_promoter_activity_kernel(
    tc, tab_words, tab_scales, tab2_words, tab2_scales, offs, offs2, abund, w, w4_words, w4_scales,
    out_0, out_1, out_2,
):
    nc = tc.nc
    with ExitStack() as ctx:
        keep = ctx.enter_context(tc.tile_pool(name="keep", bufs=1))
        work = ctx.enter_context(tc.tile_pool(name="work", bufs=3))
        psum = ctx.enter_context(tc.psum_pool(name="psum", bufs=2))
        by_offset = ctx.enter_context(tc.tile_pool(name="by_offset", bufs=1))

        def placed(shape, dtype, name, offset):
            return by_offset.tile(shape, dtype, name=name, offset=offset, align_bytes=ROW_ALIGN)

        def held(shape, dtype, name, tag="", align=64):
            return keep.tile(shape, dtype, name=name, tag=tag, align_bytes=align)

        def woven(dst, run):
            return dst[:].rearrange("p (x i t) -> p x t i", i=run, t=PACK)

        def sliced(src, run):
            return src[:].rearrange("p (t x i) -> p x t i", i=run, t=PACK)

        def woven_genes(dst, j0, run, near=LINE):
            return dst[:, PACK * j0 : PACK * (j0 + run)].rearrange("p (x i t) -> p x t i", i=near, t=PACK)

        def sliced_genes(src, j0, run, near=LINE):
            return src[:].rearrange("p (t j) -> p t j", t=PACK)[:, :, j0 : j0 + run].rearrange(
                "p t (x i) -> p x t i", i=near
            )

        win1_s = held([P, T1], U8, "win1_s", tag="win1_s", align=ROW_ALIGN)
        win2_s = held([P, T2], U8, "win2_s", tag="win2_s", align=ROW_ALIGN)
        nc.vector.memset(win1_s[:ROW0, :].bitcast(I32), 0)
        nc.vector.memset(win2_s[QUADRANT : 2 * QUADRANT, :].bitcast(I32), 0)
        nc.gpsimd.memset(win2_s[2 * QUADRANT :, :].bitcast(I32), 0)
        idx1 = keep.tile([P, S1 // 16], U16, name="idx1")
        idx2 = keep.tile([P, S2 // 16], U16, name="idx2")
        win1 = [held([P, T1], U32, "win1_%d" % a, tag="win1_%d" % a, align=ROW_ALIGN) for a in range(PASSES)]
        win2 = [placed([P, T2], U32, "win2_%d" % a, 4 * T2 * a) for a in range(PASSES)]
        planes = [held([P, S1 + S2], U8, "plane%d" % a, tag=("win1_s", "win2_s")[a], align=ROW_ALIGN) for a in range(PASSES)]

        def load_words(dst, src):
            nc.sync.dma_start(dst[:].bitcast(I32), src.rearrange("p n t -> p (n t)").bitcast(I32))

        def load_scales(win, row, src):
            nc.scalar.dma_start(win[row : row + QUADRANT, :].bitcast(I32), src.rearrange("a q n -> (a q) n").bitcast(I32))

        nc.sync.dma_start(idx1[:], offs)
        load_scales(win1_s, ROW0, tab_scales)
        nc.sync.dma_start(idx2[:], offs2)
        load_scales(win2_s, 0, tab2_scales)
        ab = held([P, PASSES * PACK], F32, "ab")
        nc.scalar.dma_start(
            ab[:].rearrange("p (b t) -> p b t", b=PASSES), abund.rearrange("(b p t) -> p b t", b=PASSES, t=PACK)
        )
        one = held([P, 1], F32, "one")
        nc.gpsimd.memset(one[:], 1.0)
        unit_row = held([P, 1], F32, "unit_row")
        nc.scalar.activation(unit_row[:], one[:], ACT.Abs_reciprocal_sqrt)
        unit = unit_row[:, 0:1]
        ab_second = {}
        for g in range(1, len(GROUPS)):
            ab_second[g] = held([P, 1], F32, "ab_%d" % g, tag="codes_%d" % (g - 1))
            column = PACK * GROUPS[g][0] + 1
            nc.scalar.copy(ab_second[g][:], ab[:, column : column + 1])
        w4_raw = held([P, PASSES * 2 * N], U8, "w4_raw", align=ROW_ALIGN)
        w4_s_raw = held([P, N], U8, "w4_s_raw")
        nc.vector.memset(w4_s_raw[:ROW0, :].bitcast(I32), 0)
        for a in range(PASSES):
            if a:
                nc.sync.dma_start(
                    w4_s_raw[ROW0:, :].bitcast(I32), w4_scales.rearrange("a q n -> (a q) n").bitcast(I32)
                )
            load_words(win1[a], tab_words[a])
            if a + 1 == PASSES:
                nc.sync.dma_start(
                    w4_raw[:].bitcast(I32).rearrange("p (b n) -> p b n", b=PASSES),
                    w4_words.bitcast(I32).rearrange("b p n -> p b n"),
                )
            else:
                load_words(win2[a], tab2_words[a])

        def deal(dst, src, column_bytes, copy=nc.vector.tensor_copy):
            per_line = LINE_BYTES // column_bytes
            copy(
                dst.rearrange("p (b t x i) -> p b x t i", x=P // per_line, t=PACK, i=per_line),
                src.rearrange("p (b x i t) -> p b x t i", x=P // per_line, t=PACK, i=per_line),
            )

        w4 = held([P, PASSES * 2 * N], U8, "w4")
        deal(w4[:].bitcast(U16), w4_raw[:].bitcast(U16), 2, nc.scalar.copy)

        picked_s = held([P, S1], U8, "picked_s")
        picked2_s = held([P, S2], U8, "picked2_s")
        nc.vector.tensor_copy(picked_s[:], win1_s[:].indirect(idx1[:]))
        nc.vector.tensor_copy(picked2_s[:], win2_s[:].indirect(idx2[:]))
        deal(planes[0][:, :S1], picked_s[:], 1)
        nc.vector.tensor_copy(planes[0][ROW0:, S1:].bitcast(I32), picked2_s[:QUADRANT, :].bitcast(I32))
        def move_first_pass(cols):
            for q in range(3):
                to, at = QUADRANT * q + PLANE_ROW[0], ROW0 + 4 * q
                nc.sync.dma_start(planes[0][to : to + 4, cols].bitcast(I32), planes[0][at : at + 4, cols].bitcast(I32))

        move_first_pass(slice(0, S1 + PASS))
        load_words(win2[1], tab2_words[1])
        for r in range(4):
            nc.sync.dma_start(
                planes[1][PLANE_ROW[1] + r : P : QUADRANT, :].bitcast(I32),
                planes[0][ROW0 + ROWS + r : P : 4, :].bitcast(I32),
            )
        w_raw = {}
        for b, n0, n1 in W_PIECES:
            w_raw[b, n0] = held([P, PACK, n1 - n0], F32, "w_raw%d_%d" % (b, n0), align=ROW_ALIGN)
            nc.sync.dma_start(
                w_raw[b, n0][:], w[b * PASS : (b + 1) * PASS, n0:n1].rearrange("(p r) n -> p r n", r=PACK)
            )
            if b + 1 == PASSES:
                move_first_pass(slice(S1 + PASS, S1 + S2))
        v1, v2 = {}, {}

        def gather_factors(a):
            picked = [held([P, PASS], U32, "picked%d%d" % (a, b), tag="picked%d%d" % (a, b)) for b in range(PASSES)]
            for b in range(PASSES):
                nc.vector.tensor_copy(
                    picked[b][:], win1[a][:].indirect(idx1[:, b * PASS // 16 : (b + 1) * PASS // 16])
                )
            for b in range(PASSES):
                v1[a, b] = held([P, PASS], U32, "v1_%d%d" % (a, b))
                deal(v1[a, b][:], picked[b][:], 4)

        def gather_genes(a, j0, genes, tile):
            nc.vector.tensor_copy(tile[:], win2[a][:].indirect(idx2[:, j0 // 16 : (j0 + genes) // 16]))
            for j in range(0, genes, SHORT):
                v2[a, j0 + j] = (tile, j)

        gather_factors(0)
        gather_genes(0, 0, HALF, held([P, HALF], U32, "v2_00"))
        gather_factors(1)
        dealt = held([P, N], U8, "w4_s_dealt", tag="picked01")
        deal(dealt[:], w4_s_raw[:], 1, nc.gpsimd.tensor_copy)
        w4_s = held([P, PASSES * N], U8, "w4_s", tag="picked10")
        for b in range(PASSES):
            for q in range(4):
                at = ROW0 + ROWS * b + 4 * q
                nc.sync.dma_start(
                    w4_s[QUADRANT * q : QUADRANT * q + 4, b * N : (b + 1) * N].bitcast(I32),
                    dealt[at : at + 4, :].bitcast(I32),
                )
        j0 = 0
        for n, piece in enumerate(LAST_PIECES):
            gather_genes(1, j0, piece, held([P, piece], U32, "v2_1%d" % n))
            j0 = j0 + piece

        wq = [held([P, N], U32, "wq%d" % b) for b in range(PASSES)]
        wq_s = [held([P, N], U8, "wq_s%d" % b) for b in range(PASSES)]
        w_bf = {}

        def cast_w(b):
            w_bf[b] = held([P, N * PACK], BF16, "w_bf%d" % b, tag="win1_%d" % b, align=ROW_ALIGN)
            dealt = w_bf[b][:].rearrange("p (t m r) -> p m r t", t=PACK, r=PACK)
            for n0, n1 in [piece[1:] for piece in W_PIECES if piece[0] == b]:
                for t0 in range(0, PACK, 2):
                    nc.vector.tensor_copy(
                        dealt[:, n0 // PACK : n1 // PACK, :, t0 : t0 + 2],
                        w_raw[b, n0][:].rearrange("p r (m t) -> p m r t", t=PACK)[:, :, :, t0 : t0 + 2],
                    )

        def quantise_w():
            for b in range(PASSES):
                for n0 in range(0, N, N // 2):
                    nc.vector.quantize_mx(
                        out=wq[b][:, n0 : n0 + N // 2].bitcast(FP8X4),
                        scales=wq_s[b][:, n0 : n0 + N // 2],
                        in_=w_bf[b][:, PACK * n0 : PACK * (n0 + N // 2)],
                    )

        starts = [sum(CHUNKS[:c]) for c in range(len(CHUNKS))]
        groups = len(GROUPS)
        aff, sq, rs, partial, hb, hi, hq, hq_s = {}, {}, {}, {}, {}, {}, {}, {}

        def width(g):
            return GROUPS[g][2]

        def banks(jc):
            return PACK * jc // BANK

        def slices_of(g):
            if g == 0:
                return [(0, 1), (1, 2), (2, PACK)]
            per_bank = BANK // width(g)
            return [(t, t + per_bank) for t in range(0, PACK, per_bank)]

        def affinity(g, u, a):
            b, j0, jc = GROUPS[g]
            t0, t1 = slices_of(g)[u]
            per_bank = t1 - t0
            genes, at = v2[a, j0]
            opens = (g, u) not in aff
            if opens:
                aff[g, u] = psum.tile([P, BANK], F32, name="aff", bufs=AFF_BANKS)
            for e in range(per_bank):
                m0 = (t0 + e) * P
                nc.tensor.matmul_mx(
                    out=aff[g, u][:, e * jc : (e + 1) * jc],
                    lhsT=v1[a, b][:, m0 : m0 + P].bitcast(FP8X4),
                    lhsT_scale=planes[a][PLANE_ROW[a] :, b * PASS + m0 : b * PASS + m0 + P],
                    rhs=genes[:, at : at + jc].bitcast(FP8X4),
                    rhs_scale=planes[a][PLANE_ROW[a] :, S1 + j0 : S1 + j0 + jc],
                    start=(opens and e == 0),
                    stop=(not opens and e == per_bank - 1),
                )

        def square(g, u):
            for a in (1,) if (g, u) in aff else (0, 1):
                affinity(g, u, a)
            if u == 0:
                sq[g] = held([P, PACK * width(g)], F32, "sq_%d" % g, tag="sq_%d" % g, align=ROW_ALIGN)
            t0, t1 = slices_of(g)[u]
            jc = width(g)
            nc.scalar.activation(sq[g][:, t0 * jc : t1 * jc], aff[g, u][:, : (t1 - t0) * jc], ACT.Square)

        def root(g, t0=0, t1=PACK):
            if t0 == 0:
                rs[g] = held([P, PACK * width(g)], F32, "rs_%d" % g, tag="rs_%d" % g)
            cols = slice(t0 * width(g), t1 * width(g))
            nc.scalar.activation(rs[g][:, cols], sq[g][:, cols], ACT.Abs_reciprocal_sqrt, bias=unit)

        def square_root(g, t0=0, t1=PACK):
            if t0 == 0:
                partial[g] = work.tile([P, PACK * width(g)], F32, name="partial", bufs=AHEAD)
            if g in SQUARED:
                cols = slice(t0 * width(g), t1 * width(g))
                nc.scalar.activation(partial[g][:, cols], rs[g][:, cols], ACT.Square)

        def weigh(g):
            b, j0, jc = GROUPS[g]
            if g in SQUARED:
                hb[g] = work.tile([P, PACK * jc], BF16, name="hb")
                dst, factor = hb[g], partial[g]
            else:
                dst, factor = partial[g], rs[g]
            for t in range(PACK):
                cols = slice(t * jc, (t + 1) * jc)
                abundance = ab[:, PACK * b + t : PACK * b + t + 1]
                if t == 1 and g in ab_second:
                    abundance = ab_second[g][:]
                nc.vector.scalar_tensor_tensor(
                    dst[:, cols], sq[g][:, cols], abundance, factor[:, cols], ALU.mult, ALU.mult
                )

        def pooled_genes(g):
            return min(POOLED, width(g)) if g in pathways_at and g in SQUARED else 0

        def pool_weave(dst, src, genes, n):
            nc.gpsimd.tensor_scalar(
                dst[:].rearrange("p (j t) -> p j t", t=PACK)[:, genes - n :, :],
                src[:].rearrange("p (t j) -> p j t", t=PACK)[:, genes - n :, :],
                1.0,
                -0.0,
                ALU.mult,
                ALU.add,
            )

        def open_woven(g):
            if g + 1 == groups:
                hi[g] = held([P, PACK * width(g)], BF16, "hi_last", tag="hi_last")
            else:
                hi[g] = work.tile([P, PACK * width(g)], BF16, name="hi", align_bytes=64, bufs=2)

        def weave_pooled(g):
            n = pooled_genes(g)
            open_woven(g)
            pool_weave(hi[g], hb[g], width(g), n)

        def weave_h(g):
            if not pooled_genes(g):
                open_woven(g)
            if g in SQUARED:
                n = width(g) - pooled_genes(g)
                nc.vector.tensor_copy(woven_genes(hi[g], 0, n), sliced_genes(hb[g], 0, n))
            else:
                nc.vector.tensor_tensor(woven(hi[g], PAIR), sliced(partial[g], PAIR), sliced(rs[g], PAIR), ALU.mult)

        def quantise_h(g):
            hq[g] = held([P, width(g)], U32, "hq_%d" % g, tag="codes_%d" % g)
            hq_s[g] = work.tile([P, width(g)], U8, name="hq_s", bufs=AHEAD + 1, align_bytes=64)
            nc.vector.quantize_mx(out=hq[g][:].bitcast(FP8X4), scales=hq_s[g][:], in_=hi[g][:])

        def group_of(b, j):
            return [g for g, (gb, j0, jc) in enumerate(GROUPS) if gb == b and j0 <= j < j0 + jc][0]

        ys, yqs = {}, {}
        y_s = held([P, S2], U8, "y_s", align=ROW_ALIGN)
        out_rows = out_0.rearrange("(p t) j -> p t j", t=PACK)
        out_words = out_1[0].rearrange("p m t -> p (m t)").bitcast(I32)

        def pathways(c, w4, w4_s):
            jc = CHUNKS[c]
            per_bank = BANK // jc
            bytes_of = "sq_%d" % pathways_at[c] if jc == WIDE else ""
            y = ys[c] = held([P, PACK * jc], F32, "y_%d" % c, tag=bytes_of, align=ROW_ALIGN)
            first = work.tile([P, PACK * jc], F32, name="first", bufs=2)
            for u in range(banks(jc)):
                if c != PASSES:
                    p1 = psum.tile([P, BANK], F32, name="p1")
                    p2 = psum.tile([P, BANK], F32, name="p2")
                else:
                    p1 = psum.tile([P, BANK], F32, name="aff", bufs=AFF_BANKS)
                    p2 = psum.tile([P, BANK], F32, name="aff", bufs=AFF_BANKS)
                for b in range(PASSES):
                    g = group_of(b, starts[c])
                    h0 = starts[c] - GROUPS[g][1]
                    for e in range(per_bank):
                        m = slice((per_bank * u + e) * P, (per_bank * u + e + 1) * P)
                        nc.tensor.matmul_mx(
                            out=p1[:, e * jc : (e + 1) * jc],
                            lhsT=wq[b][:, m].bitcast(FP8X4),
                            lhsT_scale=wq_s[b][:, m],
                            rhs=hq[g][:, h0 : h0 + jc].bitcast(FP8X4),
                            rhs_scale=hq_s[g][:, h0 : h0 + jc],
                            start=(b == 0 and e == 0),
                            stop=(b == PASSES - 1 and e == per_bank - 1),
                        )
                    for e in range(per_bank):
                        m0 = b * N + (per_bank * u + e) * P
                        for j0 in range(0, jc, P):
                            nc.tensor.matmul_mx(
                                out=p2[:, e * jc + j0 : e * jc + j0 + P],
                                lhsT=w4[:, 2 * m0 : 2 * (m0 + P)].bitcast(FP4X4),
                                lhsT_scale=w4_s[:, m0 : m0 + P],
                                rhs=hq[g][:, h0 + j0 : h0 + j0 + P].bitcast(FP8X4),
                                rhs_scale=hq_s[g][:, h0 + j0 : h0 + j0 + P],
                                start=(b == 0 and e == 0 and j0 == 0),
                                stop=(b == PASSES - 1 and e == per_bank - 1 and j0 == jc - P),
                            )
                cols = slice(u * BANK, (u + 1) * BANK)
                run = jc // 2 if c + 1 == len(CHUNKS) else jc
                for j0 in range(0, jc, run):
                    y_run, p1_run, p2_run, first_run = [
                        ap.rearrange("p (e j) -> p e j", e=per_bank)[:, :, j0 : j0 + run]
                        for ap in (y[:, cols], p1[:], p2[:], first[:, cols])
                    ]
                    nc.scalar.copy(first_run, p1_run)
                    nc.vector.tensor_tensor(y_run, p2_run, first_run, ALU.mult)
                nc.sync.dma_start(
                    out_rows[:, per_bank * u : per_bank * (u + 1), starts[c] : starts[c] + jc],
                    y[:, cols].rearrange("p (e j) -> p e j", e=per_bank),
                )

        def quantise_out(c):
            jc = CHUNKS[c]
            y = ys[c]
            yi = held([P, PACK * jc], BF16, "yi_%d" % c, tag=("picked00", "picked11", "hi_last", "", "")[c])
            first, end = [run for run in CODE_STORES if run[0] <= c < run[1]][0]
            genes = sum(CHUNKS[first:end])
            if c == first:
                yqs[c] = (held([P, genes], U32, "yq_%d" % c, align=ROW_ALIGN), starts[c])
            else:
                yqs[c] = yqs[c - 1]
            yq, base = yqs[c]
            at = starts[c] - base
            run = jc if c + 1 < len(CHUNKS) else jc // 2
            pooled = POOLED_OUT if c == 2 else 0
            if pooled:
                pool_weave(yi, y, jc, pooled)
            piece = (jc - pooled) // 2 if pooled else run
            for j0 in range(0, jc - pooled, piece):
                copy = nc.vector.tensor_copy if c + 1 == len(CHUNKS) else nc.scalar.copy
                copy(woven_genes(yi, j0, piece, PAIR), sliced_genes(y, j0, piece, PAIR))
            for j0 in range(0, jc, run):
                nc.vector.quantize_mx(
                    out=yq[:, at + j0 : at + j0 + run].bitcast(FP8X4),
                    scales=y_s[:, starts[c] + j0 : starts[c] + j0 + run],
                    in_=yi[:, PACK * j0 : PACK * (j0 + run)],
                )
            if at + jc == genes:
                nc.sync.dma_start(out_words[:, base : base + genes], yq[:].bitcast(I32))

        last_group = [group_of(PASSES - 1, j0) for j0 in starts]
        pathways_at = [g + (LAG_TWO_PRODUCTS if g < 4 else LAG_SQUARED) for g in last_group]
        pathways_at[2] = groups - 1
        codes_at = [pathways_at[c] + banks(jc) for c, jc in enumerate(CHUNKS)]

        codes_at[0] = codes_at[1] = groups

        def finish(step, w4, w4_s):
            for c in range(len(CHUNKS)):
                if pathways_at[c] == step:
                    pathways(c, w4, w4_s)
            for c in range(len(CHUNKS)):
                if codes_at[c] == step:
                    quantise_out(c)

        first_banks = slices_of(0)
        for u in range(len(first_banks)):
            affinity(0, u, 0)
        affinity(1, 0, 0)
        for u in range(len(first_banks)):
            square(0, u)
            if u:
                root(0, *first_banks[u - 1])
        ahead = [(g, u) for g in range(1, groups) for u in range(banks(width(g)))]
        for g in range(groups):
            if g in SQUARED and width(g) == WIDE:
                square(*ahead[2 * g])
                for step in (root, square_root):
                    for t0 in range(0, PACK, PAIR):
                        step(g, t0, t0 + PAIR)
                square(*ahead[2 * g + 1])
            elif 2 * g < len(ahead):
                square(*ahead[2 * g])
                root(g, *(first_banks[-1] if g == 0 else ()))
                square(*ahead[2 * g + 1])
                square_root(g)
            elif g + 1 < groups:
                root(g)
                root(g + 1)
                square_root(g)
                square_root(g + 1)
            weigh(g)
            if pooled_genes(g):
                quantise_h(g - 1)
                weave_pooled(g)
            else:
                if g >= 1:
                    quantise_h(g - 1)
                weave_h(g)
            if g == PASSES - 1:
                cast_w(0)
            if g == PASSES:
                cast_w(1)
                quantise_w()
            if g >= PASSES:
                finish(g, w4, w4_s)
            if 0 < pooled_genes(g) < width(g):
                weave_h(g)
        quantise_h(groups - 1)
        for step in range(groups, codes_at[-1] + 1):
            finish(step, w4, w4_s)
        for q in range(4):
            queue = nc.scalar if q % 2 else nc.sync
            queue.dma_start(out_2[0, 4 * q : 4 * q + 4, :].bitcast(I32), y_s[QUADRANT * q : QUADRANT * q + 4, :].bitcast(I32))
